import numpy as np
import ml_dtypes


def mxq(x, axis, fmt="e4m3"):
    dtype, down = {"e4m3": (ml_dtypes.float8_e4m3fn, 7), "e5m2": (ml_dtypes.float8_e5m2, 14)}[fmt]
    v = np.moveaxis(np.asarray(x, np.float32).astype(ml_dtypes.bfloat16).astype(np.float64), axis, -1)
    blocks = v.reshape(v.shape[:-1] + (-1, 32))
    amax = np.abs(blocks).max(-1, keepdims=True)
    byte = np.maximum(np.where(amax > 0, np.frexp(amax)[1] - 1 + 127, 0) - down, 1)
    scale = np.exp2(byte - 127.0)
    codes = (blocks / scale).astype(np.float32).astype(dtype).astype(np.float64)
    return np.moveaxis((codes * scale).reshape(v.shape), -1, axis)


WIDE = False


def mx_kscale(k):
    if not WIDE:
        return np.ones(k)
    levels = np.array([18, -18])
    if k % 512:
        return np.exp2(np.random.permutation(np.resize(levels, k // 32))).repeat(32)
    a = np.empty((k // 512, 16))
    for p in range(k // 512):
        a[p, :8] = np.random.permutation(np.resize(levels, 8))
        for g in range(8):
            far = levels[np.abs(levels - a[p, g]) >= 10]
            a[p, g + 8] = far[np.random.randint(len(far))]
    return np.exp2(a.ravel()).repeat(32)


def f64(x):
    return np.asarray(x).astype(np.float64)


def striped(idx):
    return np.tile(np.asarray(idx).reshape(-1, 16).T, (8, 1)).astype(np.uint16)


def unstriped(offs):
    return offs[:16].T.reshape(-1).astype(np.int64)


E2M1 = np.array([0.0, 0.5, 1.0, 1.5, 2.0, 3.0, 4.0, 6.0, -0.0, -0.5, -1.0, -1.5, -2.0, -3.0, -4.0, -6.0])


def pack_weight(w, fmt):
    k, n = w.shape
    w = f64(np.asarray(w, np.float32).astype(ml_dtypes.bfloat16)).reshape(k // 32, 32, n)
    amax = np.abs(w).max(1)
    if fmt == "e4m3":
        byte = np.frexp(amax)[1] - 1 + 127 - 7
    else:
        mant, ex = np.frexp(amax / 6.0)
        byte = np.where(mant > 0.5, ex, ex - 1) + 127
    byte = np.clip(np.where(amax > 0, byte, 1), 1, 254)
    scaled = (w * np.exp2(127.0 - byte)[:, None, :]).reshape(k, n).astype(np.float32)
    by_word = np.ascontiguousarray(scaled.reshape(k // 512, 128, 4, n).transpose(0, 1, 3, 2))
    if fmt == "e4m3":
        words = by_word.astype(ml_dtypes.float8_e4m3fn).view(np.uint8)
    else:
        c = by_word.astype(ml_dtypes.float4_e2m1fn).view(np.uint8) & 0xF
        words = (c[..., 0::2] | (c[..., 1::2] << 4)).reshape(k // 512, 128, 2 * n)
    return np.ascontiguousarray(words), np.ascontiguousarray(byte.astype(np.uint8).reshape(k // 512, 16, n))


def unpack_weight(words, scales, fmt):
    g, _, n = scales.shape
    words = np.ascontiguousarray(words).reshape(g, 128, n, -1)
    if fmt == "e4m3":
        vals = words.view(ml_dtypes.float8_e4m3fn).astype(np.float64)
    else:
        nib = np.empty((g, 128, n, 4), np.uint8)
        nib[..., 0::2] = words & 0xF
        nib[..., 1::2] = words >> 4
        vals = E2M1[nib]
    vals = vals * np.repeat(np.exp2(scales.astype(np.float64) - 127.0), 8, axis=1)[..., None]
    return vals.transpose(0, 1, 3, 2).reshape(g * 512, n)


N, T, D, V = 512, 1024, 512, 1024


def setup_inputs():
    n = np.random.standard_normal
    idx = np.random.permutation(T)[:N]
    s = mx_kscale(D)[:, None]
    z = mx_kscale(V)[:, None]
    w = n((D, V)) / np.sqrt(D)
    wd, wv = pack_weight(w * s, "e4m3"), pack_weight(w.T / z, "e4m3")
    return {
        "xT": (n((D, T)) / s).astype(np.float32),
        "wd_words": wd[0],
        "wd_scales": wd[1],
        "wv_words": wv[0],
        "wv_scales": wv[1],
        "y": n((V, N)).astype(np.float32),
        "cw": (np.random.uniform(0.5, 1.5, (V, 1)) / np.sqrt(V) * z).astype(np.float32),
        "rw": np.tile(np.random.uniform(0.5, 1.5, N), (128, 1)).astype(np.float32),
        "offs": striped(idx),
    }


def reference(xT, wd_words, wd_scales, wv_words, wv_scales, y, cw, rw, offs):
    idx = unstriped(offs)
    a = unpack_weight(wd_words, wd_scales, "e4m3").T @ mxq(f64(xT)[:, idx], 0, "e4m3")
    g = f64(cw) * f64(rw)[:1] * np.tanh(a - f64(y))
    dx = unpack_weight(wv_words, wv_scales, "e4m3").T @ mxq(g, 0, "e5m2")
    gx = np.zeros((D, T))
    gx[:, idx] = dx
    return gx

@@ -1,0 +1,162 @@
+from contextlib import ExitStack
+
+import concourse.mybir as mybir
+
+N, T, D, V = 512, 1024, 512, 1024
+FLOPS = 2 * 2 * N * D * V
+
+F32 = mybir.dt.float32
+BF16 = mybir.dt.bfloat16
+I32 = mybir.dt.int32
+U32 = mybir.dt.uint32
+U16 = mybir.dt.uint16
+U8 = mybir.dt.uint8
+E4M3 = mybir.dt.float8_e4m3fn_x4
+E5M2 = mybir.dt.float8_e5m2_x4
+ACT = mybir.ActivationFunctionType
+ALU = mybir.AluOpType
+
+P = 128
+LANES = 4
+PASSES = V // (P * LANES)
+HALF_T = T // 2
+HALF_N = N // 2
+
+
+def tile_attend_gml_lch_kernel(tc, xT, wd_words, wd_scales, wv_words, wv_scales, y, cw, rw, offs, out):
+    nc = tc.nc
+    with ExitStack() as ctx:
+        sb = ctx.enter_context(tc.tile_pool(name="sb", bufs=1))
+        ps_a = ctx.enter_context(tc.psum_pool(name="ps_a", bufs=4))
+        ps_dx = ctx.enter_context(tc.psum_pool(name="ps_dx", bufs=1))
+
+        offsets = sb.tile([P, N // 16], U16, name="offsets")
+        nc.sync.dma_start(offsets[:], offs)
+
+        wd_sc_raw = sb.tile([P, V], U8, name="wd_sc_raw", align_bytes=64)
+        wv_sc = sb.tile([P, PASSES, D], U8, name="wv_sc", align_bytes=64)
+        warm = sb.tile([P, 8], F32, name="warm")
+        nc.vector.memset(wd_sc_raw[:].bitcast(I32), 0)
+        nc.vector.memset(warm[:], 0.0)
+        nc.vector.memset(wv_sc[:].rearrange("p o d -> p (o d)").bitcast(I32), 0)
+        warm_out = sb.tile([P, 8], F32, name="warm_out")
+        nc.scalar.activation(warm_out[:], warm[:], ACT.Tanh)
+
+        x_rows = xT.rearrange("(p j) n -> p j n", j=LANES)
+        x_raw = {}
+        for u in range(2):
+            for h in range(2):
+                x_raw[u, h] = sb.tile([P, 2, HALF_T], F32, name=f"x_raw{u}{h}")
+                nc.sync.dma_start(x_raw[u, h][:], x_rows[:, 2 * u : 2 * u + 2, h * HALF_T : (h + 1) * HALF_T])
+
+        wd_sc_rows = wd_scales[0].rearrange("(q r) v -> r q v", r=4)
+        for r in range(4):
+            nc.scalar.dma_start(wd_sc_raw[r:P:32, :].bitcast(I32), wd_sc_rows[r].bitcast(I32))
+
+        wd_raw = sb.tile([P, V], I32, name="wd_raw")
+        nc.sync.dma_start(wd_raw[:], wd_words[0].rearrange("p v t -> p (v t)").bitcast(I32))
+        rw_sb = sb.tile([P, N], F32, name="rw_sb")
+        nc.sync.dma_start(rw_sb[:], rw)
+        cw_sb = sb.tile([P, PASSES, 8], F32, name="cw_sb")
+        nc.sync.dma_start(cw_sb[:, :, 0:LANES], cw.rearrange("(o p t) e -> p o (t e)", p=P, t=LANES))
+        y_rows = y.rearrange("(o p t) i -> o p t i", p=P, t=LANES)
+        y_sb = {}
+        for o in range(PASSES):
+            for u in range(2):
+                y_sb[o, u] = sb.tile([P, 2, N], F32, name=f"y_sb{o}{u}")
+                nc.sync.dma_start(y_sb[o, u][:], y_rows[o][:, 2 * u : 2 * u + 2, :])
+        wv_sc_rows = wv_scales.rearrange("o (q r) d -> r q o d", r=4)
+        for r in range(4):
+            nc.sync.dma_start(wv_sc[r:P:32, :, :].bitcast(I32), wv_sc_rows[r].bitcast(I32))
+        wv_sb = sb.tile([P, PASSES, D], I32, name="wv_sb", align_bytes=64)
+        nc.sync.dma_start(wv_sb[:], wv_words.rearrange("o p d t -> p o (d t)").bitcast(I32))
+
+        windows = []
+        for k in range(D // P):
+            window = sb.tile([P, T], F32, name=f"window{k}")
+            nc.vector.memset(window[:], 0.0)
+            windows.append(window)
+
+        wd_sc = sb.tile([P, V], U8, name="wd_sc", align_bytes=64)
+        nc.vector.tensor_copy(
+            wd_sc[:].rearrange("p (o t m) -> p o t m", o=PASSES, t=LANES),
+            wd_sc_raw[:].rearrange("p (o m t) -> p o t m", o=PASSES, t=LANES),
+        )
+
+        xg = sb.tile([P, N * LANES], BF16, name="xg", align_bytes=64)
+        xg_words = xg[:].bitcast(U32).rearrange("p (i u) -> p i u", u=2)
+        for u in range(2):
+            pairs = sb.tile([P, 2 * T], BF16, name=f"pairs{u}")
+            for h in range(2):
+                dst = pairs[:, h * T : (h + 1) * T].rearrange("p (n e) -> p n e", e=2)
+                src = x_raw[u, h][:].rearrange("p e n -> p n e")
+                if (u, h) == (1, 1):
+                    nc.vector.tensor_copy(dst, src)
+                else:
+                    nc.scalar.activation(dst, src, ACT.Copy)
+            nc.vector.tensor_copy(xg_words[:, :, u], pairs[:].bitcast(U32).indirect(offsets[:]))
+
+        wd_sb = sb.tile([P, V], I32, name="wd_sb", align_bytes=64)
+
+        def permute_wd(o):
+            cols = slice(o * 512, (o + 1) * 512)
+            nc.vector.tensor_copy(
+                wd_sb[:, cols].rearrange("p (t c i) -> p c t i", t=LANES, i=4),
+                wd_raw[:, cols].rearrange("p (c i t) -> p c t i", t=LANES, i=4),
+            )
+
+        x_codes = sb.tile([P, N], U32, name="x_codes", align_bytes=64)
+        x_sc = sb.tile([P, N], U8, name="x_sc", align_bytes=64)
+        permute_wd(0)
+        nc.vector.quantize_mx(out=x_codes[:].bitcast(E4M3), scales=x_sc[:], in_=xg[:])
+        permute_wd(1)
+
+        weight = [sb.tile([P, LANES, N], F32, name=f"weight{o}") for o in range(PASSES)]
+        slope = [sb.tile([P, LANES, N], F32, name=f"slope{o}") for o in range(PASSES)]
+
+        def make_weight(o):
+            for t in range(LANES):
+                nc.scalar.activation(weight[o][:, t, :], rw_sb[:], ACT.Copy, scale=cw_sb[:, o, t : t + 1])
+
+        make_weight(0)
+        for o in range(PASSES):
+            for t in range(LANES):
+                cols = slice((o * LANES + t) * P, (o * LANES + t + 1) * P)
+                a = ps_a.tile([P, N], F32, name="a")
+                nc.tensor.matmul_mx(
+                    out=a[:], lhsT=wd_sb[:, cols].bitcast(E4M3), lhsT_scale=wd_sc[:, cols],
+                    rhs=x_codes[:].bitcast(E4M3), rhs_scale=x_sc[:], start=True, stop=True,
+                )
+                diff = sb.tile([P, N], F32, name=f"diff{o}{t}")
+                nc.vector.tensor_tensor(diff[:], a[:], y_sb[o, t // 2][:, t % 2, :], ALU.subtract)
+                nc.scalar.activation(slope[o][:, t, :], diff[:], ACT.Tanh)
+        make_weight(1)
+
+        dx = [ps_dx.tile([P, N], F32, name=f"dx{k}") for k in range(D // P)]
+        for o in range(PASSES):
+            g = sb.tile([P, N * LANES], BF16, name=f"g{o}", align_bytes=64)
+            g_codes = sb.tile([P, N], U32, name=f"g_codes{o}", align_bytes=64)
+            g_sc = sb.tile([P, N], U8, name=f"g_sc{o}", align_bytes=64)
+            for h in range(2):
+                cols = slice(h * HALF_N, (h + 1) * HALF_N)
+                nc.vector.tensor_tensor(
+                    g[:, h * 1024 : (h + 1) * 1024].rearrange("p (c i t) -> p c t i", t=LANES, i=4),
+                    slope[o][:, :, cols].rearrange("p t (c i) -> p c t i", i=4),
+                    weight[o][:, :, cols].rearrange("p t (c i) -> p c t i", i=4),
+                    ALU.mult,
+                )
+            for h in range(2):
+                cols = slice(h * HALF_N, (h + 1) * HALF_N)
+                nc.vector.quantize_mx(out=g_codes[:, cols].bitcast(E5M2), scales=g_sc[:, cols], in_=g[:, h * 1024 : (h + 1) * 1024])
+            for k in range(D // P):
+                cols = slice(k * P, (k + 1) * P)
+                nc.tensor.matmul_mx(
+                    out=dx[k][:], lhsT=wv_sb[:, o, cols].bitcast(E4M3), lhsT_scale=wv_sc[:, o, cols],
+                    rhs=g_codes[:].bitcast(E5M2), rhs_scale=g_sc[:], start=(o == 0), stop=(o == PASSES - 1),
+                )
+
+        for k in range(D // P):
+            dx_sb = sb.tile([P, N], F32, name=f"dx_sb{k}")
+            nc.scalar.activation(dx_sb[:], dx[k][:], ACT.Copy)
+            nc.vector.tensor_copy(windows[k][:].indirect(offsets[:]), dx_sb[:])
+            nc.sync.dma_start(out[k * P : (k + 1) * P, :], windows[k][:])

@@ -21,6 +21,9 @@ LANES = 4
 PASSES = V // (P * LANES)
 HALF_T = T // 2
 HALF_N = N // 2
+D_TILES = D // P
+EARLY_TILES = 2
+VECTOR_CAST = 320
 
 
 def tile_attend_gml_lch_kernel(tc, xT, wd_words, wd_scales, wv_words, wv_scales, y, cw, rw, offs, out):
@@ -28,7 +31,7 @@ def tile_attend_gml_lch_kernel(tc, xT, wd_words, wd_scales, wv_words, wv_scales,
     with ExitStack() as ctx:
         sb = ctx.enter_context(tc.tile_pool(name="sb", bufs=1))
         ps_a = ctx.enter_context(tc.psum_pool(name="ps_a", bufs=4))
-        ps_dx = ctx.enter_context(tc.psum_pool(name="ps_dx", bufs=1))
+        ps_dx = ctx.enter_context(tc.psum_pool(name="ps_dx", bufs=4))
 
         offsets = sb.tile([P, N // 16], U16, name="offsets")
         nc.sync.dma_start(offsets[:], offs)
@@ -42,6 +45,11 @@ def tile_attend_gml_lch_kernel(tc, xT, wd_words, wd_scales, wv_words, wv_scales,
         warm_out = sb.tile([P, 8], F32, name="warm_out")
         nc.scalar.activation(warm_out[:], warm[:], ACT.Tanh)
 
+        cw_sb = sb.tile([P, PASSES, 8], F32, name="cw_sb")
+        nc.scalar.dma_start(cw_sb[:, :, 0:LANES], cw.rearrange("(o p t) e -> p o (t e)", p=P, t=LANES))
+        rw_sb = sb.tile([P, N], F32, name="rw_sb")
+        nc.sync.dma_start(rw_sb[:], rw)
+
         x_rows = xT.rearrange("(p j) n -> p j n", j=LANES)
         x_raw = {}
         for u in range(2):
@@ -53,28 +61,34 @@ def tile_attend_gml_lch_kernel(tc, xT, wd_words, wd_scales, wv_words, wv_scales,
         for r in range(4):
             nc.scalar.dma_start(wd_sc_raw[r:P:32, :].bitcast(I32), wd_sc_rows[r].bitcast(I32))
 
-        wd_raw = sb.tile([P, V], I32, name="wd_raw")
-        nc.sync.dma_start(wd_raw[:], wd_words[0].rearrange("p v t -> p (v t)").bitcast(I32))
-        rw_sb = sb.tile([P, N], F32, name="rw_sb")
-        nc.sync.dma_start(rw_sb[:], rw)
-        cw_sb = sb.tile([P, PASSES, 8], F32, name="cw_sb")
-        nc.sync.dma_start(cw_sb[:, :, 0:LANES], cw.rearrange("(o p t) e -> p o (t e)", p=P, t=LANES))
+        wd_hbm = wd_words[0].rearrange("p v t -> p (v t)").bitcast(I32)
+        wd_raw = []
+        for o in range(PASSES):
+            wd_raw.append(sb.tile([P, 512], I32, name=f"wd_raw{o}"))
+            nc.sync.dma_start(wd_raw[o][:], wd_hbm[:, o * 512 : (o + 1) * 512])
+        wv_sc_rows = wv_scales.rearrange("o (q r) d -> r q o d", r=4)
+
         y_rows = y.rearrange("(o p t) i -> o p t i", p=P, t=LANES)
         y_sb = {}
-        for o in range(PASSES):
-            for u in range(2):
-                y_sb[o, u] = sb.tile([P, 2, N], F32, name=f"y_sb{o}{u}")
-                nc.sync.dma_start(y_sb[o, u][:], y_rows[o][:, 2 * u : 2 * u + 2, :])
-        wv_sc_rows = wv_scales.rearrange("o (q r) d -> r q o d", r=4)
-        for r in range(4):
-            nc.sync.dma_start(wv_sc[r:P:32, :, :].bitcast(I32), wv_sc_rows[r].bitcast(I32))
         wv_sb = sb.tile([P, PASSES, D], I32, name="wv_sb", align_bytes=64)
-        nc.sync.dma_start(wv_sb[:], wv_words.rearrange("o p d t -> p o (d t)").bitcast(I32))
+        for h in range(2):
+            for o in range(PASSES):
+                y_sb[o, h] = sb.tile([P, LANES, HALF_N], F32, name=f"y_sb{o}{h}")
+                nc.sync.dma_start(y_sb[o, h][:], y_rows[o][:, :, h * HALF_N : (h + 1) * HALF_N])
+            if h == 0:
+                nc.sync.dma_start(wv_sb[:], wv_words.rearrange("o p d t -> p o (d t)").bitcast(I32))
+                for r in range(4):
+                    nc.sync.dma_start(wv_sc[r:P:32, :, :].bitcast(I32), wv_sc_rows[r].bitcast(I32))
+
+        g_codes = sb.tile([P, PASSES, N], I32, name="g_codes", align_bytes=64)
+        g_sc = sb.tile([P, PASSES, N], U8, name="g_sc", align_bytes=64)
+        nc.vector.memset(g_codes[:, :, HALF_N:N], 0)
+        nc.vector.memset(g_sc[:].rearrange("p o i -> p (o i)").bitcast(I32), 0)
 
         windows = []
         for k in range(D // P):
             window = sb.tile([P, T], F32, name=f"window{k}")
-            nc.vector.memset(window[:], 0.0)
+            nc.vector.memset(window[:].bitcast(I32), 0)
             windows.append(window)
 
         wd_sc = sb.tile([P, V], U8, name="wd_sc", align_bytes=64)
@@ -85,16 +99,19 @@ def tile_attend_gml_lch_kernel(tc, xT, wd_words, wd_scales, wv_words, wv_scales,
 
         xg = sb.tile([P, N * LANES], BF16, name="xg", align_bytes=64)
         xg_words = xg[:].bitcast(U32).rearrange("p (i u) -> p i u", u=2)
-        for u in range(2):
-            pairs = sb.tile([P, 2 * T], BF16, name=f"pairs{u}")
-            for h in range(2):
-                dst = pairs[:, h * T : (h + 1) * T].rearrange("p (n e) -> p n e", e=2)
-                src = x_raw[u, h][:].rearrange("p e n -> p n e")
-                if (u, h) == (1, 1):
-                    nc.vector.tensor_copy(dst, src)
-                else:
-                    nc.scalar.activation(dst, src, ACT.Copy)
-            nc.vector.tensor_copy(xg_words[:, :, u], pairs[:].bitcast(U32).indirect(offsets[:]))
+        pairs = [sb.tile([P, 2 * T], BF16, name=f"pairs{u}") for u in range(2)]
+
+        def cast(on_vector, u, h, lo, hi):
+            base = h * HALF_T
+            dst = pairs[u][:, 2 * (base + lo) : 2 * (base + hi)].rearrange("p (n e) -> p n e", e=2)
+            src = x_raw[u, h][:, :, lo:hi].rearrange("p e n -> p n e")
+            if on_vector:
+                nc.vector.tensor_copy(dst, src)
+            else:
+                nc.scalar.activation(dst, src, ACT.Copy)
+
+        def gather(u, lo, hi):
+            nc.vector.tensor_copy(xg_words[:, lo:hi, u], pairs[u][:].bitcast(U32).indirect(offsets[:, lo // 16 : hi // 16]))
 
         wd_sb = sb.tile([P, V], I32, name="wd_sb", align_bytes=64)
 
@@ -102,61 +119,104 @@ def tile_attend_gml_lch_kernel(tc, xT, wd_words, wd_scales, wv_words, wv_scales,
             cols = slice(o * 512, (o + 1) * 512)
             nc.vector.tensor_copy(
                 wd_sb[:, cols].rearrange("p (t c i) -> p c t i", t=LANES, i=4),
-                wd_raw[:, cols].rearrange("p (c i t) -> p c t i", t=LANES, i=4),
+                wd_raw[o][:].rearrange("p (c i t) -> p c t i", t=LANES, i=4),
             )
 
         x_codes = sb.tile([P, N], U32, name="x_codes", align_bytes=64)
         x_sc = sb.tile([P, N], U8, name="x_sc", align_bytes=64)
+
+        def quantize_x(lo, hi):
+            nc.vector.quantize_mx(out=x_codes[:, lo:hi].bitcast(E4M3), scales=x_sc[:, lo:hi], in_=xg[:, LANES * lo : LANES * hi])
+
+        cast(False, 0, 0, 0, HALF_T)
+        cast(True, 0, 1, 0, HALF_T)
+        gather(0, 0, N)
+        cast(False, 1, 0, 0, HALF_T)
+        cast(True, 1, 1, 0, VECTOR_CAST)
+        cast(False, 1, 1, VECTOR_CAST, HALF_T)
+        gather(1, 0, HALF_N)
         permute_wd(0)
-        nc.vector.quantize_mx(out=x_codes[:].bitcast(E4M3), scales=x_sc[:], in_=xg[:])
+        quantize_x(0, HALF_N)
+        gather(1, HALF_N, N)
         permute_wd(1)
+        quantize_x(HALF_N, N)
 
-        weight = [sb.tile([P, LANES, N], F32, name=f"weight{o}") for o in range(PASSES)]
-        slope = [sb.tile([P, LANES, N], F32, name=f"slope{o}") for o in range(PASSES)]
-
-        def make_weight(o):
-            for t in range(LANES):
-                nc.scalar.activation(weight[o][:, t, :], rw_sb[:], ACT.Copy, scale=cw_sb[:, o, t : t + 1])
-
-        make_weight(0)
+        weight = sb.tile([P, PASSES, LANES, N], F32, name="weight")
         for o in range(PASSES):
             for t in range(LANES):
-                cols = slice((o * LANES + t) * P, (o * LANES + t + 1) * P)
-                a = ps_a.tile([P, N], F32, name="a")
-                nc.tensor.matmul_mx(
-                    out=a[:], lhsT=wd_sb[:, cols].bitcast(E4M3), lhsT_scale=wd_sc[:, cols],
-                    rhs=x_codes[:].bitcast(E4M3), rhs_scale=x_sc[:], start=True, stop=True,
-                )
-                diff = sb.tile([P, N], F32, name=f"diff{o}{t}")
-                nc.vector.tensor_tensor(diff[:], a[:], y_sb[o, t // 2][:, t % 2, :], ALU.subtract)
-                nc.scalar.activation(slope[o][:, t, :], diff[:], ACT.Tanh)
-        make_weight(1)
+                nc.scalar.activation(weight[:, o, t, :], rw_sb[:], ACT.Copy, scale=cw_sb[:, o, t : t + 1])
 
-        dx = [ps_dx.tile([P, N], F32, name=f"dx{k}") for k in range(D // P)]
-        for o in range(PASSES):
-            g = sb.tile([P, N * LANES], BF16, name=f"g{o}", align_bytes=64)
-            g_codes = sb.tile([P, N], U32, name=f"g_codes{o}", align_bytes=64)
-            g_sc = sb.tile([P, N], U8, name=f"g_sc{o}", align_bytes=64)
-            for h in range(2):
-                cols = slice(h * HALF_N, (h + 1) * HALF_N)
-                nc.vector.tensor_tensor(
-                    g[:, h * 1024 : (h + 1) * 1024].rearrange("p (c i t) -> p c t i", t=LANES, i=4),
-                    slope[o][:, :, cols].rearrange("p t (c i) -> p c t i", i=4),
-                    weight[o][:, :, cols].rearrange("p t (c i) -> p c t i", i=4),
-                    ALU.mult,
-                )
-            for h in range(2):
-                cols = slice(h * HALF_N, (h + 1) * HALF_N)
-                nc.vector.quantize_mx(out=g_codes[:, cols].bitcast(E5M2), scales=g_sc[:, cols], in_=g[:, h * 1024 : (h + 1) * 1024])
-            for k in range(D // P):
-                cols = slice(k * P, (k + 1) * P)
-                nc.tensor.matmul_mx(
-                    out=dx[k][:], lhsT=wv_sb[:, o, cols].bitcast(E4M3), lhsT_scale=wv_sc[:, o, cols],
-                    rhs=g_codes[:].bitcast(E5M2), rhs_scale=g_sc[:], start=(o == 0), stop=(o == PASSES - 1),
-                )
+        slope = {}
 
-        for k in range(D // P):
-            dx_sb = sb.tile([P, N], F32, name=f"dx_sb{k}")
-            nc.scalar.activation(dx_sb[:], dx[k][:], ACT.Copy)
-            nc.vector.tensor_copy(windows[k][:].indirect(offsets[:]), dx_sb[:])
+        def residual(h, o):
+            pos = slice(h * HALF_N, (h + 1) * HALF_N)
+            slope[h, o] = sb.tile([P, LANES, HALF_N], F32, name=f"slope{h}{o}", tag=f"slope{h}{o}")
+            for u in range(2):
+                a = ps_a.tile([P, 2, HALF_N], F32, name="a")
+                for e in range(2):
+                    j = o * LANES + 2 * u + e
+                    cols = slice(j * P, (j + 1) * P)
+                    nc.tensor.matmul_mx(
+                        out=a[:, e, :], lhsT=wd_sb[:, cols].bitcast(E4M3), lhsT_scale=wd_sc[:, cols],
+                        rhs=x_codes[:, pos].bitcast(E4M3), rhs_scale=x_sc[:, pos], start=True, stop=True,
+                    )
+                diff = sb.tile([P, 2, HALF_N], F32, name=f"diff{h}{o}{u}")
+                nc.vector.tensor_tensor(diff[:], a[:], y_sb[o, h][:, 2 * u : 2 * u + 2, :], ALU.subtract)
+                nc.scalar.activation(slope[h, o][:, 2 * u : 2 * u + 2, :], diff[:], ACT.Tanh)
+
+        g = {}
+
+        def weigh(h, o):
+            g[h, o] = sb.tile([P, HALF_N * LANES], BF16, name=f"g{h}{o}", align_bytes=64)
+            nc.vector.tensor_tensor(
+                g[h, o][:].rearrange("p (b i t) -> p b t i", t=LANES, i=4),
+                slope[h, o][:].rearrange("p t (b i) -> p b t i", i=4),
+                weight[:, o, :, h * HALF_N : (h + 1) * HALF_N].rearrange("p t (b i) -> p b t i", i=4),
+                ALU.mult,
+            )
+
+        def quantize_g(h, o):
+            pos = slice(h * HALF_N, (h + 1) * HALF_N)
+            nc.vector.quantize_mx(out=g_codes[:, o, pos].bitcast(E5M2), scales=g_sc[:, o, pos], in_=g[h, o][:])
+
+        def project(tiles):
+            banks = {k: ps_dx.tile([P, N], F32, name="dx_ps") for k in tiles}
+            for k in tiles:
+                for o in range(PASSES):
+                    cols = slice(k * P, (k + 1) * P)
+                    nc.tensor.matmul_mx(
+                        out=banks[k][:], lhsT=wv_sb[:, o, cols].bitcast(E4M3), lhsT_scale=wv_sc[:, o, cols],
+                        rhs=g_codes[:, o, :].bitcast(E5M2), rhs_scale=g_sc[:, o, :], start=(o == 0), stop=(o == PASSES - 1),
+                    )
+            return banks
+
+        def unload(bank, k, lo, hi, tag):
+            dx = sb.tile([P, hi - lo], F32, name=f"dx{k}_{lo}", tag=tag)
+            nc.scalar.activation(dx[:], bank[:, lo:hi], ACT.Copy)
+            return dx
+
+        def scatter(dx, k, lo, hi):
+            nc.vector.tensor_copy(windows[k][:].indirect(offsets[:, lo // 16 : hi // 16]), dx[:])
+
+        residual(0, 0)
+        residual(0, 1)
+        weigh(0, 0)
+        weigh(0, 1)
+        quantize_g(0, 0)
+        quantize_g(0, 1)
+        early = project(range(EARLY_TILES))
+        residual(1, 0)
+        residual(1, 1)
+        weigh(1, 0)
+        early_dx0 = unload(early[0], 0, 0, HALF_N, "slope10")
+        weigh(1, 1)
+        early_dx1 = unload(early[1], 1, 0, HALF_N, "slope11")
+        quantize_g(1, 0)
+        quantize_g(1, 1)
+        late = project(range(D_TILES))
+        scatter(early_dx0, 0, 0, HALF_N)
+        scatter(early_dx1, 1, 0, HALF_N)
+        for k in range(D_TILES):
+            lo = HALF_N if k < EARLY_TILES else 0
+            scatter(unload(late[k], k, lo, N, f"late{k}"), k, lo, N)
             nc.sync.dma_start(out[k * P : (k + 1) * P, :], windows[k][:])

@@ -47,8 +47,7 @@ def tile_attend_gml_lch_kernel(tc, xT, wd_words, wd_scales, wv_words, wv_scales,
 
         cw_sb = sb.tile([P, PASSES, 8], F32, name="cw_sb")
         nc.scalar.dma_start(cw_sb[:, :, 0:LANES], cw.rearrange("(o p t) e -> p o (t e)", p=P, t=LANES))
-        rw_sb = sb.tile([P, N], F32, name="rw_sb")
-        nc.sync.dma_start(rw_sb[:], rw)
+        rw_sb = [sb.tile([P, HALF_N], F32, name=f"rw_sb{h}") for h in range(2)]
 
         x_rows = xT.rearrange("(p j) n -> p j n", j=LANES)
         x_raw = {}
@@ -56,6 +55,8 @@ def tile_attend_gml_lch_kernel(tc, xT, wd_words, wd_scales, wv_words, wv_scales,
             for h in range(2):
                 x_raw[u, h] = sb.tile([P, 2, HALF_T], F32, name=f"x_raw{u}{h}")
                 nc.sync.dma_start(x_raw[u, h][:], x_rows[:, 2 * u : 2 * u + 2, h * HALF_T : (h + 1) * HALF_T])
+            if u == 0:
+                nc.sync.dma_start(rw_sb[0][:], rw[:, 0:HALF_N])
 
         wd_sc_rows = wd_scales[0].rearrange("(q r) v -> r q v", r=4)
         for r in range(4):
@@ -76,9 +77,10 @@ def tile_attend_gml_lch_kernel(tc, xT, wd_words, wd_scales, wv_words, wv_scales,
                 y_sb[o, h] = sb.tile([P, LANES, HALF_N], F32, name=f"y_sb{o}{h}")
                 nc.sync.dma_start(y_sb[o, h][:], y_rows[o][:, :, h * HALF_N : (h + 1) * HALF_N])
             if h == 0:
-                nc.sync.dma_start(wv_sb[:], wv_words.rearrange("o p d t -> p o (d t)").bitcast(I32))
-                for r in range(4):
-                    nc.sync.dma_start(wv_sc[r:P:32, :, :].bitcast(I32), wv_sc_rows[r].bitcast(I32))
+                nc.sync.dma_start(rw_sb[1][:], rw[:, HALF_N:N])
+        nc.sync.dma_start(wv_sb[:], wv_words.rearrange("o p d t -> p o (d t)").bitcast(I32))
+        for r in range(4):
+            nc.sync.dma_start(wv_sc[r:P:32, :, :].bitcast(I32), wv_sc_rows[r].bitcast(I32))
 
         g_codes = sb.tile([P, PASSES, N], I32, name="g_codes", align_bytes=64)
         g_sc = sb.tile([P, PASSES, N], U8, name="g_sc", align_bytes=64)
@@ -88,7 +90,8 @@ def tile_attend_gml_lch_kernel(tc, xT, wd_words, wd_scales, wv_words, wv_scales,
         windows = []
         for k in range(D // P):
             window = sb.tile([P, T], F32, name=f"window{k}")
-            nc.vector.memset(window[:].bitcast(I32), 0)
+            zeroing = nc.vector if k < EARLY_TILES else nc.gpsimd
+            zeroing.memset(window[:].bitcast(I32), 0)
             windows.append(window)
 
         wd_sc = sb.tile([P, V], U8, name="wd_sc", align_bytes=64)
@@ -110,8 +113,13 @@ def tile_attend_gml_lch_kernel(tc, xT, wd_words, wd_scales, wv_words, wv_scales,
             else:
                 nc.scalar.activation(dst, src, ACT.Copy)
 
+        picked = sb.tile([P, 2, N], U32, name="picked", tag="picked")
+
+        def interleave(lo, hi):
+            nc.scalar.copy(xg_words[:, lo:hi, :], picked[:, :, lo:hi].rearrange("p u i -> p i u"))
+
         def gather(u, lo, hi):
-            nc.vector.tensor_copy(xg_words[:, lo:hi, u], pairs[u][:].bitcast(U32).indirect(offsets[:, lo // 16 : hi // 16]))
+            nc.vector.tensor_copy(picked[:, u, lo:hi], pairs[u][:].bitcast(U32).indirect(offsets[:, lo // 16 : hi // 16]))
 
         wd_sb = sb.tile([P, V], I32, name="wd_sb", align_bytes=64)
 
@@ -135,16 +143,21 @@ def tile_attend_gml_lch_kernel(tc, xT, wd_words, wd_scales, wv_words, wv_scales,
         cast(True, 1, 1, 0, VECTOR_CAST)
         cast(False, 1, 1, VECTOR_CAST, HALF_T)
         gather(1, 0, HALF_N)
+        interleave(0, HALF_N)
+        gather(1, HALF_N, N)
+        interleave(HALF_N, N)
         permute_wd(0)
         quantize_x(0, HALF_N)
-        gather(1, HALF_N, N)
         permute_wd(1)
         quantize_x(HALF_N, N)
 
-        weight = sb.tile([P, PASSES, LANES, N], F32, name="weight")
-        for o in range(PASSES):
-            for t in range(LANES):
-                nc.scalar.activation(weight[:, o, t, :], rw_sb[:], ACT.Copy, scale=cw_sb[:, o, t : t + 1])
+        weight = {}
+
+        def make_weight(h, tag):
+            weight[h] = sb.tile([P, PASSES, LANES, HALF_N], F32, name=f"weight{h}", tag=tag)
+            for o in range(PASSES):
+                for t in range(LANES):
+                    nc.scalar.activation(weight[h][:, o, t, :], rw_sb[h][:], ACT.Copy, scale=cw_sb[:, o, t : t + 1])
 
         slope = {}
 
@@ -171,7 +184,7 @@ def tile_attend_gml_lch_kernel(tc, xT, wd_words, wd_scales, wv_words, wv_scales,
             nc.vector.tensor_tensor(
                 g[h, o][:].rearrange("p (b i t) -> p b t i", t=LANES, i=4),
                 slope[h, o][:].rearrange("p t (b i) -> p b t i", i=4),
-                weight[:, o, :, h * HALF_N : (h + 1) * HALF_N].rearrange("p t (b i) -> p b t i", i=4),
+                weight[h][:, o, :, :].rearrange("p t (b i) -> p b t i", i=4),
                 ALU.mult,
             )
 
@@ -198,8 +211,10 @@ def tile_attend_gml_lch_kernel(tc, xT, wd_words, wd_scales, wv_words, wv_scales,
         def scatter(dx, k, lo, hi):
             nc.vector.tensor_copy(windows[k][:].indirect(offsets[:, lo // 16 : hi // 16]), dx[:])
 
+        make_weight(0, "weight0")
         residual(0, 0)
         residual(0, 1)
+        make_weight(1, "picked")
         weigh(0, 0)
         weigh(0, 1)
         quantize_g(0, 0)

@@ -1,6 +1,7 @@
 from contextlib import ExitStack
 
 import concourse.mybir as mybir
+from concourse.masks import make_identity
 
 N, T, D, V = 512, 1024, 512, 1024
 FLOPS = 2 * 2 * N * D * V
@@ -22,16 +23,18 @@ PASSES = V // (P * LANES)
 HALF_T = T // 2
 HALF_N = N // 2
 D_TILES = D // P
+CHUNK = 128
+VECTOR_WINDOWS = 2
 EARLY_TILES = 2
-VECTOR_CAST = 320
+VECTOR_CAST = 384
+X_LOADS = ((0, 0, HALF_T), (0, HALF_T, T), (1, 0, HALF_T), (1, HALF_T, T))
 
 
 def tile_attend_gml_lch_kernel(tc, xT, wd_words, wd_scales, wv_words, wv_scales, y, cw, rw, offs, out):
     nc = tc.nc
     with ExitStack() as ctx:
         sb = ctx.enter_context(tc.tile_pool(name="sb", bufs=1))
-        ps_a = ctx.enter_context(tc.psum_pool(name="ps_a", bufs=4))
-        ps_dx = ctx.enter_context(tc.psum_pool(name="ps_dx", bufs=4))
+        ps = ctx.enter_context(tc.psum_pool(name="ps", bufs=1))
 
         offsets = sb.tile([P, N // 16], U16, name="offsets")
         nc.sync.dma_start(offsets[:], offs)
@@ -39,58 +42,60 @@ def tile_attend_gml_lch_kernel(tc, xT, wd_words, wd_scales, wv_words, wv_scales,
         wd_sc_raw = sb.tile([P, V], U8, name="wd_sc_raw", align_bytes=64)
         wv_sc = sb.tile([P, PASSES, D], U8, name="wv_sc", align_bytes=64)
         warm = sb.tile([P, 8], F32, name="warm")
-        nc.vector.memset(wd_sc_raw[:].bitcast(I32), 0)
+        nc.gpsimd.memset(wd_sc_raw[:].bitcast(I32), 0)
         nc.vector.memset(warm[:], 0.0)
-        nc.vector.memset(wv_sc[:].rearrange("p o d -> p (o d)").bitcast(I32), 0)
+        nc.gpsimd.memset(wv_sc[:].rearrange("p o d -> p (o d)").bitcast(I32), 0)
+
+        rw_sb = sb.tile([P, N], F32, name="rw_sb")
+        nc.sync.dma_start(rw_sb[:], rw)
+        cw_sb = sb.tile([P, PASSES, 8], F32, name="cw_sb")
+        nc.sync.dma_start(cw_sb[:, :, 0:LANES], cw.rearrange("(o p t) e -> p o (t e)", p=P, t=LANES))
+        wd_sc_rows = wd_scales[0].rearrange("(q r) v -> r q v", r=4)
+        for r in range(4):
+            nc.sync.dma_start(wd_sc_raw[r:P:32, :].bitcast(I32), wd_sc_rows[r].bitcast(I32))
         warm_out = sb.tile([P, 8], F32, name="warm_out")
         nc.scalar.activation(warm_out[:], warm[:], ACT.Tanh)
 
-        cw_sb = sb.tile([P, PASSES, 8], F32, name="cw_sb")
-        nc.scalar.dma_start(cw_sb[:, :, 0:LANES], cw.rearrange("(o p t) e -> p o (t e)", p=P, t=LANES))
-        rw_sb = [sb.tile([P, HALF_N], F32, name=f"rw_sb{h}") for h in range(2)]
-
         x_rows = xT.rearrange("(p j) n -> p j n", j=LANES)
         x_raw = {}
-        for u in range(2):
-            for h in range(2):
-                x_raw[u, h] = sb.tile([P, 2, HALF_T], F32, name=f"x_raw{u}{h}")
-                nc.sync.dma_start(x_raw[u, h][:], x_rows[:, 2 * u : 2 * u + 2, h * HALF_T : (h + 1) * HALF_T])
-            if u == 0:
-                nc.sync.dma_start(rw_sb[0][:], rw[:, 0:HALF_N])
-
-        wd_sc_rows = wd_scales[0].rearrange("(q r) v -> r q v", r=4)
-        for r in range(4):
-            nc.scalar.dma_start(wd_sc_raw[r:P:32, :].bitcast(I32), wd_sc_rows[r].bitcast(I32))
+        for u, lo, hi in X_LOADS:
+            x_raw[u, lo] = sb.tile([P, 2, hi - lo], F32, name=f"x_raw{u}_{lo}", tag=f"x_raw{u}_{lo}", align_bytes=64)
+            nc.sync.dma_start(x_raw[u, lo][:], x_rows[:, 2 * u : 2 * u + 2, lo:hi])
 
         wd_hbm = wd_words[0].rearrange("p v t -> p (v t)").bitcast(I32)
-        wd_raw = []
-        for o in range(PASSES):
-            wd_raw.append(sb.tile([P, 512], I32, name=f"wd_raw{o}"))
-            nc.sync.dma_start(wd_raw[o][:], wd_hbm[:, o * 512 : (o + 1) * 512])
+        wd_raw = [sb.tile([P, 512], I32, name=f"wd_raw{o}", tag=f"wd_raw{o}") for o in range(PASSES)]
         wv_sc_rows = wv_scales.rearrange("o (q r) d -> r q o d", r=4)
 
         y_rows = y.rearrange("(o p t) i -> o p t i", p=P, t=LANES)
         y_sb = {}
         wv_sb = sb.tile([P, PASSES, D], I32, name="wv_sb", align_bytes=64)
-        for h in range(2):
-            for o in range(PASSES):
-                y_sb[o, h] = sb.tile([P, LANES, HALF_N], F32, name=f"y_sb{o}{h}")
-                nc.sync.dma_start(y_sb[o, h][:], y_rows[o][:, :, h * HALF_N : (h + 1) * HALF_N])
-            if h == 0:
-                nc.sync.dma_start(rw_sb[1][:], rw[:, HALF_N:N])
-        nc.sync.dma_start(wv_sb[:], wv_words.rearrange("o p d t -> p o (d t)").bitcast(I32))
+
+        def load_y(o, h):
+            y_sb[o, h] = sb.tile([P, LANES, HALF_N], F32, name=f"y_sb{o}{h}", tag=f"y_sb{o}{h}", align_bytes=64)
+            nc.sync.dma_start(y_sb[o, h][:], y_rows[o][:, :, h * HALF_N : (h + 1) * HALF_N])
+
+        for o in range(PASSES):
+            nc.sync.dma_start(wd_raw[o][:], wd_hbm[:, o * 512 : (o + 1) * 512])
+        load_y(0, 0)
+        load_y(1, 0)
+        load_y(0, 1)
+        load_y(1, 1)
         for r in range(4):
             nc.sync.dma_start(wv_sc[r:P:32, :, :].bitcast(I32), wv_sc_rows[r].bitcast(I32))
+        nc.sync.dma_start(wv_sb[:], wv_words.rearrange("o p d t -> p o (d t)").bitcast(I32))
 
-        g_codes = sb.tile([P, PASSES, N], I32, name="g_codes", align_bytes=64)
-        g_sc = sb.tile([P, PASSES, N], U8, name="g_sc", align_bytes=64)
-        nc.vector.memset(g_codes[:, :, HALF_N:N], 0)
-        nc.vector.memset(g_sc[:].rearrange("p o i -> p (o i)").bitcast(I32), 0)
+        g_codes = [sb.tile([P, HALF_N + N], I32, name=f"g_codes{o}", align_bytes=64) for o in range(PASSES)]
+        g_sc = [sb.tile([P, HALF_N + N], U8, name=f"g_sc{o}", align_bytes=64) for o in range(PASSES)]
+        for o in range(PASSES):
+            nc.vector.memset(g_codes[o][:, 0:HALF_N], 0)
+            nc.vector.memset(g_sc[o][:, 0:HALF_N].bitcast(I32), 0)
+        ident = sb.tile([P, P], F32, name="ident")
+        make_identity(nc, ident[:])
 
         windows = []
         for k in range(D // P):
             window = sb.tile([P, T], F32, name=f"window{k}")
-            zeroing = nc.vector if k < EARLY_TILES else nc.gpsimd
+            zeroing = nc.vector if k < VECTOR_WINDOWS else nc.gpsimd
             zeroing.memset(window[:].bitcast(I32), 0)
             windows.append(window)
 
@@ -100,26 +105,26 @@ def tile_attend_gml_lch_kernel(tc, xT, wd_words, wd_scales, wv_words, wv_scales,
             wd_sc_raw[:].rearrange("p (o m t) -> p o t m", o=PASSES, t=LANES),
         )
 
-        xg = sb.tile([P, N * LANES], BF16, name="xg", align_bytes=64)
-        xg_words = xg[:].bitcast(U32).rearrange("p (i u) -> p i u", u=2)
+        xg = [sb.tile([P, HALF_N * LANES], BF16, name=f"xg{h}", tag=tag, align_bytes=64) for h, tag in enumerate(("xg0", f"x_raw1_{HALF_T}"))]
+        xg_words = [xg[h][:].bitcast(U32).rearrange("p (i u) -> p i u", u=2) for h in range(2)]
         pairs = [sb.tile([P, 2 * T], BF16, name=f"pairs{u}") for u in range(2)]
 
-        def cast(on_vector, u, h, lo, hi):
-            base = h * HALF_T
+        def cast(on_vector, u, base, lo, hi):
             dst = pairs[u][:, 2 * (base + lo) : 2 * (base + hi)].rearrange("p (n e) -> p n e", e=2)
-            src = x_raw[u, h][:, :, lo:hi].rearrange("p e n -> p n e")
+            src = x_raw[u, base][:, :, lo:hi].rearrange("p e n -> p n e")
             if on_vector:
                 nc.vector.tensor_copy(dst, src)
             else:
                 nc.scalar.activation(dst, src, ACT.Copy)
 
-        picked = sb.tile([P, 2, N], U32, name="picked", tag="picked")
 
-        def interleave(lo, hi):
-            nc.scalar.copy(xg_words[:, lo:hi, :], picked[:, :, lo:hi].rearrange("p u i -> p i u"))
+        def gather(dst, u, lo, hi):
+            nc.vector.tensor_copy(dst, pairs[u][:].bitcast(U32).indirect(offsets[:, lo // 16 : hi // 16]))
 
-        def gather(u, lo, hi):
-            nc.vector.tensor_copy(picked[:, u, lo:hi], pairs[u][:].bitcast(U32).indirect(offsets[:, lo // 16 : hi // 16]))
+        def pick(u, tag):
+            picked = sb.tile([P, HALF_N], U32, name=f"picked{u}", tag=tag)
+            gather(picked[:], u, HALF_N, N)
+            nc.scalar.copy(xg_words[1][:, :, u], picked[:])
 
         wd_sb = sb.tile([P, V], I32, name="wd_sb", align_bytes=64)
 
@@ -130,105 +135,141 @@ def tile_attend_gml_lch_kernel(tc, xT, wd_words, wd_scales, wv_words, wv_scales,
                 wd_raw[o][:].rearrange("p (c i t) -> p c t i", t=LANES, i=4),
             )
 
-        x_codes = sb.tile([P, N], U32, name="x_codes", align_bytes=64)
-        x_sc = sb.tile([P, N], U8, name="x_sc", align_bytes=64)
+        x_codes, x_sc = {}, {}
 
-        def quantize_x(lo, hi):
-            nc.vector.quantize_mx(out=x_codes[:, lo:hi].bitcast(E4M3), scales=x_sc[:, lo:hi], in_=xg[:, LANES * lo : LANES * hi])
-
-        cast(False, 0, 0, 0, HALF_T)
-        cast(True, 0, 1, 0, HALF_T)
-        gather(0, 0, N)
-        cast(False, 1, 0, 0, HALF_T)
-        cast(True, 1, 1, 0, VECTOR_CAST)
-        cast(False, 1, 1, VECTOR_CAST, HALF_T)
-        gather(1, 0, HALF_N)
-        interleave(0, HALF_N)
-        gather(1, HALF_N, N)
-        interleave(HALF_N, N)
-        permute_wd(0)
-        quantize_x(0, HALF_N)
-        permute_wd(1)
-        quantize_x(HALF_N, N)
+        def quantize_x(h, tag):
+            x_codes[h] = sb.tile([P, HALF_N], U32, name=f"x_codes{h}", tag=tag, align_bytes=64)
+            x_sc[h] = sb.tile([P, HALF_N], U8, name=f"x_sc{h}", align_bytes=64)
+            nc.vector.quantize_mx(out=x_codes[h][:].bitcast(E4M3), scales=x_sc[h][:], in_=xg[h][:])
 
         weight = {}
 
-        def make_weight(h, tag):
-            weight[h] = sb.tile([P, PASSES, LANES, HALF_N], F32, name=f"weight{h}", tag=tag)
+        def make_weight(h):
             for o in range(PASSES):
+                weight[h, o] = sb.tile([P, LANES, HALF_N], F32, name=f"weight{h}{o}", tag=f"weight{h}{o}", align_bytes=64)
                 for t in range(LANES):
-                    nc.scalar.activation(weight[h][:, o, t, :], rw_sb[h][:], ACT.Copy, scale=cw_sb[:, o, t : t + 1])
+                    rows = rw_sb[:, h * HALF_N : (h + 1) * HALF_N]
+                    if h == 0:
+                        nc.vector.tensor_scalar(weight[h, o][:, t, :], rows, cw_sb[:, o, t : t + 1], None, ALU.mult)
+                    else:
+                        nc.scalar.activation(weight[h, o][:, t, :], rows, ACT.Copy, scale=cw_sb[:, o, t : t + 1])
 
-        slope = {}
+        cast(False, 0, 0, 0, HALF_T)
+        cast(True, 0, HALF_T, 0, HALF_T)
+        gather(xg_words[0][:, :, 0], 0, 0, HALF_N)
+        pick(0, "picked0")
+        cast(False, 1, 0, 0, HALF_T)
+        cast(True, 1, HALF_T, 0, VECTOR_CAST)
+        cast(False, 1, HALF_T, VECTOR_CAST, HALF_T)
+        gather(xg_words[0][:, :, 1], 1, 0, HALF_N)
+        permute_wd(0)
+        quantize_x(0, "x_codes0")
+        permute_wd(1)
 
-        def residual(h, o):
-            pos = slice(h * HALF_N, (h + 1) * HALF_N)
-            slope[h, o] = sb.tile([P, LANES, HALF_N], F32, name=f"slope{h}{o}", tag=f"slope{h}{o}")
-            for u in range(2):
-                a = ps_a.tile([P, 2, HALF_N], F32, name="a")
-                for e in range(2):
-                    j = o * LANES + 2 * u + e
-                    cols = slice(j * P, (j + 1) * P)
-                    nc.tensor.matmul_mx(
-                        out=a[:, e, :], lhsT=wd_sb[:, cols].bitcast(E4M3), lhsT_scale=wd_sc[:, cols],
-                        rhs=x_codes[:, pos].bitcast(E4M3), rhs_scale=x_sc[:, pos], start=True, stop=True,
-                    )
-                diff = sb.tile([P, 2, HALF_N], F32, name=f"diff{h}{o}{u}")
-                nc.vector.tensor_tensor(diff[:], a[:], y_sb[o, h][:, 2 * u : 2 * u + 2, :], ALU.subtract)
-                nc.scalar.activation(slope[h, o][:, 2 * u : 2 * u + 2, :], diff[:], ACT.Tanh)
+        def scores(tag, o, planes, lo, hi):
+            a = ps.tile([P, len(planes), hi - lo], F32, name="a", tag=tag)
+            h = lo // HALF_N
+            pos = slice(lo - h * HALF_N, hi - h * HALF_N)
+            for e, t in enumerate(planes):
+                j = o * LANES + t
+                cols = slice(j * P, (j + 1) * P)
+                nc.tensor.matmul_mx(
+                    out=a[:, e, :], lhsT=wd_sb[:, cols].bitcast(E4M3), lhsT_scale=wd_sc[:, cols],
+                    rhs=x_codes[h][:, pos].bitcast(E4M3), rhs_scale=x_sc[h][:, pos], start=True, stop=True,
+                )
+            return a
+
+        def targets(o, lo, hi):
+            h = lo // HALF_N
+            return y_sb[o, h][:, :, lo - h * HALF_N : hi - h * HALF_N]
+
+        def slope_direct(o, lo, hi, tags):
+            slope = sb.tile([P, LANES, hi - lo], F32, name=f"slope{o}_{lo}")
+            step = LANES // len(tags)
+            for u, tag in enumerate(tags):
+                planes = range(u * step, (u + 1) * step)
+                a = scores(tag, o, planes, lo, hi)
+                diff = sb.tile([P, step, hi - lo], F32, name=f"diff{o}_{lo}_{u}")
+                nc.vector.tensor_tensor(diff[:], a[:], targets(o, lo, hi)[:, planes.start : planes.stop, :], ALU.subtract)
+                nc.scalar.activation(slope[:, planes.start : planes.stop, :], diff[:], ACT.Tanh)
+            return slope
+
+        def slope_turned(o, lo, hi, tag, tag_turned, tag_back):
+            a = scores(tag, o, range(LANES), lo, hi)
+            minus_a = sb.tile([P, LANES, CHUNK], F32, name=f"minus_a{o}")
+            nc.scalar.activation(minus_a[:], a[:], ACT.Copy, scale=-1.0)
+            diff = ps.tile([P, LANES, P], F32, name="diff_t", tag=tag_turned)
+            for t in range(LANES):
+                nc.tensor.matmul(diff[:, t, :], targets(o, lo, hi)[:, t, :], ident[:], start=(t == 0), stop=False, is_transpose=True)
+            for t in range(LANES):
+                nc.tensor.matmul(diff[:, t, :], minus_a[:, t, :], ident[:], start=False, stop=(t == LANES - 1), is_transpose=True)
+            slope_t = sb.tile([P, LANES, P], F32, name=f"slope_t{o}")
+            nc.scalar.activation(slope_t[:], diff[:], ACT.Tanh, scale=-1.0)
+            slope = ps.tile([P, LANES, CHUNK], F32, name="slope_ps", tag=tag_back)
+            for t in range(LANES):
+                nc.tensor.transpose(slope[:, t, :], slope_t[:, t, :], ident[:])
+            return slope
 
         g = {}
+        for h in range(2):
+            for o in range(PASSES):
+                g[h, o] = sb.tile([P, HALF_N * LANES], BF16, name=f"g{h}{o}", align_bytes=64)
 
-        def weigh(h, o):
-            g[h, o] = sb.tile([P, HALF_N * LANES], BF16, name=f"g{h}{o}", align_bytes=64)
+        def weigh(slope, o, lo, hi):
+            h = lo // HALF_N
+            lo, hi = lo - h * HALF_N, hi - h * HALF_N
             nc.vector.tensor_tensor(
-                g[h, o][:].rearrange("p (b i t) -> p b t i", t=LANES, i=4),
-                slope[h, o][:].rearrange("p t (b i) -> p b t i", i=4),
-                weight[h][:, o, :, :].rearrange("p t (b i) -> p b t i", i=4),
+                g[h, o][:, LANES * lo : LANES * hi].rearrange("p (b i t) -> p b t i", t=LANES, i=4),
+                slope[:].rearrange("p t (b i) -> p b t i", i=4),
+                weight[h, o][:, :, lo:hi].rearrange("p t (b i) -> p b t i", i=4),
                 ALU.mult,
             )
 
         def quantize_g(h, o):
-            pos = slice(h * HALF_N, (h + 1) * HALF_N)
-            nc.vector.quantize_mx(out=g_codes[:, o, pos].bitcast(E5M2), scales=g_sc[:, o, pos], in_=g[h, o][:])
+            pos = slice((h + 1) * HALF_N, (h + 2) * HALF_N)
+            nc.vector.quantize_mx(out=g_codes[o][:, pos].bitcast(E5M2), scales=g_sc[o][:, pos], in_=g[h, o][:])
 
-        def project(tiles):
-            banks = {k: ps_dx.tile([P, N], F32, name="dx_ps") for k in tiles}
-            for k in tiles:
-                for o in range(PASSES):
-                    cols = slice(k * P, (k + 1) * P)
-                    nc.tensor.matmul_mx(
-                        out=banks[k][:], lhsT=wv_sb[:, o, cols].bitcast(E4M3), lhsT_scale=wv_sc[:, o, cols],
-                        rhs=g_codes[:, o, :].bitcast(E5M2), rhs_scale=g_sc[:, o, :], start=(o == 0), stop=(o == PASSES - 1),
-                    )
-            return banks
+        def project(k, tag, first):
+            bank = ps.tile([P, N], F32, name="dx_ps", tag=tag)
+            cols = slice(k * P, (k + 1) * P)
+            for o in range(PASSES):
+                nc.tensor.matmul_mx(
+                    out=bank[:], lhsT=wv_sb[:, o, cols].bitcast(E4M3), lhsT_scale=wv_sc[:, o, cols],
+                    rhs=g_codes[o][:, first : first + N].bitcast(E5M2), rhs_scale=g_sc[o][:, first : first + N], start=(o == 0), stop=(o == PASSES - 1),
+                )
+            return bank
 
         def unload(bank, k, lo, hi, tag):
-            dx = sb.tile([P, hi - lo], F32, name=f"dx{k}_{lo}", tag=tag)
+            dx = sb.tile([P, hi - lo], F32, name=f"dx_{tag}", tag=tag, align_bytes=64)
             nc.scalar.activation(dx[:], bank[:, lo:hi], ACT.Copy)
             return dx
 
         def scatter(dx, k, lo, hi):
             nc.vector.tensor_copy(windows[k][:].indirect(offsets[:, lo // 16 : hi // 16]), dx[:])
 
-        make_weight(0, "weight0")
-        residual(0, 0)
-        residual(0, 1)
-        make_weight(1, "picked")
-        weigh(0, 0)
-        weigh(0, 1)
-        quantize_g(0, 0)
-        quantize_g(0, 1)
-        early = project(range(EARLY_TILES))
-        residual(1, 0)
-        residual(1, 1)
-        weigh(1, 0)
-        early_dx0 = unload(early[0], 0, 0, HALF_N, "slope10")
-        weigh(1, 1)
-        early_dx1 = unload(early[1], 1, 0, HALF_N, "slope11")
-        quantize_g(1, 0)
-        quantize_g(1, 1)
-        late = project(range(D_TILES))
+        make_weight(0)
+        first = [slope_direct(0, 0, HALF_N, ("b0", "b1"))]
+        pick(1, "wd_raw1")
+        quantize_x(1, "y_sb00")
+        first.append(slope_direct(1, 0, HALF_N, ("b2", "b3")))
+        weigh(first[0], 0, 0, HALF_N)
+        third = [slope_direct(0, HALF_N, N - CHUNK, ("b0",))]
+        weigh(first[1], 1, 0, HALF_N)
+        third.append(slope_direct(1, HALF_N, N - CHUNK, ("b1",)))
+        last = [slope_turned(o, N - CHUNK, N, f"b{6 + o}", f"b{4 + o}", f"b{2 + o}") for o in range(PASSES)]
+        for o in range(PASSES):
+            quantize_g(0, o)
+        early = [project(k, f"b{6 + k}", 0) for k in range(EARLY_TILES)]
+        early_dx0 = unload(early[0], 0, HALF_N, N, "early0")
+        make_weight(1)
+        for o in range(PASSES):
+            weigh(third[o], o, HALF_N, N - CHUNK)
+        for o in range(PASSES):
+            weigh(last[o], o, N - CHUNK, N)
+        for o in range(PASSES):
+            quantize_g(1, o)
+        early_dx1 = unload(early[1], 1, HALF_N, N, "weight11")
+        late = [project(k, tag, HALF_N) for k, tag in enumerate(("b0", "b1", "b4", "b5"))]
         scatter(early_dx0, 0, 0, HALF_N)
         scatter(early_dx1, 1, 0, HALF_N)
         for k in range(D_TILES):

@@ -24,7 +24,6 @@ HALF_T = T // 2
 HALF_N = N // 2
 D_TILES = D // P
 CHUNK = 128
-VECTOR_WINDOWS = 2
 EARLY_TILES = 2
 VECTOR_CAST = 384
 X_LOADS = ((0, 0, HALF_T), (0, HALF_T, T), (1, 0, HALF_T), (1, HALF_T, T))
@@ -34,6 +33,8 @@ def tile_attend_gml_lch_kernel(tc, xT, wd_words, wd_scales, wv_words, wv_scales,
     nc = tc.nc
     with ExitStack() as ctx:
         sb = ctx.enter_context(tc.tile_pool(name="sb", bufs=1))
+        reuse = ctx.enter_context(tc.tile_pool(name="reuse", bufs=1))
+        reuse_x = ctx.enter_context(tc.tile_pool(name="reuse_x", bufs=1))
         ps = ctx.enter_context(tc.psum_pool(name="ps", bufs=1))
 
         offsets = sb.tile([P, N // 16], U16, name="offsets")
@@ -59,7 +60,10 @@ def tile_attend_gml_lch_kernel(tc, xT, wd_words, wd_scales, wv_words, wv_scales,
         x_rows = xT.rearrange("(p j) n -> p j n", j=LANES)
         x_raw = {}
         for u, lo, hi in X_LOADS:
-            x_raw[u, lo] = sb.tile([P, 2, hi - lo], F32, name=f"x_raw{u}_{lo}", tag=f"x_raw{u}_{lo}", align_bytes=64)
+            if (u, lo) == (1, HALF_T):
+                x_raw[u, lo] = reuse_x.tile([P, 2, hi - lo], F32, name=f"x_raw{u}_{lo}", offset=0, align_bytes=64)
+            else:
+                x_raw[u, lo] = sb.tile([P, 2, hi - lo], F32, name=f"x_raw{u}_{lo}")
             nc.sync.dma_start(x_raw[u, lo][:], x_rows[:, 2 * u : 2 * u + 2, lo:hi])
 
         wd_hbm = wd_words[0].rearrange("p v t -> p (v t)").bitcast(I32)
@@ -93,11 +97,9 @@ def tile_attend_gml_lch_kernel(tc, xT, wd_words, wd_scales, wv_words, wv_scales,
         make_identity(nc, ident[:])
 
         windows = []
-        for k in range(D // P):
-            window = sb.tile([P, T], F32, name=f"window{k}")
-            zeroing = nc.vector if k < VECTOR_WINDOWS else nc.gpsimd
-            zeroing.memset(window[:].bitcast(I32), 0)
-            windows.append(window)
+        for k in range(EARLY_TILES):
+            windows.append(sb.tile([P, T], F32, name=f"window{k}"))
+            nc.vector.memset(windows[k][:].bitcast(I32), 0)
 
         wd_sc = sb.tile([P, V], U8, name="wd_sc", align_bytes=64)
         nc.vector.tensor_copy(
@@ -105,8 +107,11 @@ def tile_attend_gml_lch_kernel(tc, xT, wd_words, wd_scales, wv_words, wv_scales,
             wd_sc_raw[:].rearrange("p (o m t) -> p o t m", o=PASSES, t=LANES),
         )
 
-        xg = [sb.tile([P, HALF_N * LANES], BF16, name=f"xg{h}", tag=tag, align_bytes=64) for h, tag in enumerate(("xg0", f"x_raw1_{HALF_T}"))]
-        xg_words = [xg[h][:].bitcast(U32).rearrange("p (i u) -> p i u", u=2) for h in range(2)]
+        xg = {}
+        for lo, tag in ((0, "xg0"), (CHUNK, "xg1")):
+            xg[lo] = sb.tile([P, CHUNK * LANES], BF16, name=f"xg{lo}", tag=tag, align_bytes=64)
+        xg[HALF_N] = reuse_x.tile([P, HALF_N * LANES], BF16, name="xg_late", offset=3 * T, align_bytes=64)
+        xg_words = {lo: xg[lo][:].bitcast(U32).rearrange("p (i u) -> p i u", u=2) for lo in xg}
         pairs = [sb.tile([P, 2 * T], BF16, name=f"pairs{u}") for u in range(2)]
 
         def cast(on_vector, u, base, lo, hi):
@@ -122,31 +127,38 @@ def tile_attend_gml_lch_kernel(tc, xT, wd_words, wd_scales, wv_words, wv_scales,
             nc.vector.tensor_copy(dst, pairs[u][:].bitcast(U32).indirect(offsets[:, lo // 16 : hi // 16]))
 
         def pick(u, tag):
-            picked = sb.tile([P, HALF_N], U32, name=f"picked{u}", tag=tag)
+            picked = sb.tile([P, HALF_N], U32, name=f"picked{u}", tag=tag, align_bytes=64)
             gather(picked[:], u, HALF_N, N)
-            nc.scalar.copy(xg_words[1][:, :, u], picked[:])
+            nc.scalar.copy(xg_words[HALF_N][:, :, u], picked[:])
 
-        wd_sb = sb.tile([P, V], I32, name="wd_sb", align_bytes=64)
+        wd_sb = {}
 
-        def permute_wd(o):
-            cols = slice(o * 512, (o + 1) * 512)
+        def permute_wd(o, tag):
+            wd_sb[o] = sb.tile([P, 512], I32, name=f"wd_sb{o}", tag=tag, align_bytes=64)
             nc.vector.tensor_copy(
-                wd_sb[:, cols].rearrange("p (t c i) -> p c t i", t=LANES, i=4),
+                wd_sb[o][:].rearrange("p (t c i) -> p c t i", t=LANES, i=4),
                 wd_raw[o][:].rearrange("p (c i t) -> p c t i", t=LANES, i=4),
             )
 
         x_codes, x_sc = {}, {}
 
-        def quantize_x(h, tag):
+        def quantize_x(h, tag, width):
             x_codes[h] = sb.tile([P, HALF_N], U32, name=f"x_codes{h}", tag=tag, align_bytes=64)
             x_sc[h] = sb.tile([P, HALF_N], U8, name=f"x_sc{h}", align_bytes=64)
-            nc.vector.quantize_mx(out=x_codes[h][:].bitcast(E4M3), scales=x_sc[h][:], in_=xg[h][:])
+            for lo in range(0, HALF_N, width):
+                nc.vector.quantize_mx(
+                    out=x_codes[h][:, lo : lo + width].bitcast(E4M3), scales=x_sc[h][:, lo : lo + width],
+                    in_=xg[h * HALF_N + lo][:],
+                )
 
         weight = {}
 
         def make_weight(h):
             for o in range(PASSES):
-                weight[h, o] = sb.tile([P, LANES, HALF_N], F32, name=f"weight{h}{o}", tag=f"weight{h}{o}", align_bytes=64)
+                if (h, o) == (1, 1):
+                    weight[h, o] = reuse.tile([P, LANES, HALF_N], F32, name=f"weight{h}{o}", offset=0)
+                else:
+                    weight[h, o] = sb.tile([P, LANES, HALF_N], F32, name=f"weight{h}{o}")
                 for t in range(LANES):
                     rows = rw_sb[:, h * HALF_N : (h + 1) * HALF_N]
                     if h == 0:
@@ -156,15 +168,17 @@ def tile_attend_gml_lch_kernel(tc, xT, wd_words, wd_scales, wv_words, wv_scales,
 
         cast(False, 0, 0, 0, HALF_T)
         cast(True, 0, HALF_T, 0, HALF_T)
-        gather(xg_words[0][:, :, 0], 0, 0, HALF_N)
+        for lo in range(0, HALF_N, CHUNK):
+            gather(xg_words[lo][:, :, 0], 0, lo, lo + CHUNK)
         pick(0, "picked0")
         cast(False, 1, 0, 0, HALF_T)
         cast(True, 1, HALF_T, 0, VECTOR_CAST)
         cast(False, 1, HALF_T, VECTOR_CAST, HALF_T)
-        gather(xg_words[0][:, :, 1], 1, 0, HALF_N)
-        permute_wd(0)
-        quantize_x(0, "x_codes0")
-        permute_wd(1)
+        for lo in range(0, HALF_N, CHUNK):
+            gather(xg_words[lo][:, :, 1], 1, lo, lo + CHUNK)
+        permute_wd(0, "wd_sb0")
+        quantize_x(0, "x_codes0", CHUNK)
+        permute_wd(1, "xg0")
 
         def scores(tag, o, planes, lo, hi):
             a = ps.tile([P, len(planes), hi - lo], F32, name="a", tag=tag)
@@ -174,7 +188,7 @@ def tile_attend_gml_lch_kernel(tc, xT, wd_words, wd_scales, wv_words, wv_scales,
                 j = o * LANES + t
                 cols = slice(j * P, (j + 1) * P)
                 nc.tensor.matmul_mx(
-                    out=a[:, e, :], lhsT=wd_sb[:, cols].bitcast(E4M3), lhsT_scale=wd_sc[:, cols],
+                    out=a[:, e, :], lhsT=wd_sb[o][:, t * P : (t + 1) * P].bitcast(E4M3), lhsT_scale=wd_sc[:, cols],
                     rhs=x_codes[h][:, pos].bitcast(E4M3), rhs_scale=x_sc[h][:, pos], start=True, stop=True,
                 )
             return a
@@ -185,25 +199,27 @@ def tile_attend_gml_lch_kernel(tc, xT, wd_words, wd_scales, wv_words, wv_scales,
 
         def slope_direct(o, lo, hi, tags):
             slope = sb.tile([P, LANES, hi - lo], F32, name=f"slope{o}_{lo}")
-            step = LANES // len(tags)
             for u, tag in enumerate(tags):
-                planes = range(u * step, (u + 1) * step)
-                a = scores(tag, o, planes, lo, hi)
-                diff = sb.tile([P, step, hi - lo], F32, name=f"diff{o}_{lo}_{u}")
-                nc.vector.tensor_tensor(diff[:], a[:], targets(o, lo, hi)[:, planes.start : planes.stop, :], ALU.subtract)
-                nc.scalar.activation(slope[:, planes.start : planes.stop, :], diff[:], ACT.Tanh)
+                first = lo + u * CHUNK
+                a = scores(tag, o, range(LANES), first, first + CHUNK)
+                diff = sb.tile([P, LANES, CHUNK], F32, name=f"diff{o}_{first}")
+                nc.vector.tensor_tensor(diff[:], a[:], targets(o, first, first + CHUNK), ALU.subtract)
+                nc.scalar.activation(slope[:, :, u * CHUNK : (u + 1) * CHUNK], diff[:], ACT.Tanh)
             return slope
 
-        def slope_turned(o, lo, hi, tag, tag_turned, tag_back):
+        def negate_scores(o, lo, hi, tag):
             a = scores(tag, o, range(LANES), lo, hi)
-            minus_a = sb.tile([P, LANES, CHUNK], F32, name=f"minus_a{o}")
+            minus_a = sb.tile([P, LANES, CHUNK], F32, name=f"minus_a{o}_{lo}")
             nc.scalar.activation(minus_a[:], a[:], ACT.Copy, scale=-1.0)
+            return minus_a
+
+        def slope_turned(minus_a, o, lo, hi, tag_turned, tag_back):
             diff = ps.tile([P, LANES, P], F32, name="diff_t", tag=tag_turned)
             for t in range(LANES):
                 nc.tensor.matmul(diff[:, t, :], targets(o, lo, hi)[:, t, :], ident[:], start=(t == 0), stop=False, is_transpose=True)
             for t in range(LANES):
                 nc.tensor.matmul(diff[:, t, :], minus_a[:, t, :], ident[:], start=False, stop=(t == LANES - 1), is_transpose=True)
-            slope_t = sb.tile([P, LANES, P], F32, name=f"slope_t{o}")
+            slope_t = sb.tile([P, LANES, P], F32, name=f"slope_t{o}_{lo}")
             nc.scalar.activation(slope_t[:], diff[:], ACT.Tanh, scale=-1.0)
             slope = ps.tile([P, LANES, CHUNK], F32, name="slope_ps", tag=tag_back)
             for t in range(LANES):
@@ -239,8 +255,7 @@ def tile_attend_gml_lch_kernel(tc, xT, wd_words, wd_scales, wv_words, wv_scales,
                 )
             return bank
 
-        def unload(bank, k, lo, hi, tag):
-            dx = sb.tile([P, hi - lo], F32, name=f"dx_{tag}", tag=tag, align_bytes=64)
+        def unload(dx, bank, lo, hi):
             nc.scalar.activation(dx[:], bank[:, lo:hi], ACT.Copy)
             return dx
 
@@ -249,18 +264,21 @@ def tile_attend_gml_lch_kernel(tc, xT, wd_words, wd_scales, wv_words, wv_scales,
 
         make_weight(0)
         first = [slope_direct(0, 0, HALF_N, ("b0", "b1"))]
-        pick(1, "wd_raw1")
-        quantize_x(1, "y_sb00")
+        pick(1, "xg1")
+        quantize_x(1, "y_sb00", HALF_N)
+        for k in range(EARLY_TILES, D_TILES):
+            windows.append(reuse_x.tile([P, T], F32, name=f"window{k}", offset=(k - EARLY_TILES) * 4 * T, align_bytes=64))
+            nc.gpsimd.memset(windows[k][:].bitcast(I32), 0)
         first.append(slope_direct(1, 0, HALF_N, ("b2", "b3")))
+        negated = [negate_scores(o, N - CHUNK, N, f"b{6 + o}") for o in range(PASSES)]
         weigh(first[0], 0, 0, HALF_N)
         third = [slope_direct(0, HALF_N, N - CHUNK, ("b0",))]
         weigh(first[1], 1, 0, HALF_N)
         third.append(slope_direct(1, HALF_N, N - CHUNK, ("b1",)))
-        last = [slope_turned(o, N - CHUNK, N, f"b{6 + o}", f"b{4 + o}", f"b{2 + o}") for o in range(PASSES)]
+        last = [slope_turned(negated[o], o, N - CHUNK, N, f"b{4 + o}", f"b{2 + o}") for o in range(PASSES)]
         for o in range(PASSES):
             quantize_g(0, o)
         early = [project(k, f"b{6 + k}", 0) for k in range(EARLY_TILES)]
-        early_dx0 = unload(early[0], 0, HALF_N, N, "early0")
         make_weight(1)
         for o in range(PASSES):
             weigh(third[o], o, HALF_N, N - CHUNK)
@@ -268,11 +286,11 @@ def tile_attend_gml_lch_kernel(tc, xT, wd_words, wd_scales, wv_words, wv_scales,
             weigh(last[o], o, N - CHUNK, N)
         for o in range(PASSES):
             quantize_g(1, o)
-        early_dx1 = unload(early[1], 1, HALF_N, N, "weight11")
+        early_dx = [unload(reuse.tile([P, HALF_N], F32, name=f"early_dx{k}", offset=k * HALF_N * 4), early[k], HALF_N, N) for k in range(EARLY_TILES)]
         late = [project(k, tag, HALF_N) for k, tag in enumerate(("b0", "b1", "b4", "b5"))]
-        scatter(early_dx0, 0, 0, HALF_N)
-        scatter(early_dx1, 1, 0, HALF_N)
+        for k in range(EARLY_TILES):
+            scatter(early_dx[k], k, 0, HALF_N)
         for k in range(D_TILES):
             lo = HALF_N if k < EARLY_TILES else 0
-            scatter(unload(late[k], k, lo, N, f"late{k}"), k, lo, N)
+            scatter(unload(sb.tile([P, N - lo], F32, name=f"late_dx{k}"), late[k], lo, N), k, lo, N)
             nc.sync.dma_start(out[k * P : (k + 1) * P, :], windows[k][:])

@@ -25,8 +25,9 @@ HALF_N = N // 2
 D_TILES = D // P
 CHUNK = 128
 EARLY_TILES = 2
-VECTOR_CAST = 384
-X_LOADS = ((0, 0, HALF_T), (0, HALF_T, T), (1, 0, HALF_T), (1, HALF_T, T))
+VECTOR_CAST = 320
+VECTOR_CAST_FIRST = 640
+X_LOADS = ((0, 0, T), (1, 0, HALF_T), (1, HALF_T, T))
 
 
 def tile_attend_gml_lch_kernel(tc, xT, wd_words, wd_scales, wv_words, wv_scales, y, cw, rw, offs, out):
@@ -166,8 +167,8 @@ def tile_attend_gml_lch_kernel(tc, xT, wd_words, wd_scales, wv_words, wv_scales,
                     else:
                         nc.scalar.activation(weight[h, o][:, t, :], rows, ACT.Copy, scale=cw_sb[:, o, t : t + 1])
 
-        cast(False, 0, 0, 0, HALF_T)
-        cast(True, 0, HALF_T, 0, HALF_T)
+        cast(True, 0, 0, 0, VECTOR_CAST_FIRST)
+        cast(False, 0, 0, VECTOR_CAST_FIRST, T)
         for lo in range(0, HALF_N, CHUNK):
             gather(xg_words[lo][:, :, 0], 0, lo, lo + CHUNK)
         pick(0, "picked0")

@@ -19,15 +19,27 @@ ALU = mybir.AluOpType
 
 P = 128
 LANES = 4
-PASSES = V // (P * LANES)
+K_PASS = P * LANES
+PASSES = V // K_PASS
+SCALE_ROWS = 4
+BAND = 16
+RUN = 4
 HALF_T = T // 2
 HALF_N = N // 2
 D_TILES = D // P
 CHUNK = 128
+LAST_CHUNK = N - CHUNK
 EARLY_TILES = 2
-VECTOR_CAST = 320
-VECTOR_CAST_FIRST = 640
+
 X_LOADS = ((0, 0, T), (1, 0, HALF_T), (1, HALF_T, T))
+VECTOR_CAST_FIRST = 768
+VECTOR_CAST_LAST = 320
+
+WINDOW_BYTES = 4 * T
+AT_LAST_WEIGHT = 0
+AT_LATE_WINDOWS = WINDOW_BYTES
+AT_LATE_X = 2 * WINDOW_BYTES - 1024
+AT_LAST_X_LOAD = WINDOW_BYTES - 512
 
 
 def tile_attend_gml_lch_kernel(tc, xT, wd_words, wd_scales, wv_words, wv_scales, y, cw, rw, offs, out):
@@ -35,57 +47,46 @@ def tile_attend_gml_lch_kernel(tc, xT, wd_words, wd_scales, wv_words, wv_scales,
     with ExitStack() as ctx:
         sb = ctx.enter_context(tc.tile_pool(name="sb", bufs=1))
         reuse = ctx.enter_context(tc.tile_pool(name="reuse", bufs=1))
-        reuse_x = ctx.enter_context(tc.tile_pool(name="reuse_x", bufs=1))
         ps = ctx.enter_context(tc.psum_pool(name="ps", bufs=1))
 
-        offsets = sb.tile([P, N // 16], U16, name="offsets")
-        nc.sync.dma_start(offsets[:], offs)
+        offsets = sb.tile([P, N // BAND], U16, name="offsets")
 
         wd_sc_raw = sb.tile([P, V], U8, name="wd_sc_raw", align_bytes=64)
         wv_sc = sb.tile([P, PASSES, D], U8, name="wv_sc", align_bytes=64)
-        warm = sb.tile([P, 8], F32, name="warm")
         nc.gpsimd.memset(wd_sc_raw[:].bitcast(I32), 0)
-        nc.vector.memset(warm[:], 0.0)
         nc.gpsimd.memset(wv_sc[:].rearrange("p o d -> p (o d)").bitcast(I32), 0)
 
         rw_sb = sb.tile([P, N], F32, name="rw_sb")
         nc.sync.dma_start(rw_sb[:], rw)
         cw_sb = sb.tile([P, PASSES, 8], F32, name="cw_sb")
         nc.sync.dma_start(cw_sb[:, :, 0:LANES], cw.rearrange("(o p t) e -> p o (t e)", p=P, t=LANES))
-        wd_sc_rows = wd_scales[0].rearrange("(q r) v -> r q v", r=4)
-        for r in range(4):
+        nc.sync.dma_start(offsets[:], offs)
+        wd_sc_rows = wd_scales[0].rearrange("(q r) v -> r q v", r=SCALE_ROWS)
+        for r in range(SCALE_ROWS):
             nc.sync.dma_start(wd_sc_raw[r:P:32, :].bitcast(I32), wd_sc_rows[r].bitcast(I32))
-        warm_out = sb.tile([P, 8], F32, name="warm_out")
-        nc.scalar.activation(warm_out[:], warm[:], ACT.Tanh)
 
-        x_rows = xT.rearrange("(p j) n -> p j n", j=LANES)
+        x_rows = xT.rearrange("(p t) n -> p t n", t=LANES)
         x_raw = {}
         for u, lo, hi in X_LOADS:
-            if (u, lo) == (1, HALF_T):
-                x_raw[u, lo] = reuse_x.tile([P, 2, hi - lo], F32, name=f"x_raw{u}_{lo}", offset=0, align_bytes=64)
+            if (u, lo, hi) == X_LOADS[-1]:
+                x_raw[u, lo] = reuse.tile([P, 2, hi - lo], F32, name=f"x_raw{u}_{lo}", offset=AT_LAST_X_LOAD, align_bytes=64)
             else:
                 x_raw[u, lo] = sb.tile([P, 2, hi - lo], F32, name=f"x_raw{u}_{lo}")
             nc.sync.dma_start(x_raw[u, lo][:], x_rows[:, 2 * u : 2 * u + 2, lo:hi])
 
         wd_hbm = wd_words[0].rearrange("p v t -> p (v t)").bitcast(I32)
-        wd_raw = [sb.tile([P, 512], I32, name=f"wd_raw{o}", tag=f"wd_raw{o}") for o in range(PASSES)]
-        wv_sc_rows = wv_scales.rearrange("o (q r) d -> r q o d", r=4)
-
+        wd_raw = [sb.tile([P, K_PASS], I32, name=f"wd_raw{o}") for o in range(PASSES)]
+        wv_sc_rows = wv_scales.rearrange("o (q r) d -> r q o d", r=SCALE_ROWS)
         y_rows = y.rearrange("(o p t) i -> o p t i", p=P, t=LANES)
         y_sb = {}
         wv_sb = sb.tile([P, PASSES, D], I32, name="wv_sb", align_bytes=64)
-
-        def load_y(o, h):
-            y_sb[o, h] = sb.tile([P, LANES, HALF_N], F32, name=f"y_sb{o}{h}", tag=f"y_sb{o}{h}", align_bytes=64)
-            nc.sync.dma_start(y_sb[o, h][:], y_rows[o][:, :, h * HALF_N : (h + 1) * HALF_N])
-
         for o in range(PASSES):
-            nc.sync.dma_start(wd_raw[o][:], wd_hbm[:, o * 512 : (o + 1) * 512])
-        load_y(0, 0)
-        load_y(1, 0)
-        load_y(0, 1)
-        load_y(1, 1)
-        for r in range(4):
+            nc.sync.dma_start(wd_raw[o][:], wd_hbm[:, o * K_PASS : (o + 1) * K_PASS])
+        for h in range(2):
+            for o in range(PASSES):
+                y_sb[o, h] = sb.tile([P, LANES, HALF_N], F32, name=f"y_sb{o}{h}", tag=f"y_sb{o}{h}", align_bytes=64)
+                nc.sync.dma_start(y_sb[o, h][:], y_rows[o][:, :, h * HALF_N : (h + 1) * HALF_N])
+        for r in range(SCALE_ROWS):
             nc.sync.dma_start(wv_sc[r:P:32, :, :].bitcast(I32), wv_sc_rows[r].bitcast(I32))
         nc.sync.dma_start(wv_sb[:], wv_words.rearrange("o p d t -> p o (d t)").bitcast(I32))
 
@@ -110,8 +111,8 @@ def tile_attend_gml_lch_kernel(tc, xT, wd_words, wd_scales, wv_words, wv_scales,
 
         xg = {}
         for lo, tag in ((0, "xg0"), (CHUNK, "xg1")):
-            xg[lo] = sb.tile([P, CHUNK * LANES], BF16, name=f"xg{lo}", tag=tag, align_bytes=64)
-        xg[HALF_N] = reuse_x.tile([P, HALF_N * LANES], BF16, name="xg_late", offset=3 * T, align_bytes=64)
+            xg[lo] = sb.tile([P, CHUNK * LANES], BF16, name=tag, tag=tag, align_bytes=64)
+        xg[HALF_N] = reuse.tile([P, HALF_N * LANES], BF16, name="xg_late", offset=AT_LATE_X, align_bytes=64)
         xg_words = {lo: xg[lo][:].bitcast(U32).rearrange("p (i u) -> p i u", u=2) for lo in xg}
         pairs = [sb.tile([P, 2 * T], BF16, name=f"pairs{u}") for u in range(2)]
 
@@ -123,22 +124,25 @@ def tile_attend_gml_lch_kernel(tc, xT, wd_words, wd_scales, wv_words, wv_scales,
             else:
                 nc.scalar.activation(dst, src, ACT.Copy)
 
-
         def gather(dst, u, lo, hi):
-            nc.vector.tensor_copy(dst, pairs[u][:].bitcast(U32).indirect(offsets[:, lo // 16 : hi // 16]))
+            nc.vector.tensor_copy(dst, pairs[u][:].bitcast(U32).indirect(offsets[:, lo // BAND : hi // BAND]))
 
-        def pick(u, tag):
+        def gather_first_half(u):
+            for lo in range(0, HALF_N, CHUNK):
+                gather(xg_words[lo][:, :, u], u, lo, lo + CHUNK)
+
+        def gather_second_half(u, tag):
             picked = sb.tile([P, HALF_N], U32, name=f"picked{u}", tag=tag, align_bytes=64)
             gather(picked[:], u, HALF_N, N)
             nc.scalar.copy(xg_words[HALF_N][:, :, u], picked[:])
 
         wd_sb = {}
 
-        def permute_wd(o, tag):
-            wd_sb[o] = sb.tile([P, 512], I32, name=f"wd_sb{o}", tag=tag, align_bytes=64)
+        def deal_wd(o, tag):
+            wd_sb[o] = sb.tile([P, K_PASS], I32, name=f"wd_sb{o}", tag=tag, align_bytes=64)
             nc.vector.tensor_copy(
-                wd_sb[o][:].rearrange("p (t c i) -> p c t i", t=LANES, i=4),
-                wd_raw[o][:].rearrange("p (c i t) -> p c t i", t=LANES, i=4),
+                wd_sb[o][:].rearrange("p (t c i) -> p c t i", t=LANES, i=RUN),
+                wd_raw[o][:].rearrange("p (c i t) -> p c t i", t=LANES, i=RUN),
             )
 
         x_codes, x_sc = {}, {}
@@ -155,90 +159,72 @@ def tile_attend_gml_lch_kernel(tc, xT, wd_words, wd_scales, wv_words, wv_scales,
         weight = {}
 
         def make_weight(h):
+            rows = rw_sb[:, h * HALF_N : (h + 1) * HALF_N]
             for o in range(PASSES):
-                if (h, o) == (1, 1):
-                    weight[h, o] = reuse.tile([P, LANES, HALF_N], F32, name=f"weight{h}{o}", offset=0)
+                if (h, o) == (1, PASSES - 1):
+                    weight[h, o] = reuse.tile([P, LANES, HALF_N], F32, name=f"weight{h}{o}", offset=AT_LAST_WEIGHT, align_bytes=64)
                 else:
                     weight[h, o] = sb.tile([P, LANES, HALF_N], F32, name=f"weight{h}{o}")
                 for t in range(LANES):
-                    rows = rw_sb[:, h * HALF_N : (h + 1) * HALF_N]
                     if h == 0:
                         nc.vector.tensor_scalar(weight[h, o][:, t, :], rows, cw_sb[:, o, t : t + 1], None, ALU.mult)
                     else:
                         nc.scalar.activation(weight[h, o][:, t, :], rows, ACT.Copy, scale=cw_sb[:, o, t : t + 1])
 
-        cast(True, 0, 0, 0, VECTOR_CAST_FIRST)
-        cast(False, 0, 0, VECTOR_CAST_FIRST, T)
-        for lo in range(0, HALF_N, CHUNK):
-            gather(xg_words[lo][:, :, 0], 0, lo, lo + CHUNK)
-        pick(0, "picked0")
-        cast(False, 1, 0, 0, HALF_T)
-        cast(True, 1, HALF_T, 0, VECTOR_CAST)
-        cast(False, 1, HALF_T, VECTOR_CAST, HALF_T)
-        for lo in range(0, HALF_N, CHUNK):
-            gather(xg_words[lo][:, :, 1], 1, lo, lo + CHUNK)
-        permute_wd(0, "wd_sb0")
-        quantize_x(0, "x_codes0", CHUNK)
-        permute_wd(1, "xg0")
-
-        def scores(tag, o, planes, lo, hi):
-            a = ps.tile([P, len(planes), hi - lo], F32, name="a", tag=tag)
-            h = lo // HALF_N
-            pos = slice(lo - h * HALF_N, hi - h * HALF_N)
-            for e, t in enumerate(planes):
-                j = o * LANES + t
-                cols = slice(j * P, (j + 1) * P)
+        def scores(o, lo, bank):
+            a = ps.tile([P, LANES, CHUNK], F32, name="a", tag=bank)
+            h, start = divmod(lo, HALF_N)
+            pos = slice(start, start + CHUNK)
+            for t in range(LANES):
                 nc.tensor.matmul_mx(
-                    out=a[:, e, :], lhsT=wd_sb[o][:, t * P : (t + 1) * P].bitcast(E4M3), lhsT_scale=wd_sc[:, cols],
+                    out=a[:, t, :], lhsT=wd_sb[o][:, t * P : (t + 1) * P].bitcast(E4M3),
+                    lhsT_scale=wd_sc[:, o * K_PASS + t * P : o * K_PASS + (t + 1) * P],
                     rhs=x_codes[h][:, pos].bitcast(E4M3), rhs_scale=x_sc[h][:, pos], start=True, stop=True,
                 )
             return a
 
-        def targets(o, lo, hi):
-            h = lo // HALF_N
-            return y_sb[o, h][:, :, lo - h * HALF_N : hi - h * HALF_N]
+        def targets(o, lo):
+            h, start = divmod(lo, HALF_N)
+            return y_sb[o, h][:, :, start : start + CHUNK]
 
-        def slope_direct(o, lo, hi, tags):
-            slope = sb.tile([P, LANES, hi - lo], F32, name=f"slope{o}_{lo}")
-            for u, tag in enumerate(tags):
-                first = lo + u * CHUNK
-                a = scores(tag, o, range(LANES), first, first + CHUNK)
-                diff = sb.tile([P, LANES, CHUNK], F32, name=f"diff{o}_{first}")
-                nc.vector.tensor_tensor(diff[:], a[:], targets(o, first, first + CHUNK), ALU.subtract)
-                nc.scalar.activation(slope[:, :, u * CHUNK : (u + 1) * CHUNK], diff[:], ACT.Tanh)
+        def slope_direct(o, lo, banks):
+            slope = sb.tile([P, LANES, len(banks) * CHUNK], F32, name=f"slope{o}_{lo}")
+            for c, bank in enumerate(banks):
+                chunk_lo = lo + c * CHUNK
+                a = scores(o, chunk_lo, bank)
+                diff = sb.tile([P, LANES, CHUNK], F32, name=f"diff{o}_{chunk_lo}")
+                nc.vector.tensor_tensor(diff[:], a[:], targets(o, chunk_lo), ALU.subtract)
+                nc.scalar.activation(slope[:, :, c * CHUNK : (c + 1) * CHUNK], diff[:], ACT.Tanh)
             return slope
 
-        def negate_scores(o, lo, hi, tag):
-            a = scores(tag, o, range(LANES), lo, hi)
-            minus_a = sb.tile([P, LANES, CHUNK], F32, name=f"minus_a{o}_{lo}")
+        def negated_scores(o, bank):
+            a = scores(o, LAST_CHUNK, bank)
+            minus_a = sb.tile([P, LANES, CHUNK], F32, name=f"minus_a{o}")
             nc.scalar.activation(minus_a[:], a[:], ACT.Copy, scale=-1.0)
             return minus_a
 
-        def slope_turned(minus_a, o, lo, hi, tag_turned, tag_back):
-            diff = ps.tile([P, LANES, P], F32, name="diff_t", tag=tag_turned)
+        def slope_turned(minus_a, o, bank_sum, bank_back):
+            y_minus_a = ps.tile([P, LANES, P], F32, name="y_minus_a", tag=bank_sum)
             for t in range(LANES):
-                nc.tensor.matmul(diff[:, t, :], targets(o, lo, hi)[:, t, :], ident[:], start=(t == 0), stop=False, is_transpose=True)
+                nc.tensor.matmul(y_minus_a[:, t, :], targets(o, LAST_CHUNK)[:, t, :], ident[:], start=(t == 0), stop=False, is_transpose=True)
             for t in range(LANES):
-                nc.tensor.matmul(diff[:, t, :], minus_a[:, t, :], ident[:], start=False, stop=(t == LANES - 1), is_transpose=True)
-            slope_t = sb.tile([P, LANES, P], F32, name=f"slope_t{o}_{lo}")
-            nc.scalar.activation(slope_t[:], diff[:], ACT.Tanh, scale=-1.0)
-            slope = ps.tile([P, LANES, CHUNK], F32, name="slope_ps", tag=tag_back)
+                nc.tensor.matmul(y_minus_a[:, t, :], minus_a[:, t, :], ident[:], start=False, stop=(t == LANES - 1), is_transpose=True)
+            slope_t = sb.tile([P, LANES, P], F32, name=f"slope_t{o}")
+            nc.scalar.activation(slope_t[:], y_minus_a[:], ACT.Tanh, scale=-1.0)
+            slope = ps.tile([P, LANES, CHUNK], F32, name="slope_ps", tag=bank_back)
             for t in range(LANES):
                 nc.tensor.transpose(slope[:, t, :], slope_t[:, t, :], ident[:])
             return slope
 
         g = {}
-        for h in range(2):
-            for o in range(PASSES):
-                g[h, o] = sb.tile([P, HALF_N * LANES], BF16, name=f"g{h}{o}", align_bytes=64)
 
         def weigh(slope, o, lo, hi):
-            h = lo // HALF_N
-            lo, hi = lo - h * HALF_N, hi - h * HALF_N
+            h, start = divmod(lo, HALF_N)
+            end = start + hi - lo
             nc.vector.tensor_tensor(
-                g[h, o][:, LANES * lo : LANES * hi].rearrange("p (b i t) -> p b t i", t=LANES, i=4),
-                slope[:].rearrange("p t (b i) -> p b t i", i=4),
-                weight[h, o][:, :, lo:hi].rearrange("p t (b i) -> p b t i", i=4),
+                g[h, o][:, LANES * start : LANES * end].rearrange("p (b i t) -> p b t i", t=LANES, i=RUN),
+                slope[:].rearrange("p t (b i) -> p b t i", i=RUN),
+                weight[h, o][:, :, start:end].rearrange("p t (b i) -> p b t i", i=RUN),
                 ALU.mult,
             )
 
@@ -246,52 +232,73 @@ def tile_attend_gml_lch_kernel(tc, xT, wd_words, wd_scales, wv_words, wv_scales,
             pos = slice((h + 1) * HALF_N, (h + 2) * HALF_N)
             nc.vector.quantize_mx(out=g_codes[o][:, pos].bitcast(E5M2), scales=g_sc[o][:, pos], in_=g[h, o][:])
 
-        def project(k, tag, first):
-            bank = ps.tile([P, N], F32, name="dx_ps", tag=tag)
+        def project(k, bank, g_col):
+            dx_ps = ps.tile([P, N], F32, name="dx_ps", tag=bank)
             cols = slice(k * P, (k + 1) * P)
             for o in range(PASSES):
                 nc.tensor.matmul_mx(
-                    out=bank[:], lhsT=wv_sb[:, o, cols].bitcast(E4M3), lhsT_scale=wv_sc[:, o, cols],
-                    rhs=g_codes[o][:, first : first + N].bitcast(E5M2), rhs_scale=g_sc[o][:, first : first + N], start=(o == 0), stop=(o == PASSES - 1),
+                    out=dx_ps[:], lhsT=wv_sb[:, o, cols].bitcast(E4M3), lhsT_scale=wv_sc[:, o, cols],
+                    rhs=g_codes[o][:, g_col : g_col + N].bitcast(E5M2), rhs_scale=g_sc[o][:, g_col : g_col + N],
+                    start=(o == 0), stop=(o == PASSES - 1),
                 )
-            return bank
+            return dx_ps
 
-        def unload(dx, bank, lo, hi):
-            nc.scalar.activation(dx[:], bank[:, lo:hi], ACT.Copy)
+        def unload(dx, dx_ps, lo):
+            nc.scalar.activation(dx[:], dx_ps[:, lo:N], ACT.Copy)
             return dx
 
         def scatter(dx, k, lo, hi):
-            nc.vector.tensor_copy(windows[k][:].indirect(offsets[:, lo // 16 : hi // 16]), dx[:])
+            nc.vector.tensor_copy(windows[k][:].indirect(offsets[:, lo // BAND : hi // BAND]), dx[:])
 
-        make_weight(0)
-        first = [slope_direct(0, 0, HALF_N, ("b0", "b1"))]
-        pick(1, "xg1")
+        cast(True, 0, 0, 0, VECTOR_CAST_FIRST)
+        cast(False, 0, 0, VECTOR_CAST_FIRST, T)
+        gather_first_half(0)
+        gather_second_half(0, "picked0")
+        cast(False, 1, 0, 0, HALF_T)
+        cast(True, 1, HALF_T, 0, VECTOR_CAST_LAST)
+        cast(False, 1, HALF_T, VECTOR_CAST_LAST, HALF_T)
+        gather_first_half(1)
+        deal_wd(0, "wd_sb0")
+        quantize_x(0, "x_codes0", CHUNK)
+        deal_wd(1, "xg0")
+        for h in range(2):
+            for o in range(PASSES):
+                g[h, o] = sb.tile([P, HALF_N * LANES], BF16, name=f"g{h}{o}", align_bytes=64)
+        for h in range(2):
+            make_weight(h)
+        gather_second_half(1, "xg1")
+
+        first_half = [slope_direct(0, 0, ("b0", "b1"))]
         quantize_x(1, "y_sb00", HALF_N)
-        for k in range(EARLY_TILES, D_TILES):
-            windows.append(reuse_x.tile([P, T], F32, name=f"window{k}", offset=(k - EARLY_TILES) * 4 * T, align_bytes=64))
-            nc.gpsimd.memset(windows[k][:].bitcast(I32), 0)
-        first.append(slope_direct(1, 0, HALF_N, ("b2", "b3")))
-        negated = [negate_scores(o, N - CHUNK, N, f"b{6 + o}") for o in range(PASSES)]
-        weigh(first[0], 0, 0, HALF_N)
-        third = [slope_direct(0, HALF_N, N - CHUNK, ("b0",))]
-        weigh(first[1], 1, 0, HALF_N)
-        third.append(slope_direct(1, HALF_N, N - CHUNK, ("b1",)))
-        last = [slope_turned(negated[o], o, N - CHUNK, N, f"b{4 + o}", f"b{2 + o}") for o in range(PASSES)]
+        for e in range(D_TILES - EARLY_TILES):
+            windows.append(reuse.tile([P, T], F32, name=f"late_window{e}", offset=AT_LATE_WINDOWS + e * WINDOW_BYTES, align_bytes=64))
+            nc.gpsimd.memset(windows[-1][:].bitcast(I32), 0)
+        first_half.append(slope_direct(1, 0, ("b2", "b3")))
+        negated = [negated_scores(o, f"b{6 + o}") for o in range(PASSES)]
+        third_chunk = []
+        for o in range(PASSES):
+            weigh(first_half[o], o, 0, HALF_N)
+            third_chunk.append(slope_direct(o, HALF_N, (f"b{o}",)))
+        last_chunk = [slope_turned(negated[o], o, f"b{4 + o}", f"b{2 + o}") for o in range(PASSES)]
         for o in range(PASSES):
             quantize_g(0, o)
-        early = [project(k, f"b{6 + k}", 0) for k in range(EARLY_TILES)]
-        make_weight(1)
+        early_ps = [project(k, f"b{6 + k}", 0) for k in range(EARLY_TILES)]
+
         for o in range(PASSES):
-            weigh(third[o], o, HALF_N, N - CHUNK)
+            weigh(third_chunk[o], o, HALF_N, LAST_CHUNK)
         for o in range(PASSES):
-            weigh(last[o], o, N - CHUNK, N)
+            weigh(last_chunk[o], o, LAST_CHUNK, N)
         for o in range(PASSES):
             quantize_g(1, o)
-        early_dx = [unload(reuse.tile([P, HALF_N], F32, name=f"early_dx{k}", offset=k * HALF_N * 4), early[k], HALF_N, N) for k in range(EARLY_TILES)]
-        late = [project(k, tag, HALF_N) for k, tag in enumerate(("b0", "b1", "b4", "b5"))]
+        early_dx = []
+        for k in range(EARLY_TILES):
+            dx = reuse.tile([P, HALF_N], F32, name=f"early_dx{k}", offset=AT_LAST_WEIGHT + k * HALF_N * 4, align_bytes=64)
+            early_dx.append(unload(dx, early_ps[k], HALF_N))
+        whole_ps = [project(k, bank, HALF_N) for k, bank in enumerate(("b0", "b1", "b4", "b5"))]
+
         for k in range(EARLY_TILES):
             scatter(early_dx[k], k, 0, HALF_N)
         for k in range(D_TILES):
             lo = HALF_N if k < EARLY_TILES else 0
-            scatter(unload(sb.tile([P, N - lo], F32, name=f"late_dx{k}"), late[k], lo, N), k, lo, N)
+            scatter(unload(sb.tile([P, N - lo], F32, name=f"whole_dx{k}"), whole_ps[k], lo), k, lo, N)
             nc.sync.dma_start(out[k * P : (k + 1) * P, :], windows[k][:])

@@ -24,6 +24,7 @@ PASSES = V // K_PASS
 SCALE_ROWS = 4
 BAND = 16
 RUN = 4
+PAIR = 2
 HALF_T = T // 2
 HALF_N = N // 2
 D_TILES = D // P
@@ -222,9 +223,9 @@ def tile_attend_gml_lch_kernel(tc, xT, wd_words, wd_scales, wv_words, wv_scales,
             h, start = divmod(lo, HALF_N)
             end = start + hi - lo
             nc.vector.tensor_tensor(
-                g[h, o][:, LANES * start : LANES * end].rearrange("p (b i t) -> p b t i", t=LANES, i=RUN),
-                slope[:].rearrange("p t (b i) -> p b t i", i=RUN),
-                weight[h, o][:, :, start:end].rearrange("p t (b i) -> p b t i", i=RUN),
+                g[h, o][:, LANES * start : LANES * end].rearrange("p (b i t) -> p b t i", t=LANES, i=PAIR),
+                slope[:].rearrange("p t (b i) -> p b t i", i=PAIR),
+                weight[h, o][:, :, start:end].rearrange("p t (b i) -> p b t i", i=PAIR),
                 ALU.mult,
             )
 

@@ -32,15 +32,17 @@ CHUNK = 128
 LAST_CHUNK = N - CHUNK
 EARLY_TILES = 2
 
-X_LOADS = ((0, 0, T), (1, 0, HALF_T), (1, HALF_T, T))
-VECTOR_CAST_FIRST = 768
-VECTOR_CAST_LAST = 320
+X_SPLIT = 512
+X_LOADS = ((0, 0, HALF_T), (0, HALF_T, T), (1, 0, X_SPLIT), (1, X_SPLIT, T))
+VECTOR_PLANES = 6
+VECTOR_CAST_THIRD = 128
+VECTOR_CAST_LAST = 384
 
 WINDOW_BYTES = 4 * T
 AT_LAST_WEIGHT = 0
-AT_LATE_WINDOWS = WINDOW_BYTES
-AT_LATE_X = 2 * WINDOW_BYTES - 1024
-AT_LAST_X_LOAD = WINDOW_BYTES - 512
+AT_LATE_WINDOWS = 2 * WINDOW_BYTES
+AT_LATE_X = 3 * WINDOW_BYTES - 1024
+AT_LAST_X_LOAD = 2 * WINDOW_BYTES
 
 
 def tile_attend_gml_lch_kernel(tc, xT, wd_words, wd_scales, wv_words, wv_scales, y, cw, rw, offs, out):
@@ -52,7 +54,7 @@ def tile_attend_gml_lch_kernel(tc, xT, wd_words, wd_scales, wv_words, wv_scales,
 
         offsets = sb.tile([P, N // BAND], U16, name="offsets")
 
-        wd_sc_raw = sb.tile([P, V], U8, name="wd_sc_raw", align_bytes=64)
+        wd_sc_raw = sb.tile([P, K_PASS], U8, name="wd_sc_raw", align_bytes=64)
         wv_sc = sb.tile([P, PASSES, D], U8, name="wv_sc", align_bytes=64)
         nc.gpsimd.memset(wd_sc_raw[:].bitcast(I32), 0)
         nc.gpsimd.memset(wv_sc[:].rearrange("p o d -> p (o d)").bitcast(I32), 0)
@@ -61,10 +63,9 @@ def tile_attend_gml_lch_kernel(tc, xT, wd_words, wd_scales, wv_words, wv_scales,
         nc.sync.dma_start(rw_sb[:], rw)
         cw_sb = sb.tile([P, PASSES, 8], F32, name="cw_sb")
         nc.sync.dma_start(cw_sb[:, :, 0:LANES], cw.rearrange("(o p t) e -> p o (t e)", p=P, t=LANES))
-        nc.sync.dma_start(offsets[:], offs)
-        wd_sc_rows = wd_scales[0].rearrange("(q r) v -> r q v", r=SCALE_ROWS)
-        for r in range(SCALE_ROWS):
-            nc.sync.dma_start(wd_sc_raw[r:P:32, :].bitcast(I32), wd_sc_rows[r].bitcast(I32))
+        wd_sc_rows = wd_scales[0].bitcast(I32).rearrange("(q r) (o c) -> q o r c", r=SCALE_ROWS, o=PASSES)
+        for q in range(P // 32):
+            nc.sync.dma_start(wd_sc_raw[32 * q : 32 * q + PASSES * SCALE_ROWS, :].bitcast(I32), wd_sc_rows[q])
 
         x_rows = xT.rearrange("(p t) n -> p t n", t=LANES)
         x_raw = {}
@@ -74,6 +75,8 @@ def tile_attend_gml_lch_kernel(tc, xT, wd_words, wd_scales, wv_words, wv_scales,
             else:
                 x_raw[u, lo] = sb.tile([P, 2, hi - lo], F32, name=f"x_raw{u}_{lo}")
             nc.sync.dma_start(x_raw[u, lo][:], x_rows[:, 2 * u : 2 * u + 2, lo:hi])
+            if (u, lo, hi) == X_LOADS[1]:
+                nc.sync.dma_start(offsets[:], offs)
 
         wd_hbm = wd_words[0].rearrange("p v t -> p (v t)").bitcast(I32)
         wd_raw = [sb.tile([P, K_PASS], I32, name=f"wd_raw{o}") for o in range(PASSES)]
@@ -102,12 +105,12 @@ def tile_attend_gml_lch_kernel(tc, xT, wd_words, wd_scales, wv_words, wv_scales,
         windows = []
         for k in range(EARLY_TILES):
             windows.append(sb.tile([P, T], F32, name=f"window{k}"))
-            nc.vector.memset(windows[k][:].bitcast(I32), 0)
+            (nc.vector if k == 0 else nc.gpsimd).memset(windows[k][:].bitcast(I32), 0)
 
-        wd_sc = sb.tile([P, V], U8, name="wd_sc", align_bytes=64)
+        wd_sc = sb.tile([P, K_PASS], U8, name="wd_sc", align_bytes=64)
         nc.vector.tensor_copy(
-            wd_sc[:].rearrange("p (o t m) -> p o t m", o=PASSES, t=LANES),
-            wd_sc_raw[:].rearrange("p (o m t) -> p o t m", o=PASSES, t=LANES),
+            wd_sc[:].rearrange("p (t m) -> p t m", t=LANES),
+            wd_sc_raw[:].rearrange("p (m t) -> p t m", t=LANES),
         )
 
         xg = {}
@@ -158,19 +161,19 @@ def tile_attend_gml_lch_kernel(tc, xT, wd_words, wd_scales, wv_words, wv_scales,
                 )
 
         weight = {}
+        cw_copy = sb.tile([P, PASSES, LANES], F32, name="cw_copy")
+        nc.scalar.activation(cw_copy[:], cw_sb[:, :, 0:LANES], ACT.Copy)
 
-        def make_weight(h):
-            rows = rw_sb[:, h * HALF_N : (h + 1) * HALF_N]
-            for o in range(PASSES):
-                if (h, o) == (1, PASSES - 1):
-                    weight[h, o] = reuse.tile([P, LANES, HALF_N], F32, name=f"weight{h}{o}", offset=AT_LAST_WEIGHT, align_bytes=64)
+        def make_weight(o):
+            if o == PASSES - 1:
+                weight[o] = reuse.tile([P, LANES, N], F32, name=f"weight{o}", offset=AT_LAST_WEIGHT, align_bytes=64)
+            else:
+                weight[o] = sb.tile([P, LANES, N], F32, name=f"weight{o}")
+            for t in range(LANES):
+                if o * LANES + t < VECTOR_PLANES:
+                    nc.vector.tensor_scalar(weight[o][:, t, :], rw_sb[:], cw_sb[:, o, t : t + 1], None, ALU.mult)
                 else:
-                    weight[h, o] = sb.tile([P, LANES, HALF_N], F32, name=f"weight{h}{o}")
-                for t in range(LANES):
-                    if h == 0:
-                        nc.vector.tensor_scalar(weight[h, o][:, t, :], rows, cw_sb[:, o, t : t + 1], None, ALU.mult)
-                    else:
-                        nc.scalar.activation(weight[h, o][:, t, :], rows, ACT.Copy, scale=cw_sb[:, o, t : t + 1])
+                    nc.scalar.activation(weight[o][:, t, :], rw_sb[:], ACT.Copy, scale=cw_copy[:, o, t : t + 1])
 
         def scores(o, lo, bank):
             a = ps.tile([P, LANES, CHUNK], F32, name="a", tag=bank)
@@ -179,7 +182,7 @@ def tile_attend_gml_lch_kernel(tc, xT, wd_words, wd_scales, wv_words, wv_scales,
             for t in range(LANES):
                 nc.tensor.matmul_mx(
                     out=a[:, t, :], lhsT=wd_sb[o][:, t * P : (t + 1) * P].bitcast(E4M3),
-                    lhsT_scale=wd_sc[:, o * K_PASS + t * P : o * K_PASS + (t + 1) * P],
+                    lhsT_scale=wd_sc[SCALE_ROWS * o : P, t * P : (t + 1) * P],
                     rhs=x_codes[h][:, pos].bitcast(E4M3), rhs_scale=x_sc[h][:, pos], start=True, stop=True,
                 )
             return a
@@ -225,7 +228,7 @@ def tile_attend_gml_lch_kernel(tc, xT, wd_words, wd_scales, wv_words, wv_scales,
             nc.vector.tensor_tensor(
                 g[h, o][:, LANES * start : LANES * end].rearrange("p (b i t) -> p b t i", t=LANES, i=PAIR),
                 slope[:].rearrange("p t (b i) -> p b t i", i=PAIR),
-                weight[h, o][:, :, start:end].rearrange("p t (b i) -> p b t i", i=PAIR),
+                weight[o][:, :, lo:hi].rearrange("p t (b i) -> p b t i", i=PAIR),
                 ALU.mult,
             )
 
@@ -251,13 +254,14 @@ def tile_attend_gml_lch_kernel(tc, xT, wd_words, wd_scales, wv_words, wv_scales,
         def scatter(dx, k, lo, hi):
             nc.vector.tensor_copy(windows[k][:].indirect(offsets[:, lo // BAND : hi // BAND]), dx[:])
 
-        cast(True, 0, 0, 0, VECTOR_CAST_FIRST)
-        cast(False, 0, 0, VECTOR_CAST_FIRST, T)
+        cast(False, 0, 0, 0, HALF_T)
+        cast(True, 0, HALF_T, 0, HALF_T)
         gather_first_half(0)
         gather_second_half(0, "picked0")
-        cast(False, 1, 0, 0, HALF_T)
-        cast(True, 1, HALF_T, 0, VECTOR_CAST_LAST)
-        cast(False, 1, HALF_T, VECTOR_CAST_LAST, HALF_T)
+        cast(False, 1, 0, VECTOR_CAST_THIRD, X_SPLIT)
+        cast(True, 1, 0, 0, VECTOR_CAST_THIRD)
+        cast(True, 1, X_SPLIT, 0, VECTOR_CAST_LAST)
+        cast(False, 1, X_SPLIT, VECTOR_CAST_LAST, T - X_SPLIT)
         gather_first_half(1)
         deal_wd(0, "wd_sb0")
         quantize_x(0, "x_codes0", CHUNK)
@@ -265,8 +269,8 @@ def tile_attend_gml_lch_kernel(tc, xT, wd_words, wd_scales, wv_words, wv_scales,
         for h in range(2):
             for o in range(PASSES):
                 g[h, o] = sb.tile([P, HALF_N * LANES], BF16, name=f"g{h}{o}", align_bytes=64)
-        for h in range(2):
-            make_weight(h)
+        for o in range(PASSES):
+            make_weight(o)
         gather_second_half(1, "xg1")
 
         first_half = [slope_direct(0, 0, ("b0", "b1"))]

@@ -21,6 +21,7 @@ P = 128
 LANES = 4
 K_PASS = P * LANES
 PASSES = V // K_PASS
+QUADRANT = 32
 SCALE_ROWS = 4
 BAND = 16
 RUN = 4
@@ -32,17 +33,17 @@ CHUNK = 128
 LAST_CHUNK = N - CHUNK
 EARLY_TILES = 2
 
-X_SPLIT = 512
-X_LOADS = ((0, 0, HALF_T), (0, HALF_T, T), (1, 0, X_SPLIT), (1, X_SPLIT, T))
-VECTOR_PLANES = 6
+FIRST_PAIR_SPLIT = 576
+X_LOADS = ((0, 0, FIRST_PAIR_SPLIT), (0, FIRST_PAIR_SPLIT, T), (1, 0, HALF_T), (1, HALF_T, T))
 VECTOR_CAST_THIRD = 128
 VECTOR_CAST_LAST = 384
+VECTOR_PLANES = 6
 
 WINDOW_BYTES = 4 * T
 AT_LAST_WEIGHT = 0
-AT_LATE_WINDOWS = 2 * WINDOW_BYTES
-AT_LATE_X = 3 * WINDOW_BYTES - 1024
-AT_LAST_X_LOAD = 2 * WINDOW_BYTES
+AT_LATE_WINDOWS = 4 * LANES * N
+AT_LATE_X = AT_LATE_WINDOWS + WINDOW_BYTES - LANES * HALF_N
+AT_LAST_X_LOAD = AT_LATE_WINDOWS
 
 
 def tile_attend_gml_lch_kernel(tc, xT, wd_words, wd_scales, wv_words, wv_scales, y, cw, rw, offs, out):
@@ -64,8 +65,8 @@ def tile_attend_gml_lch_kernel(tc, xT, wd_words, wd_scales, wv_words, wv_scales,
         cw_sb = sb.tile([P, PASSES, 8], F32, name="cw_sb")
         nc.sync.dma_start(cw_sb[:, :, 0:LANES], cw.rearrange("(o p t) e -> p o (t e)", p=P, t=LANES))
         wd_sc_rows = wd_scales[0].bitcast(I32).rearrange("(q r) (o c) -> q o r c", r=SCALE_ROWS, o=PASSES)
-        for q in range(P // 32):
-            nc.sync.dma_start(wd_sc_raw[32 * q : 32 * q + PASSES * SCALE_ROWS, :].bitcast(I32), wd_sc_rows[q])
+        for q in range(P // QUADRANT):
+            nc.sync.dma_start(wd_sc_raw[QUADRANT * q : QUADRANT * q + PASSES * SCALE_ROWS, :].bitcast(I32), wd_sc_rows[q])
 
         x_rows = xT.rearrange("(p t) n -> p t n", t=LANES)
         x_raw = {}
@@ -91,7 +92,7 @@ def tile_attend_gml_lch_kernel(tc, xT, wd_words, wd_scales, wv_words, wv_scales,
                 y_sb[o, h] = sb.tile([P, LANES, HALF_N], F32, name=f"y_sb{o}{h}", tag=f"y_sb{o}{h}", align_bytes=64)
                 nc.sync.dma_start(y_sb[o, h][:], y_rows[o][:, :, h * HALF_N : (h + 1) * HALF_N])
         for r in range(SCALE_ROWS):
-            nc.sync.dma_start(wv_sc[r:P:32, :, :].bitcast(I32), wv_sc_rows[r].bitcast(I32))
+            nc.sync.dma_start(wv_sc[r:P:QUADRANT, :, :].bitcast(I32), wv_sc_rows[r].bitcast(I32))
         nc.sync.dma_start(wv_sb[:], wv_words.rearrange("o p d t -> p o (d t)").bitcast(I32))
 
         g_codes = [sb.tile([P, HALF_N + N], I32, name=f"g_codes{o}", align_bytes=64) for o in range(PASSES)]
@@ -105,7 +106,7 @@ def tile_attend_gml_lch_kernel(tc, xT, wd_words, wd_scales, wv_words, wv_scales,
         windows = []
         for k in range(EARLY_TILES):
             windows.append(sb.tile([P, T], F32, name=f"window{k}"))
-            (nc.vector if k == 0 else nc.gpsimd).memset(windows[k][:].bitcast(I32), 0)
+            nc.vector.memset(windows[k][:].bitcast(I32), 0)
 
         wd_sc = sb.tile([P, K_PASS], U8, name="wd_sc", align_bytes=64)
         nc.vector.tensor_copy(
@@ -254,14 +255,14 @@ def tile_attend_gml_lch_kernel(tc, xT, wd_words, wd_scales, wv_words, wv_scales,
         def scatter(dx, k, lo, hi):
             nc.vector.tensor_copy(windows[k][:].indirect(offsets[:, lo // BAND : hi // BAND]), dx[:])
 
-        cast(False, 0, 0, 0, HALF_T)
-        cast(True, 0, HALF_T, 0, HALF_T)
+        cast(False, 0, 0, 0, FIRST_PAIR_SPLIT)
+        cast(True, 0, FIRST_PAIR_SPLIT, 0, T - FIRST_PAIR_SPLIT)
         gather_first_half(0)
         gather_second_half(0, "picked0")
-        cast(False, 1, 0, VECTOR_CAST_THIRD, X_SPLIT)
+        cast(False, 1, 0, VECTOR_CAST_THIRD, HALF_T)
         cast(True, 1, 0, 0, VECTOR_CAST_THIRD)
-        cast(True, 1, X_SPLIT, 0, VECTOR_CAST_LAST)
-        cast(False, 1, X_SPLIT, VECTOR_CAST_LAST, T - X_SPLIT)
+        cast(True, 1, HALF_T, 0, VECTOR_CAST_LAST)
+        cast(False, 1, HALF_T, VECTOR_CAST_LAST, HALF_T)
         gather_first_half(1)
         deal_wd(0, "wd_sb0")
         quantize_x(0, "x_codes0", CHUNK)

@@ -296,10 +296,10 @@ def tile_attend_gml_lch_kernel(tc, xT, wd_words, wd_scales, wv_words, wv_scales,
             weigh(last_chunk[o], o, LAST_CHUNK, N)
         for o in range(PASSES):
             quantize_g(1, o)
-        early_dx = []
+        held_dx = reuse.tile([P, HALF_N], F32, name="held_dx", offset=AT_LAST_WEIGHT, align_bytes=64)
+        early_dx = [sb.tile([P, HALF_N], F32, name="free_dx"), held_dx]
         for k in range(EARLY_TILES):
-            dx = reuse.tile([P, HALF_N], F32, name=f"early_dx{k}", offset=AT_LAST_WEIGHT + k * HALF_N * 4, align_bytes=64)
-            early_dx.append(unload(dx, early_ps[k], HALF_N))
+            unload(early_dx[k], early_ps[k], HALF_N)
         whole_ps = [project(k, bank, HALF_N) for k, bank in enumerate(("b0", "b1", "b4", "b5"))]
 
         for k in range(EARLY_TILES):

@@ -1,7 +1,6 @@
 from contextlib import ExitStack
 
 import concourse.mybir as mybir
-from concourse.masks import make_identity
 
 N, T, D, V = 512, 1024, 512, 1024
 FLOPS = 2 * 2 * N * D * V
@@ -28,10 +27,7 @@ RUN = 4
 PAIR = 2
 HALF_T = T // 2
 HALF_N = N // 2
-D_TILES = D // P
 CHUNK = 128
-LAST_CHUNK = N - CHUNK
-EARLY_TILES = 2
 
 FIRST_PAIR_SPLIT = 576
 X_LOADS = ((0, 0, FIRST_PAIR_SPLIT), (0, FIRST_PAIR_SPLIT, T), (1, 0, HALF_T), (1, HALF_T, T))
@@ -40,10 +36,7 @@ VECTOR_CAST_LAST = 384
 VECTOR_PLANES = 6
 
 WINDOW_BYTES = 4 * T
-AT_LAST_WEIGHT = 0
-AT_LATE_WINDOWS = 4 * LANES * N
-AT_LATE_X = AT_LATE_WINDOWS + WINDOW_BYTES - LANES * HALF_N
-AT_LAST_X_LOAD = AT_LATE_WINDOWS
+AT_LATE_X = WINDOW_BYTES - LANES * HALF_N
 
 
 def tile_attend_gml_lch_kernel(tc, xT, wd_words, wd_scales, wv_words, wv_scales, y, cw, rw, offs, out):
@@ -54,7 +47,6 @@ def tile_attend_gml_lch_kernel(tc, xT, wd_words, wd_scales, wv_words, wv_scales,
         ps = ctx.enter_context(tc.psum_pool(name="ps", bufs=1))
 
         offsets = sb.tile([P, N // BAND], U16, name="offsets")
-
         wd_sc_raw = sb.tile([P, K_PASS], U8, name="wd_sc_raw", align_bytes=64)
         wv_sc = sb.tile([P, PASSES, D], U8, name="wv_sc", align_bytes=64)
         nc.gpsimd.memset(wd_sc_raw[:].bitcast(I32), 0)
@@ -71,40 +63,33 @@ def tile_attend_gml_lch_kernel(tc, xT, wd_words, wd_scales, wv_words, wv_scales,
         x_rows = xT.rearrange("(p t) n -> p t n", t=LANES)
         x_raw = {}
         for u, lo, hi in X_LOADS:
-            if (u, lo, hi) == X_LOADS[-1]:
-                x_raw[u, lo] = reuse.tile([P, 2, hi - lo], F32, name=f"x_raw{u}_{lo}", offset=AT_LAST_X_LOAD, align_bytes=64)
-            else:
-                x_raw[u, lo] = sb.tile([P, 2, hi - lo], F32, name=f"x_raw{u}_{lo}")
+            x_raw[u, lo] = sb.tile([P, 2, hi - lo], F32, name=f"x_raw{u}_{lo}")
             nc.sync.dma_start(x_raw[u, lo][:], x_rows[:, 2 * u : 2 * u + 2, lo:hi])
             if (u, lo, hi) == X_LOADS[1]:
                 nc.sync.dma_start(offsets[:], offs)
 
         wd_hbm = wd_words[0].rearrange("p v t -> p (v t)").bitcast(I32)
         wd_raw = [sb.tile([P, K_PASS], I32, name=f"wd_raw{o}") for o in range(PASSES)]
-        wv_sc_rows = wv_scales.rearrange("o (q r) d -> r q o d", r=SCALE_ROWS)
-        y_rows = y.rearrange("(o p t) i -> o p t i", p=P, t=LANES)
-        y_sb = {}
-        wv_sb = sb.tile([P, PASSES, D], I32, name="wv_sb", align_bytes=64)
         for o in range(PASSES):
             nc.sync.dma_start(wd_raw[o][:], wd_hbm[:, o * K_PASS : (o + 1) * K_PASS])
-        for h in range(2):
+        y_rows = y.rearrange("(o p t) i -> o p t i", p=P, t=LANES)
+        y_sb = {}
+
+        def load_targets(h):
             for o in range(PASSES):
                 y_sb[o, h] = sb.tile([P, LANES, HALF_N], F32, name=f"y_sb{o}{h}", tag=f"y_sb{o}{h}", align_bytes=64)
                 nc.sync.dma_start(y_sb[o, h][:], y_rows[o][:, :, h * HALF_N : (h + 1) * HALF_N])
+
+        load_targets(0)
+        wv_sc_rows = wv_scales.rearrange("o (q r) d -> r q o d", r=SCALE_ROWS)
         for r in range(SCALE_ROWS):
             nc.sync.dma_start(wv_sc[r:P:QUADRANT, :, :].bitcast(I32), wv_sc_rows[r].bitcast(I32))
+        wv_sb = sb.tile([P, PASSES, D], I32, name="wv_sb", align_bytes=64)
         nc.sync.dma_start(wv_sb[:], wv_words.rearrange("o p d t -> p o (d t)").bitcast(I32))
-
-        g_codes = [sb.tile([P, HALF_N + N], I32, name=f"g_codes{o}", align_bytes=64) for o in range(PASSES)]
-        g_sc = [sb.tile([P, HALF_N + N], U8, name=f"g_sc{o}", align_bytes=64) for o in range(PASSES)]
-        for o in range(PASSES):
-            nc.vector.memset(g_codes[o][:, 0:HALF_N], 0)
-            nc.vector.memset(g_sc[o][:, 0:HALF_N].bitcast(I32), 0)
-        ident = sb.tile([P, P], F32, name="ident")
-        make_identity(nc, ident[:])
+        load_targets(1)
 
         windows = []
-        for k in range(EARLY_TILES):
+        for k in range(2):
             windows.append(sb.tile([P, T], F32, name=f"window{k}"))
             nc.vector.memset(windows[k][:].bitcast(I32), 0)
 
@@ -114,11 +99,21 @@ def tile_attend_gml_lch_kernel(tc, xT, wd_words, wd_scales, wv_words, wv_scales,
             wd_sc_raw[:].rearrange("p (m t) -> p t m", t=LANES),
         )
 
-        xg = {}
-        for lo, tag in ((0, "xg0"), (CHUNK, "xg1")):
-            xg[lo] = sb.tile([P, CHUNK * LANES], BF16, name=tag, tag=tag, align_bytes=64)
-        xg[HALF_N] = reuse.tile([P, HALF_N * LANES], BF16, name="xg_late", offset=AT_LATE_X, align_bytes=64)
-        xg_words = {lo: xg[lo][:].bitcast(U32).rearrange("p (i u) -> p i u", u=2) for lo in xg}
+        cw_copy = sb.tile([P, PASSES, LANES], F32, name="cw_copy")
+        nc.scalar.activation(cw_copy[:], cw_sb[:, :, 0:LANES], ACT.Copy)
+        weight = []
+        for o in range(PASSES):
+            weight.append(sb.tile([P, LANES, N], F32, name=f"weight{o}", tag=f"weight{o}"))
+            for t in range(LANES):
+                if o * LANES + t < VECTOR_PLANES:
+                    nc.vector.tensor_scalar(weight[o][:, t, :], rw_sb[:], cw_sb[:, o, t : t + 1], None, ALU.mult)
+                else:
+                    nc.scalar.activation(weight[o][:, t, :], rw_sb[:], ACT.Copy, scale=cw_copy[:, o, t : t + 1])
+
+        xg = [
+            sb.tile([P, HALF_N * LANES], BF16, name="xg0", align_bytes=64),
+            reuse.tile([P, HALF_N * LANES], BF16, name="xg1", offset=AT_LATE_X, align_bytes=64),
+        ]
         pairs = [sb.tile([P, 2 * T], BF16, name=f"pairs{u}") for u in range(2)]
 
         def cast(on_vector, u, base, lo, hi):
@@ -129,182 +124,162 @@ def tile_attend_gml_lch_kernel(tc, xT, wd_words, wd_scales, wv_words, wv_scales,
             else:
                 nc.scalar.activation(dst, src, ACT.Copy)
 
-        def gather(dst, u, lo, hi):
-            nc.vector.tensor_copy(dst, pairs[u][:].bitcast(U32).indirect(offsets[:, lo // BAND : hi // BAND]))
+        def entries(lo, hi):
+            return offsets[:, lo // BAND : hi // BAND]
 
-        def gather_first_half(u):
-            for lo in range(0, HALF_N, CHUNK):
-                gather(xg_words[lo][:, :, u], u, lo, lo + CHUNK)
+        def gather(u):
+            for h in range(2):
+                dst = xg[h][:].bitcast(U32).rearrange("p (i u) -> p i u", u=2)[:, :, u]
+                nc.vector.tensor_copy(dst, pairs[u][:].bitcast(U32).indirect(entries(h * HALF_N, (h + 1) * HALF_N)))
 
-        def gather_second_half(u, tag):
-            picked = sb.tile([P, HALF_N], U32, name=f"picked{u}", tag=tag, align_bytes=64)
-            gather(picked[:], u, HALF_N, N)
-            nc.scalar.copy(xg_words[HALF_N][:, :, u], picked[:])
+        cast(False, 0, 0, 0, FIRST_PAIR_SPLIT)
+        cast(True, 0, FIRST_PAIR_SPLIT, 0, T - FIRST_PAIR_SPLIT)
+        gather(0)
+        cast(False, 1, 0, VECTOR_CAST_THIRD, HALF_T)
+        cast(True, 1, 0, 0, VECTOR_CAST_THIRD)
+        cast(True, 1, HALF_T, 0, VECTOR_CAST_LAST)
+        cast(False, 1, HALF_T, VECTOR_CAST_LAST, HALF_T)
+        gather(1)
 
-        wd_sb = {}
-
-        def deal_wd(o, tag):
-            wd_sb[o] = sb.tile([P, K_PASS], I32, name=f"wd_sb{o}", tag=tag, align_bytes=64)
-            nc.vector.tensor_copy(
+        wd_sb = []
+        for o in range(PASSES):
+            wd_sb.append(sb.tile([P, K_PASS], U32, name=f"wd_sb{o}", align_bytes=64))
+            nc.scalar.copy(
                 wd_sb[o][:].rearrange("p (t c i) -> p c t i", t=LANES, i=RUN),
-                wd_raw[o][:].rearrange("p (c i t) -> p c t i", t=LANES, i=RUN),
+                wd_raw[o][:].bitcast(U32).rearrange("p (c i t) -> p c t i", t=LANES, i=RUN),
             )
 
-        x_codes, x_sc = {}, {}
+        x_codes, x_sc = [], []
+        for h in range(2):
+            x_codes.append(sb.tile([P, HALF_N], U32, name=f"x_codes{h}", align_bytes=64))
+            x_sc.append(sb.tile([P, HALF_N], U8, name=f"x_sc{h}", align_bytes=64))
+            nc.vector.quantize_mx(out=x_codes[h][:].bitcast(E4M3), scales=x_sc[h][:], in_=xg[h][:])
+        for e in range(2):
+            windows.append(reuse.tile([P, T], F32, name=f"late_window{e}", offset=e * WINDOW_BYTES, align_bytes=64))
+            nc.gpsimd.memset(windows[-1][:].bitcast(I32), 0)
 
-        def quantize_x(h, tag, width):
-            x_codes[h] = sb.tile([P, HALF_N], U32, name=f"x_codes{h}", tag=tag, align_bytes=64)
-            x_sc[h] = sb.tile([P, HALF_N], U8, name=f"x_sc{h}", align_bytes=64)
-            for lo in range(0, HALF_N, width):
-                nc.vector.quantize_mx(
-                    out=x_codes[h][:, lo : lo + width].bitcast(E4M3), scales=x_sc[h][:, lo : lo + width],
-                    in_=xg[h * HALF_N + lo][:],
-                )
-
-        weight = {}
-        cw_copy = sb.tile([P, PASSES, LANES], F32, name="cw_copy")
-        nc.scalar.activation(cw_copy[:], cw_sb[:, :, 0:LANES], ACT.Copy)
-
-        def make_weight(o):
-            if o == PASSES - 1:
-                weight[o] = reuse.tile([P, LANES, N], F32, name=f"weight{o}", offset=AT_LAST_WEIGHT, align_bytes=64)
-            else:
-                weight[o] = sb.tile([P, LANES, N], F32, name=f"weight{o}")
-            for t in range(LANES):
-                if o * LANES + t < VECTOR_PLANES:
-                    nc.vector.tensor_scalar(weight[o][:, t, :], rw_sb[:], cw_sb[:, o, t : t + 1], None, ALU.mult)
-                else:
-                    nc.scalar.activation(weight[o][:, t, :], rw_sb[:], ACT.Copy, scale=cw_copy[:, o, t : t + 1])
-
-        def scores(o, lo, bank):
-            a = ps.tile([P, LANES, CHUNK], F32, name="a", tag=bank)
-            h, start = divmod(lo, HALF_N)
+        def slope_into(dst, c, o):
+            h, start = divmod(c * CHUNK, HALF_N)
             pos = slice(start, start + CHUNK)
+            a = ps.tile([P, LANES, CHUNK], F32, name="a", tag=f"b{2 * c + o}")
             for t in range(LANES):
                 nc.tensor.matmul_mx(
                     out=a[:, t, :], lhsT=wd_sb[o][:, t * P : (t + 1) * P].bitcast(E4M3),
                     lhsT_scale=wd_sc[SCALE_ROWS * o : P, t * P : (t + 1) * P],
                     rhs=x_codes[h][:, pos].bitcast(E4M3), rhs_scale=x_sc[h][:, pos], start=True, stop=True,
                 )
-            return a
+            diff = sb.tile([P, LANES, CHUNK], F32, name=f"diff{c}{o}", tag=f"diff{c}{o}")
+            nc.vector.tensor_tensor(diff[:], a[:], y_sb[o, h][:, :, pos], ALU.subtract)
+            nc.scalar.activation(dst, diff[:], ACT.Tanh)
 
-        def targets(o, lo):
-            h, start = divmod(lo, HALF_N)
-            return y_sb[o, h][:, :, start : start + CHUNK]
-
-        def slope_direct(o, lo, banks):
-            slope = sb.tile([P, LANES, len(banks) * CHUNK], F32, name=f"slope{o}_{lo}")
-            for c, bank in enumerate(banks):
-                chunk_lo = lo + c * CHUNK
-                a = scores(o, chunk_lo, bank)
-                diff = sb.tile([P, LANES, CHUNK], F32, name=f"diff{o}_{chunk_lo}")
-                nc.vector.tensor_tensor(diff[:], a[:], targets(o, chunk_lo), ALU.subtract)
-                nc.scalar.activation(slope[:, :, c * CHUNK : (c + 1) * CHUNK], diff[:], ACT.Tanh)
-            return slope
-
-        def negated_scores(o, bank):
-            a = scores(o, LAST_CHUNK, bank)
-            minus_a = sb.tile([P, LANES, CHUNK], F32, name=f"minus_a{o}")
-            nc.scalar.activation(minus_a[:], a[:], ACT.Copy, scale=-1.0)
-            return minus_a
-
-        def slope_turned(minus_a, o, bank_sum, bank_back):
-            y_minus_a = ps.tile([P, LANES, P], F32, name="y_minus_a", tag=bank_sum)
-            for t in range(LANES):
-                nc.tensor.matmul(y_minus_a[:, t, :], targets(o, LAST_CHUNK)[:, t, :], ident[:], start=(t == 0), stop=False, is_transpose=True)
-            for t in range(LANES):
-                nc.tensor.matmul(y_minus_a[:, t, :], minus_a[:, t, :], ident[:], start=False, stop=(t == LANES - 1), is_transpose=True)
-            slope_t = sb.tile([P, LANES, P], F32, name=f"slope_t{o}")
-            nc.scalar.activation(slope_t[:], y_minus_a[:], ACT.Tanh, scale=-1.0)
-            slope = ps.tile([P, LANES, CHUNK], F32, name="slope_ps", tag=bank_back)
-            for t in range(LANES):
-                nc.tensor.transpose(slope[:, t, :], slope_t[:, t, :], ident[:])
-            return slope
-
-        g = {}
-
-        def weigh(slope, o, lo, hi):
-            h, start = divmod(lo, HALF_N)
-            end = start + hi - lo
+        def weigh(dst, slope, o, lo, hi):
             nc.vector.tensor_tensor(
-                g[h, o][:, LANES * start : LANES * end].rearrange("p (b i t) -> p b t i", t=LANES, i=PAIR),
-                slope[:].rearrange("p t (b i) -> p b t i", i=PAIR),
+                dst.rearrange("p (b i t) -> p b t i", t=LANES, i=PAIR),
+                slope.rearrange("p t (b i) -> p b t i", i=PAIR),
                 weight[o][:, :, lo:hi].rearrange("p t (b i) -> p b t i", i=PAIR),
                 ALU.mult,
             )
 
-        def quantize_g(h, o):
-            pos = slice((h + 1) * HALF_N, (h + 2) * HALF_N)
-            nc.vector.quantize_mx(out=g_codes[o][:, pos].bitcast(E5M2), scales=g_sc[o][:, pos], in_=g[h, o][:])
+        def quantize_g(name, g, tag):
+            width = g.shape[1] // LANES
+            codes = sb.tile([P, width], U32, name=f"{name}_codes", tag=tag, align_bytes=64)
+            scales = sb.tile([P, width], U8, name=f"{name}_sc", align_bytes=64)
+            nc.vector.quantize_mx(out=codes[:].bitcast(E5M2), scales=scales[:], in_=g[:])
+            return codes, scales
 
-        def project(k, bank, g_col):
-            dx_ps = ps.tile([P, N], F32, name="dx_ps", tag=bank)
+        def project(dst, k, o, codes, scales):
             cols = slice(k * P, (k + 1) * P)
-            for o in range(PASSES):
-                nc.tensor.matmul_mx(
-                    out=dx_ps[:], lhsT=wv_sb[:, o, cols].bitcast(E4M3), lhsT_scale=wv_sc[:, o, cols],
-                    rhs=g_codes[o][:, g_col : g_col + N].bitcast(E5M2), rhs_scale=g_sc[o][:, g_col : g_col + N],
-                    start=(o == 0), stop=(o == PASSES - 1),
-                )
-            return dx_ps
+            nc.tensor.matmul_mx(
+                out=dst, lhsT=wv_sb[:, o, cols].bitcast(E4M3), lhsT_scale=wv_sc[:, o, cols],
+                rhs=codes.bitcast(E5M2), rhs_scale=scales, start=(o == 0), stop=(o == PASSES - 1),
+            )
 
-        def unload(dx, dx_ps, lo):
-            nc.scalar.activation(dx[:], dx_ps[:, lo:N], ACT.Copy)
+        def project_chunk(dst, k, quantized):
+            codes, scales = quantized
+            for o in range(PASSES):
+                project(dst, k, o, codes[:, o * CHUNK : (o + 1) * CHUNK], scales[:, o * CHUNK : (o + 1) * CHUNK])
+
+        def unload(on_vector, src, name, tag):
+            dx = sb.tile([P, src.shape[1]], F32, name=name, tag=tag)
+            if on_vector:
+                nc.vector.tensor_copy(dx[:], src)
+            else:
+                nc.scalar.activation(dx[:], src, ACT.Copy)
             return dx
 
-        def scatter(dx, k, lo, hi):
-            nc.vector.tensor_copy(windows[k][:].indirect(offsets[:, lo // BAND : hi // BAND]), dx[:])
+        def scatter(on_vector, src, k, lo, hi):
+            dst = windows[k][:].indirect(entries(lo, hi))
+            if on_vector:
+                nc.vector.tensor_copy(dst, src)
+            else:
+                nc.scalar.activation(dst, src, ACT.Copy)
 
-        cast(False, 0, 0, 0, FIRST_PAIR_SPLIT)
-        cast(True, 0, FIRST_PAIR_SPLIT, 0, T - FIRST_PAIR_SPLIT)
-        gather_first_half(0)
-        gather_second_half(0, "picked0")
-        cast(False, 1, 0, VECTOR_CAST_THIRD, HALF_T)
-        cast(True, 1, 0, 0, VECTOR_CAST_THIRD)
-        cast(True, 1, HALF_T, 0, VECTOR_CAST_LAST)
-        cast(False, 1, HALF_T, VECTOR_CAST_LAST, HALF_T)
-        gather_first_half(1)
-        deal_wd(0, "wd_sb0")
-        quantize_x(0, "x_codes0", CHUNK)
-        deal_wd(1, "xg0")
-        for h in range(2):
-            for o in range(PASSES):
-                g[h, o] = sb.tile([P, HALF_N * LANES], BF16, name=f"g{h}{o}", align_bytes=64)
-        for o in range(PASSES):
-            make_weight(o)
-        gather_second_half(1, "xg1")
-
-        first_half = [slope_direct(0, 0, ("b0", "b1"))]
-        quantize_x(1, "y_sb00", HALF_N)
-        for e in range(D_TILES - EARLY_TILES):
-            windows.append(reuse.tile([P, T], F32, name=f"late_window{e}", offset=AT_LATE_WINDOWS + e * WINDOW_BYTES, align_bytes=64))
-            nc.gpsimd.memset(windows[-1][:].bitcast(I32), 0)
-        first_half.append(slope_direct(1, 0, ("b2", "b3")))
-        negated = [negated_scores(o, f"b{6 + o}") for o in range(PASSES)]
-        third_chunk = []
-        for o in range(PASSES):
-            weigh(first_half[o], o, 0, HALF_N)
-            third_chunk.append(slope_direct(o, HALF_N, (f"b{o}",)))
-        last_chunk = [slope_turned(negated[o], o, f"b{4 + o}", f"b{2 + o}") for o in range(PASSES)]
-        for o in range(PASSES):
-            quantize_g(0, o)
-        early_ps = [project(k, f"b{6 + k}", 0) for k in range(EARLY_TILES)]
-
-        for o in range(PASSES):
-            weigh(third_chunk[o], o, HALF_N, LAST_CHUNK)
-        for o in range(PASSES):
-            weigh(last_chunk[o], o, LAST_CHUNK, N)
-        for o in range(PASSES):
-            quantize_g(1, o)
-        held_dx = reuse.tile([P, HALF_N], F32, name="held_dx", offset=AT_LAST_WEIGHT, align_bytes=64)
-        early_dx = [sb.tile([P, HALF_N], F32, name="free_dx"), held_dx]
-        for k in range(EARLY_TILES):
-            unload(early_dx[k], early_ps[k], HALF_N)
-        whole_ps = [project(k, bank, HALF_N) for k, bank in enumerate(("b0", "b1", "b4", "b5"))]
-
-        for k in range(EARLY_TILES):
-            scatter(early_dx[k], k, 0, HALF_N)
-        for k in range(D_TILES):
-            lo = HALF_N if k < EARLY_TILES else 0
-            scatter(unload(sb.tile([P, N - lo], F32, name=f"whole_dx{k}"), whole_ps[k], lo), k, lo, N)
+        def store(k):
             nc.sync.dma_start(out[k * P : (k + 1) * P, :], windows[k][:])
+
+        early = {(c, o): sb.tile([P, LANES, CHUNK], F32, name=f"slope{c}{o}") for c in range(2) for o in range(PASSES)}
+        late = [sb.tile([P, LANES, HALF_N], F32, name=f"late_slope{o}") for o in range(PASSES)]
+        for o in range(PASSES):
+            for c in range(2):
+                slope_into(early[c, o][:], c, o)
+
+        def weigh_chunk(c, tag):
+            g = sb.tile([P, PASSES * CHUNK * LANES], BF16, name=f"g{c}", tag=tag, align_bytes=64)
+            for o in range(PASSES):
+                weigh(g[:, o * K_PASS : (o + 1) * K_PASS], early[c, o][:], o, c * CHUNK, (c + 1) * CHUNK)
+            return g
+
+        g0 = weigh_chunk(0, "g0")
+        for c in range(2):
+            slope_into(late[0][:, :, c * CHUNK : (c + 1) * CHUNK], 2 + c, 0)
+        q0 = quantize_g("first", g0, "y_sb01")
+        for c in range(2):
+            slope_into(late[1][:, :, c * CHUNK : (c + 1) * CHUNK], 2 + c, 1)
+        first_ps = ps.tile([P, N], F32, name="first_ps", tag="b0")
+        for k in range(4):
+            project_chunk(first_ps[:, k * CHUNK : (k + 1) * CHUNK], k, q0)
+        first_dx = unload(False, first_ps[:, 0 : 3 * CHUNK], "first_dx", "diff31")
+        for k in range(3):
+            scatter(False, first_dx[:, k * CHUNK : (k + 1) * CHUNK], k, 0, CHUNK)
+
+        g1 = weigh_chunk(1, "y_sb11")
+        late_g = [sb.tile([P, HALF_N * LANES], BF16, name=f"late_g{o}", align_bytes=64) for o in range(PASSES)]
+        weigh(late_g[0][:], late[0][:], 0, HALF_N, N)
+        q1 = quantize_g("second", g1, "second_codes")
+        second_ps = ps.tile([P, HALF_N], F32, name="second_ps", tag="b2")
+        rest_ps = {1: ps.tile([P, 3 * CHUNK], F32, name="rest1_ps", tag="b1"), 3: ps.tile([P, 3 * CHUNK], F32, name="rest3_ps", tag="b3")}
+        project_chunk(second_ps[:, 0:CHUNK], 2, q1)
+        project_chunk(second_ps[:, CHUNK:HALF_N], 0, q1)
+        for k in (3, 1):
+            project_chunk(rest_ps[k][:, 0:CHUNK], k, q1)
+        second_dx = unload(False, second_ps[:], "second_dx", "second_dx")
+        scatter(False, second_dx[:, 0:CHUNK], 2, CHUNK, HALF_N)
+        scatter(False, second_dx[:, CHUNK:HALF_N], 0, CHUNK, HALF_N)
+
+        weigh(late_g[1][:], late[1][:], 1, HALF_N, N)
+        late_q = [quantize_g("late0", late_g[0], "late0_codes")]
+        held_dx = unload(True, first_ps[:, 3 * CHUNK : N], "held_dx", "weight1")
+        late_q.append(quantize_g("late1", late_g[1], "late1_codes"))
+        late_ps = {
+            2: ps.tile([P, HALF_N], F32, name="late2_ps", tag="b4")[:],
+            0: ps.tile([P, HALF_N], F32, name="late0_ps", tag="b6")[:],
+            3: rest_ps[3][:, CHUNK : 3 * CHUNK],
+            1: rest_ps[1][:, CHUNK : 3 * CHUNK],
+        }
+        for o in range(PASSES):
+            for k in late_ps:
+                project(late_ps[k], k, o, late_q[o][0][:], late_q[o][1][:])
+
+        scatter(True, held_dx[:], 3, 0, CHUNK)
+        dx2 = unload(True, late_ps[2], "dx2", "dx2")
+        dx3 = unload(True, rest_ps[3][:], "dx3", "dx3")
+        dx0 = unload(False, late_ps[0], "dx0", "dx0")
+        dx1 = unload(False, rest_ps[1][:], "dx1", "dx1")
+        scatter(True, dx2[:], 2, HALF_N, N)
+        store(2)
+        scatter(False, dx0[:], 0, HALF_N, N)
+        store(0)
+        scatter(True, dx3[:], 3, CHUNK, N)
+        store(3)
+        scatter(False, dx1[:], 1, CHUNK, N)
+        store(1)

@@ -23,7 +23,6 @@ PASSES = V // K_PASS
 QUADRANT = 32
 SCALE_ROWS = 4
 BAND = 16
-RUN = 4
 PAIR = 2
 HALF_T = T // 2
 HALF_N = N // 2
@@ -110,10 +109,8 @@ def tile_attend_gml_lch_kernel(tc, xT, wd_words, wd_scales, wv_words, wv_scales,
                 else:
                     nc.scalar.activation(weight[o][:, t, :], rw_sb[:], ACT.Copy, scale=cw_copy[:, o, t : t + 1])
 
-        xg = [
-            sb.tile([P, HALF_N * LANES], BF16, name="xg0", align_bytes=64),
-            reuse.tile([P, HALF_N * LANES], BF16, name="xg1", offset=AT_LATE_X, align_bytes=64),
-        ]
+        xg = {lo: sb.tile([P, CHUNK * LANES], BF16, name=f"xg{lo}", align_bytes=64) for lo in (0, CHUNK)}
+        xg[HALF_N] = reuse.tile([P, HALF_N * LANES], BF16, name="xg_late", offset=AT_LATE_X, align_bytes=64)
         pairs = [sb.tile([P, 2 * T], BF16, name=f"pairs{u}") for u in range(2)]
 
         def cast(on_vector, u, base, lo, hi):
@@ -127,33 +124,43 @@ def tile_attend_gml_lch_kernel(tc, xT, wd_words, wd_scales, wv_words, wv_scales,
         def entries(lo, hi):
             return offsets[:, lo // BAND : hi // BAND]
 
-        def gather(u):
-            for h in range(2):
-                dst = xg[h][:].bitcast(U32).rearrange("p (i u) -> p i u", u=2)[:, :, u]
-                nc.vector.tensor_copy(dst, pairs[u][:].bitcast(U32).indirect(entries(h * HALF_N, (h + 1) * HALF_N)))
+        def gather(u, lo, hi):
+            dst = xg[lo][:].bitcast(U32).rearrange("p (i u) -> p i u", u=2)[:, :, u]
+            nc.vector.tensor_copy(dst, pairs[u][:].bitcast(U32).indirect(entries(lo, hi)))
+
+        x_codes, x_sc = {}, {}
+
+        def quantize_x(lo, hi):
+            codes = sb.tile([P, hi - lo], U32, name=f"x_codes{lo}", align_bytes=64)
+            scales = sb.tile([P, hi - lo], U8, name=f"x_sc{lo}", align_bytes=64)
+            nc.vector.quantize_mx(out=codes[:].bitcast(E4M3), scales=scales[:], in_=xg[lo][:])
+            for start in range(0, hi - lo, CHUNK):
+                x_codes[(lo + start) // CHUNK] = codes[:, start : start + CHUNK]
+                x_sc[(lo + start) // CHUNK] = scales[:, start : start + CHUNK]
 
         cast(False, 0, 0, 0, FIRST_PAIR_SPLIT)
         cast(True, 0, FIRST_PAIR_SPLIT, 0, T - FIRST_PAIR_SPLIT)
-        gather(0)
+        for lo, hi in ((0, CHUNK), (CHUNK, HALF_N), (HALF_N, N)):
+            gather(0, lo, hi)
         cast(False, 1, 0, VECTOR_CAST_THIRD, HALF_T)
         cast(True, 1, 0, 0, VECTOR_CAST_THIRD)
         cast(True, 1, HALF_T, 0, VECTOR_CAST_LAST)
         cast(False, 1, HALF_T, VECTOR_CAST_LAST, HALF_T)
-        gather(1)
+        gather(1, 0, CHUNK)
+        gather(1, CHUNK, HALF_N)
+        quantize_x(0, CHUNK)
+        gather(1, HALF_N, N)
+        quantize_x(CHUNK, HALF_N)
+        quantize_x(HALF_N, N)
 
         wd_sb = []
         for o in range(PASSES):
             wd_sb.append(sb.tile([P, K_PASS], U32, name=f"wd_sb{o}", align_bytes=64))
             nc.scalar.copy(
-                wd_sb[o][:].rearrange("p (t c i) -> p c t i", t=LANES, i=RUN),
-                wd_raw[o][:].bitcast(U32).rearrange("p (c i t) -> p c t i", t=LANES, i=RUN),
+                wd_sb[o][:].rearrange("p (t m) -> p m t", t=LANES),
+                wd_raw[o][:].bitcast(U32).rearrange("p (m t) -> p m t", t=LANES),
             )
 
-        x_codes, x_sc = [], []
-        for h in range(2):
-            x_codes.append(sb.tile([P, HALF_N], U32, name=f"x_codes{h}", align_bytes=64))
-            x_sc.append(sb.tile([P, HALF_N], U8, name=f"x_sc{h}", align_bytes=64))
-            nc.vector.quantize_mx(out=x_codes[h][:].bitcast(E4M3), scales=x_sc[h][:], in_=xg[h][:])
         for e in range(2):
             windows.append(reuse.tile([P, T], F32, name=f"late_window{e}", offset=e * WINDOW_BYTES, align_bytes=64))
             nc.gpsimd.memset(windows[-1][:].bitcast(I32), 0)
@@ -166,7 +173,7 @@ def tile_attend_gml_lch_kernel(tc, xT, wd_words, wd_scales, wv_words, wv_scales,
                 nc.tensor.matmul_mx(
                     out=a[:, t, :], lhsT=wd_sb[o][:, t * P : (t + 1) * P].bitcast(E4M3),
                     lhsT_scale=wd_sc[SCALE_ROWS * o : P, t * P : (t + 1) * P],
-                    rhs=x_codes[h][:, pos].bitcast(E4M3), rhs_scale=x_sc[h][:, pos], start=True, stop=True,
+                    rhs=x_codes[c].bitcast(E4M3), rhs_scale=x_sc[c], start=True, stop=True,
                 )
             diff = sb.tile([P, LANES, CHUNK], F32, name=f"diff{c}{o}", tag=f"diff{c}{o}")
             nc.vector.tensor_tensor(diff[:], a[:], y_sb[o, h][:, :, pos], ALU.subtract)
@@ -215,7 +222,8 @@ def tile_attend_gml_lch_kernel(tc, xT, wd_words, wd_scales, wv_words, wv_scales,
                 nc.scalar.activation(dst, src, ACT.Copy)
 
         def store(k):
-            nc.sync.dma_start(out[k * P : (k + 1) * P, :], windows[k][:])
+            queue = nc.sync if k >= 2 else nc.scalar
+            queue.dma_start(out[k * P : (k + 1) * P, :], windows[k][:])
 
         early = {(c, o): sb.tile([P, LANES, CHUNK], F32, name=f"slope{c}{o}") for c in range(2) for o in range(PASSES)}
         late = [sb.tile([P, LANES, HALF_N], F32, name=f"late_slope{o}") for o in range(PASSES)]
@@ -239,7 +247,7 @@ def tile_attend_gml_lch_kernel(tc, xT, wd_words, wd_scales, wv_words, wv_scales,
         for k in range(4):
             project_chunk(first_ps[:, k * CHUNK : (k + 1) * CHUNK], k, q0)
         first_dx = unload(False, first_ps[:, 0 : 3 * CHUNK], "first_dx", "diff31")
-        for k in range(3):
+        for k in (2, 0, 1):
             scatter(False, first_dx[:, k * CHUNK : (k + 1) * CHUNK], k, 0, CHUNK)
 
         g1 = weigh_chunk(1, "y_sb11")
@@ -247,39 +255,39 @@ def tile_attend_gml_lch_kernel(tc, xT, wd_words, wd_scales, wv_words, wv_scales,
         weigh(late_g[0][:], late[0][:], 0, HALF_N, N)
         q1 = quantize_g("second", g1, "second_codes")
         second_ps = ps.tile([P, HALF_N], F32, name="second_ps", tag="b2")
-        rest_ps = {1: ps.tile([P, 3 * CHUNK], F32, name="rest1_ps", tag="b1"), 3: ps.tile([P, 3 * CHUNK], F32, name="rest3_ps", tag="b3")}
-        project_chunk(second_ps[:, 0:CHUNK], 2, q1)
-        project_chunk(second_ps[:, CHUNK:HALF_N], 0, q1)
-        for k in (3, 1):
+        rest_ps = {2: ps.tile([P, 3 * CHUNK], F32, name="rest2_ps", tag="b1"), 3: ps.tile([P, 3 * CHUNK], F32, name="rest3_ps", tag="b3")}
+        for k in range(2):
+            project_chunk(second_ps[:, k * CHUNK : (k + 1) * CHUNK], k, q1)
+        for k in rest_ps:
             project_chunk(rest_ps[k][:, 0:CHUNK], k, q1)
         second_dx = unload(False, second_ps[:], "second_dx", "second_dx")
-        scatter(False, second_dx[:, 0:CHUNK], 2, CHUNK, HALF_N)
-        scatter(False, second_dx[:, CHUNK:HALF_N], 0, CHUNK, HALF_N)
+        for k in range(2):
+            scatter(False, second_dx[:, k * CHUNK : (k + 1) * CHUNK], k, CHUNK, HALF_N)
 
         weigh(late_g[1][:], late[1][:], 1, HALF_N, N)
         late_q = [quantize_g("late0", late_g[0], "late0_codes")]
         held_dx = unload(True, first_ps[:, 3 * CHUNK : N], "held_dx", "weight1")
         late_q.append(quantize_g("late1", late_g[1], "late1_codes"))
         late_ps = {
-            2: ps.tile([P, HALF_N], F32, name="late2_ps", tag="b4")[:],
+            2: rest_ps[2][:, CHUNK : 3 * CHUNK],
             0: ps.tile([P, HALF_N], F32, name="late0_ps", tag="b6")[:],
             3: rest_ps[3][:, CHUNK : 3 * CHUNK],
-            1: rest_ps[1][:, CHUNK : 3 * CHUNK],
+            1: ps.tile([P, HALF_N], F32, name="late1_ps", tag="b4")[:],
         }
         for o in range(PASSES):
             for k in late_ps:
                 project(late_ps[k], k, o, late_q[o][0][:], late_q[o][1][:])
 
         scatter(True, held_dx[:], 3, 0, CHUNK)
-        dx2 = unload(True, late_ps[2], "dx2", "dx2")
+        dx2 = unload(True, rest_ps[2][:], "dx2", "dx2")
         dx3 = unload(True, rest_ps[3][:], "dx3", "dx3")
         dx0 = unload(False, late_ps[0], "dx0", "dx0")
-        dx1 = unload(False, rest_ps[1][:], "dx1", "dx1")
-        scatter(True, dx2[:], 2, HALF_N, N)
+        dx1 = unload(False, late_ps[1], "dx1", "dx1")
+        scatter(True, dx2[:], 2, CHUNK, N)
         store(2)
         scatter(False, dx0[:], 0, HALF_N, N)
         store(0)
+        scatter(False, dx1[:], 1, HALF_N, N)
+        store(1)
         scatter(True, dx3[:], 3, CHUNK, N)
         store(3)
-        scatter(False, dx1[:], 1, CHUNK, N)
-        store(1)

@@ -80,12 +80,12 @@ def tile_attend_gml_lch_kernel(tc, xT, wd_words, wd_scales, wv_words, wv_scales,
                 nc.sync.dma_start(y_sb[o, h][:], y_rows[o][:, :, h * HALF_N : (h + 1) * HALF_N])
 
         load_targets(0)
+        load_targets(1)
         wv_sc_rows = wv_scales.rearrange("o (q r) d -> r q o d", r=SCALE_ROWS)
         for r in range(SCALE_ROWS):
             nc.sync.dma_start(wv_sc[r:P:QUADRANT, :, :].bitcast(I32), wv_sc_rows[r].bitcast(I32))
         wv_sb = sb.tile([P, PASSES, D], I32, name="wv_sb", align_bytes=64)
         nc.sync.dma_start(wv_sb[:], wv_words.rearrange("o p d t -> p o (d t)").bitcast(I32))
-        load_targets(1)
 
         windows = []
         for k in range(2):
@@ -206,13 +206,6 @@ def tile_attend_gml_lch_kernel(tc, xT, wd_words, wd_scales, wv_words, wv_scales,
             for o in range(PASSES):
                 project(dst, k, o, codes[:, o * CHUNK : (o + 1) * CHUNK], scales[:, o * CHUNK : (o + 1) * CHUNK])
 
-        def unload(on_vector, src, name, tag):
-            dx = sb.tile([P, src.shape[1]], F32, name=name, tag=tag)
-            if on_vector:
-                nc.vector.tensor_copy(dx[:], src)
-            else:
-                nc.scalar.activation(dx[:], src, ACT.Copy)
-            return dx
 
         def scatter(on_vector, src, k, lo, hi):
             dst = windows[k][:].indirect(entries(lo, hi))
@@ -243,51 +236,45 @@ def tile_attend_gml_lch_kernel(tc, xT, wd_words, wd_scales, wv_words, wv_scales,
         q0 = quantize_g("first", g0, "y_sb01")
         for c in range(2):
             slope_into(late[1][:, :, c * CHUNK : (c + 1) * CHUNK], 2 + c, 1)
-        first_ps = ps.tile([P, N], F32, name="first_ps", tag="b0")
-        for k in range(4):
-            project_chunk(first_ps[:, k * CHUNK : (k + 1) * CHUNK], k, q0)
-        first_dx = unload(False, first_ps[:, 0 : 3 * CHUNK], "first_dx", "diff31")
-        for k in (2, 0, 1):
-            scatter(False, first_dx[:, k * CHUNK : (k + 1) * CHUNK], k, 0, CHUNK)
+        shared = (0, 1, 3)
+        row = {k: j for j, k in enumerate(shared)}
+        dx = sb.tile([P, len(shared), N], F32, name="dx", tag="diff31")
+        own_ps = ps.tile([P, HALF_N], F32, name="own_ps", tag="b1")
 
+        def early_product(c, quantized, bank):
+            acc = ps.tile([P, len(shared), CHUNK], F32, name="early_ps", tag=bank)
+            for j, k in enumerate(shared):
+                project_chunk(acc[:, j, :], k, quantized)
+            project_chunk(own_ps[:, c * CHUNK : (c + 1) * CHUNK], 2, quantized)
+            nc.scalar.activation(dx[:, :, c * CHUNK : (c + 1) * CHUNK], acc[:], ACT.Copy)
+            for k in range(2):
+                scatter(False, dx[:, k, c * CHUNK : (c + 1) * CHUNK], k, c * CHUNK, (c + 1) * CHUNK)
+
+        early_product(0, q0, "b0")
         g1 = weigh_chunk(1, "y_sb11")
-        late_g = [sb.tile([P, HALF_N * LANES], BF16, name=f"late_g{o}", align_bytes=64) for o in range(PASSES)]
-        weigh(late_g[0][:], late[0][:], 0, HALF_N, N)
-        q1 = quantize_g("second", g1, "second_codes")
-        second_ps = ps.tile([P, HALF_N], F32, name="second_ps", tag="b2")
-        rest_ps = {2: ps.tile([P, 3 * CHUNK], F32, name="rest2_ps", tag="b1"), 3: ps.tile([P, 3 * CHUNK], F32, name="rest3_ps", tag="b3")}
-        for k in range(2):
-            project_chunk(second_ps[:, k * CHUNK : (k + 1) * CHUNK], k, q1)
-        for k in rest_ps:
-            project_chunk(rest_ps[k][:, 0:CHUNK], k, q1)
-        second_dx = unload(False, second_ps[:], "second_dx", "second_dx")
-        for k in range(2):
-            scatter(False, second_dx[:, k * CHUNK : (k + 1) * CHUNK], k, CHUNK, HALF_N)
+        early_product(1, quantize_g("second", g1, "second_codes"), "b2")
 
-        weigh(late_g[1][:], late[1][:], 1, HALF_N, N)
+        late_g = [sb.tile([P, HALF_N * LANES], BF16, name=f"late_g{o}", align_bytes=64) for o in range(PASSES)]
+        for o in range(PASSES):
+            weigh(late_g[o][:], late[o][:], o, HALF_N, N)
         late_q = [quantize_g("late0", late_g[0], "late0_codes")]
-        held_dx = unload(True, first_ps[:, 3 * CHUNK : N], "held_dx", "weight1")
+        held_dx = sb.tile([P, HALF_N], F32, name="held_dx", tag="weight1")
+        nc.vector.tensor_copy(held_dx[:], own_ps[:])
         late_q.append(quantize_g("late1", late_g[1], "late1_codes"))
-        late_ps = {
-            2: rest_ps[2][:, CHUNK : 3 * CHUNK],
-            0: ps.tile([P, HALF_N], F32, name="late0_ps", tag="b6")[:],
-            3: rest_ps[3][:, CHUNK : 3 * CHUNK],
-            1: ps.tile([P, HALF_N], F32, name="late1_ps", tag="b4")[:],
-        }
+        late_ps = {k: ps.tile([P, HALF_N], F32, name=f"late{k}_ps", tag=bank) for k, bank in ((2, "b3"), (0, "b4"), (3, "b5"), (1, "b6"))}
         for o in range(PASSES):
             for k in late_ps:
-                project(late_ps[k], k, o, late_q[o][0][:], late_q[o][1][:])
+                project(late_ps[k][:], k, o, late_q[o][0][:], late_q[o][1][:])
 
-        scatter(True, held_dx[:], 3, 0, CHUNK)
-        dx2 = unload(True, rest_ps[2][:], "dx2", "dx2")
-        dx3 = unload(True, rest_ps[3][:], "dx3", "dx3")
-        dx0 = unload(False, late_ps[0], "dx0", "dx0")
-        dx1 = unload(False, late_ps[1], "dx1", "dx1")
-        scatter(True, dx2[:], 2, CHUNK, N)
+        scatter(True, held_dx[:], 2, 0, HALF_N)
+        late_dx2 = sb.tile([P, HALF_N], F32, name="late_dx2")
+        nc.scalar.activation(late_dx2[:], late_ps[2][:], ACT.Copy)
+        for k in (0, 3, 1):
+            nc.scalar.activation(dx[:, row[k], HALF_N:N], late_ps[k][:], ACT.Copy)
+        scatter(True, late_dx2[:], 2, HALF_N, N)
         store(2)
-        scatter(False, dx0[:], 0, HALF_N, N)
-        store(0)
-        scatter(False, dx1[:], 1, HALF_N, N)
-        store(1)
-        scatter(True, dx3[:], 3, CHUNK, N)
+        for k in range(2):
+            scatter(False, dx[:, k, HALF_N:N], k, HALF_N, N)
+            store(k)
+        scatter(True, dx[:, row[3], :], 3, 0, N)
         store(3)

@@ -1,6 +1,7 @@
 from contextlib import ExitStack
 
 import concourse.mybir as mybir
+from concourse.masks import make_identity
 
 N, T, D, V = 512, 1024, 512, 1024
 FLOPS = 2 * 2 * N * D * V
@@ -24,18 +25,16 @@ QUADRANT = 32
 SCALE_ROWS = 4
 BAND = 16
 PAIR = 2
-HALF_T = T // 2
 HALF_N = N // 2
 CHUNK = 128
 
-FIRST_PAIR_SPLIT = 576
-X_LOADS = ((0, 0, FIRST_PAIR_SPLIT), (0, FIRST_PAIR_SPLIT, T), (1, 0, HALF_T), (1, HALF_T, T))
-VECTOR_CAST_THIRD = 128
-VECTOR_CAST_LAST = 384
+FIRST_PAIR_SPLIT = 640
 VECTOR_PLANES = 6
 
 WINDOW_BYTES = 4 * T
 AT_LATE_X = WINDOW_BYTES - LANES * HALF_N
+AT_HELD = 2 * WINDOW_BYTES
+AT_WD = 4 * WINDOW_BYTES
 
 
 def tile_attend_gml_lch_kernel(tc, xT, wd_words, wd_scales, wv_words, wv_scales, y, cw, rw, offs, out):
@@ -61,14 +60,20 @@ def tile_attend_gml_lch_kernel(tc, xT, wd_words, wd_scales, wv_words, wv_scales,
 
         x_rows = xT.rearrange("(p t) n -> p t n", t=LANES)
         x_raw = {}
-        for u, lo, hi in X_LOADS:
-            x_raw[u, lo] = sb.tile([P, 2, hi - lo], F32, name=f"x_raw{u}_{lo}")
-            nc.sync.dma_start(x_raw[u, lo][:], x_rows[:, 2 * u : 2 * u + 2, lo:hi])
-            if (u, lo, hi) == X_LOADS[1]:
-                nc.sync.dma_start(offsets[:], offs)
+        for lo, hi in ((0, FIRST_PAIR_SPLIT), (FIRST_PAIR_SPLIT, T)):
+            x_raw[lo] = sb.tile([P, 2, hi - lo], F32, name=f"x_raw{lo}")
+            nc.sync.dma_start(x_raw[lo][:], x_rows[:, 0:2, lo:hi])
+        nc.sync.dma_start(offsets[:], offs)
+        x_plane = {}
+        for t in (2, 3):
+            x_plane[t] = sb.tile([P, T], F32, name=f"x_plane{t}")
+            nc.sync.dma_start(x_plane[t][:], x_rows[:, t, :])
 
         wd_hbm = wd_words[0].rearrange("p v t -> p (v t)").bitcast(I32)
-        wd_raw = [sb.tile([P, K_PASS], I32, name=f"wd_raw{o}") for o in range(PASSES)]
+        wd_raw = [
+            reuse.tile([P, K_PASS], I32, name="wd_raw0", offset=AT_WD, align_bytes=64),
+            sb.tile([P, K_PASS], I32, name="wd_raw1"),
+        ]
         for o in range(PASSES):
             nc.sync.dma_start(wd_raw[o][:], wd_hbm[:, o * K_PASS : (o + 1) * K_PASS])
         y_rows = y.rearrange("(o p t) i -> o p t i", p=P, t=LANES)
@@ -76,14 +81,17 @@ def tile_attend_gml_lch_kernel(tc, xT, wd_words, wd_scales, wv_words, wv_scales,
 
         def load_targets(h):
             for o in range(PASSES):
-                y_sb[o, h] = sb.tile([P, LANES, HALF_N], F32, name=f"y_sb{o}{h}", tag=f"y_sb{o}{h}", align_bytes=64)
+                if (o, h) == (0, 1):
+                    y_sb[o, h] = reuse.tile([P, LANES, HALF_N], F32, name="y_sb01", offset=AT_HELD, align_bytes=64)
+                else:
+                    y_sb[o, h] = sb.tile([P, LANES, HALF_N], F32, name=f"y_sb{o}{h}", tag=f"y_sb{o}{h}", align_bytes=64)
                 nc.sync.dma_start(y_sb[o, h][:], y_rows[o][:, :, h * HALF_N : (h + 1) * HALF_N])
 
         load_targets(0)
         load_targets(1)
         wv_sc_rows = wv_scales.rearrange("o (q r) d -> r q o d", r=SCALE_ROWS)
         for r in range(SCALE_ROWS):
-            nc.sync.dma_start(wv_sc[r:P:QUADRANT, :, :].bitcast(I32), wv_sc_rows[r].bitcast(I32))
+            nc.gpsimd.dma_start(wv_sc[r:P:QUADRANT, :, :].bitcast(I32), wv_sc_rows[r].bitcast(I32))
         wv_sb = sb.tile([P, PASSES, D], I32, name="wv_sb", align_bytes=64)
         nc.sync.dma_start(wv_sb[:], wv_words.rearrange("o p d t -> p o (d t)").bitcast(I32))
 
@@ -91,6 +99,9 @@ def tile_attend_gml_lch_kernel(tc, xT, wd_words, wd_scales, wv_words, wv_scales,
         for k in range(2):
             windows.append(sb.tile([P, T], F32, name=f"window{k}"))
             nc.vector.memset(windows[k][:].bitcast(I32), 0)
+
+        ident = sb.tile([P, P], F32, name="ident")
+        make_identity(nc, ident[:])
 
         wd_sc = sb.tile([P, K_PASS], U8, name="wd_sc", align_bytes=64)
         nc.vector.tensor_copy(
@@ -109,75 +120,104 @@ def tile_attend_gml_lch_kernel(tc, xT, wd_words, wd_scales, wv_words, wv_scales,
                 else:
                     nc.scalar.activation(weight[o][:, t, :], rw_sb[:], ACT.Copy, scale=cw_copy[:, o, t : t + 1])
 
-        xg = {lo: sb.tile([P, CHUNK * LANES], BF16, name=f"xg{lo}", align_bytes=64) for lo in (0, CHUNK)}
-        xg[HALF_N] = reuse.tile([P, HALF_N * LANES], BF16, name="xg_late", offset=AT_LATE_X, align_bytes=64)
-        pairs = [sb.tile([P, 2 * T], BF16, name=f"pairs{u}") for u in range(2)]
-
-        def cast(on_vector, u, base, lo, hi):
-            dst = pairs[u][:, 2 * (base + lo) : 2 * (base + hi)].rearrange("p (n e) -> p n e", e=2)
-            src = x_raw[u, base][:, :, lo:hi].rearrange("p e n -> p n e")
-            if on_vector:
-                nc.vector.tensor_copy(dst, src)
-            else:
-                nc.scalar.activation(dst, src, ACT.Copy)
+        xg = [
+            sb.tile([P, HALF_N * LANES], BF16, name="xg_early", align_bytes=64),
+            reuse.tile([P, HALF_N * LANES], BF16, name="xg_late", offset=AT_LATE_X, align_bytes=64),
+        ]
+        pairs = sb.tile([P, 2 * T], BF16, name="pairs")
 
         def entries(lo, hi):
             return offsets[:, lo // BAND : hi // BAND]
 
-        def gather(u, lo, hi):
-            dst = xg[lo][:].bitcast(U32).rearrange("p (i u) -> p i u", u=2)[:, :, u]
-            nc.vector.tensor_copy(dst, pairs[u][:].bitcast(U32).indirect(entries(lo, hi)))
+        def gather_plane(t, lo, hi):
+            dst = xg[0][:].rearrange("p (i t) -> p i t", t=LANES)[:, lo:hi, t]
+            nc.vector.tensor_copy(dst, x_plane[t][:].indirect(entries(lo, hi)))
 
         x_codes, x_sc = {}, {}
 
         def quantize_x(lo, hi):
-            codes = sb.tile([P, hi - lo], U32, name=f"x_codes{lo}", align_bytes=64)
+            if lo == 0:
+                codes = sb.tile([P, hi - lo], U32, name="x_codes0", align_bytes=64)
+            else:
+                codes = reuse.tile([P, hi - lo], U32, name=f"x_codes{lo}", offset=AT_WD + 4 * lo, align_bytes=64)
             scales = sb.tile([P, hi - lo], U8, name=f"x_sc{lo}", align_bytes=64)
-            nc.vector.quantize_mx(out=codes[:].bitcast(E4M3), scales=scales[:], in_=xg[lo][:])
+            h, first = divmod(lo, HALF_N)
+            nc.vector.quantize_mx(out=codes[:].bitcast(E4M3), scales=scales[:], in_=xg[h][:, LANES * first : LANES * (first + hi - lo)])
             for start in range(0, hi - lo, CHUNK):
                 x_codes[(lo + start) // CHUNK] = codes[:, start : start + CHUNK]
                 x_sc[(lo + start) // CHUNK] = scales[:, start : start + CHUNK]
 
-        cast(False, 0, 0, 0, FIRST_PAIR_SPLIT)
-        cast(True, 0, FIRST_PAIR_SPLIT, 0, T - FIRST_PAIR_SPLIT)
-        for lo, hi in ((0, CHUNK), (CHUNK, HALF_N), (HALF_N, N)):
-            gather(0, lo, hi)
-        cast(False, 1, 0, VECTOR_CAST_THIRD, HALF_T)
-        cast(True, 1, 0, 0, VECTOR_CAST_THIRD)
-        cast(True, 1, HALF_T, 0, VECTOR_CAST_LAST)
-        cast(False, 1, HALF_T, VECTOR_CAST_LAST, HALF_T)
-        gather(1, 0, CHUNK)
-        gather(1, CHUNK, HALF_N)
+        pair_cols = pairs[:].rearrange("p (n e) -> p n e", e=2)
+        nc.scalar.activation(pair_cols[:, 0:FIRST_PAIR_SPLIT, :], x_raw[0][:].rearrange("p e n -> p n e"), ACT.Copy)
+        nc.vector.tensor_copy(pair_cols[:, FIRST_PAIR_SPLIT:T, :], x_raw[FIRST_PAIR_SPLIT][:].rearrange("p e n -> p n e"))
+        for h in range(2):
+            dst = xg[h][:].bitcast(U32).rearrange("p (i u) -> p i u", u=2)[:, :, 0]
+            nc.vector.tensor_copy(dst, pairs[:].bitcast(U32).indirect(entries(h * HALF_N, (h + 1) * HALF_N)))
+        gather_plane(2, 0, HALF_N)
+        for lo in (0, CHUNK):
+            gather_plane(3, lo, lo + CHUNK)
+        picked = sb.tile([P, 2, HALF_N], BF16, name="picked")
+        for t in (2, 3):
+            nc.scalar.activation(picked[:, t - 2, :], x_plane[t][:].indirect(entries(HALF_N, N)), ACT.Copy)
+        nc.scalar.activation(
+            xg[1][:].rearrange("p (i t) -> p i t", t=LANES)[:, :, 2:4], picked[:].rearrange("p e i -> p i e"), ACT.Copy
+        )
+
+        wd_sb = [sb.tile([P, K_PASS], U32, name=f"wd_sb{o}", align_bytes=64) for o in range(PASSES)]
         quantize_x(0, CHUNK)
-        gather(1, HALF_N, N)
+        for t in (0, 2):
+            nc.vector.tensor_copy(
+                wd_sb[0][:].bitcast(I32).rearrange("p (t c i) -> p c t i", t=LANES, i=LANES)[:, :, t : t + 2, :],
+                wd_raw[0][:].rearrange("p (c i t) -> p c t i", t=LANES, i=LANES)[:, :, t : t + 2, :],
+            )
+        nc.scalar.copy(
+            wd_sb[1][:].rearrange("p (t m) -> p m t", t=LANES),
+            wd_raw[1][:].bitcast(U32).rearrange("p (m t) -> p m t", t=LANES),
+        )
         quantize_x(CHUNK, HALF_N)
         quantize_x(HALF_N, N)
-
-        wd_sb = []
-        for o in range(PASSES):
-            wd_sb.append(sb.tile([P, K_PASS], U32, name=f"wd_sb{o}", align_bytes=64))
-            nc.scalar.copy(
-                wd_sb[o][:].rearrange("p (t m) -> p m t", t=LANES),
-                wd_raw[o][:].bitcast(U32).rearrange("p (m t) -> p m t", t=LANES),
-            )
 
         for e in range(2):
             windows.append(reuse.tile([P, T], F32, name=f"late_window{e}", offset=e * WINDOW_BYTES, align_bytes=64))
             nc.gpsimd.memset(windows[-1][:].bitcast(I32), 0)
 
-        def slope_into(dst, c, o):
-            h, start = divmod(c * CHUNK, HALF_N)
-            pos = slice(start, start + CHUNK)
-            a = ps.tile([P, LANES, CHUNK], F32, name="a", tag=f"b{2 * c + o}")
+        def scores(c, o, bank):
+            a = ps.tile([P, LANES, CHUNK], F32, name="a", tag=bank)
             for t in range(LANES):
                 nc.tensor.matmul_mx(
                     out=a[:, t, :], lhsT=wd_sb[o][:, t * P : (t + 1) * P].bitcast(E4M3),
                     lhsT_scale=wd_sc[SCALE_ROWS * o : P, t * P : (t + 1) * P],
                     rhs=x_codes[c].bitcast(E4M3), rhs_scale=x_sc[c], start=True, stop=True,
                 )
+            return a
+
+        def targets(c, o):
+            h, start = divmod(c * CHUNK, HALF_N)
+            return y_sb[o, h][:, :, start : start + CHUNK]
+
+        def slope_into(dst, a, c, o):
             diff = sb.tile([P, LANES, CHUNK], F32, name=f"diff{c}{o}", tag=f"diff{c}{o}")
-            nc.vector.tensor_tensor(diff[:], a[:], y_sb[o, h][:, :, pos], ALU.subtract)
+            nc.vector.tensor_tensor(diff[:], a[:], targets(c, o), ALU.subtract)
             nc.scalar.activation(dst, diff[:], ACT.Tanh)
+
+        def turned_targets(c, o, bank):
+            y_minus_a = ps.tile([P, LANES, P], F32, name="y_minus_a", tag=bank)
+            for t in range(LANES):
+                nc.tensor.matmul(y_minus_a[:, t, :], targets(c, o)[:, t, :], ident[:], start=(t == 0), stop=False, is_transpose=True)
+            return y_minus_a
+
+        def turned_slope(y_minus_a, minus_a, c):
+            for t in range(LANES):
+                nc.tensor.matmul(y_minus_a[:, t, :], minus_a[:, t, :], ident[:], start=False, stop=(t == LANES - 1), is_transpose=True)
+            slope_t = sb.tile([P, LANES, P], F32, name=f"slope_t{c}", tag=f"slope_t{c}")
+            nc.scalar.activation(slope_t[:], y_minus_a[:], ACT.Tanh, scale=-1.0)
+            return slope_t
+
+        def turn_back(slope_t, bank):
+            slope = ps.tile([P, LANES, CHUNK], F32, name="slope_ps", tag=bank)
+            for t in range(LANES):
+                nc.tensor.transpose(slope[:, t, :], slope_t[:, t, :], ident[:])
+            return slope
 
         def weigh(dst, slope, o, lo, hi):
             nc.vector.tensor_tensor(
@@ -187,24 +227,25 @@ def tile_attend_gml_lch_kernel(tc, xT, wd_words, wd_scales, wv_words, wv_scales,
                 ALU.mult,
             )
 
-        def quantize_g(name, g, tag):
+        def quantize_g(name, g, codes=None):
             width = g.shape[1] // LANES
-            codes = sb.tile([P, width], U32, name=f"{name}_codes", tag=tag, align_bytes=64)
+            if codes is None:
+                codes = sb.tile([P, width], U32, name=f"{name}_codes", align_bytes=64)
             scales = sb.tile([P, width], U8, name=f"{name}_sc", align_bytes=64)
             nc.vector.quantize_mx(out=codes[:].bitcast(E5M2), scales=scales[:], in_=g[:])
             return codes, scales
 
-        def project(dst, k, o, codes, scales):
+        def project(dst, k, o, codes, scales, start, stop):
             cols = slice(k * P, (k + 1) * P)
             nc.tensor.matmul_mx(
                 out=dst, lhsT=wv_sb[:, o, cols].bitcast(E4M3), lhsT_scale=wv_sc[:, o, cols],
-                rhs=codes.bitcast(E5M2), rhs_scale=scales, start=(o == 0), stop=(o == PASSES - 1),
+                rhs=codes.bitcast(E5M2), rhs_scale=scales, start=start, stop=stop,
             )
 
         def project_chunk(dst, k, quantized):
             codes, scales = quantized
             for o in range(PASSES):
-                project(dst, k, o, codes[:, o * CHUNK : (o + 1) * CHUNK], scales[:, o * CHUNK : (o + 1) * CHUNK])
+                project(dst, k, o, codes[:, o * CHUNK : (o + 1) * CHUNK], scales[:, o * CHUNK : (o + 1) * CHUNK], o == 0, o == PASSES - 1)
 
 
         def scatter(on_vector, src, k, lo, hi):
@@ -219,62 +260,68 @@ def tile_attend_gml_lch_kernel(tc, xT, wd_words, wd_scales, wv_words, wv_scales,
             queue.dma_start(out[k * P : (k + 1) * P, :], windows[k][:])
 
         early = {(c, o): sb.tile([P, LANES, CHUNK], F32, name=f"slope{c}{o}") for c in range(2) for o in range(PASSES)}
-        late = [sb.tile([P, LANES, HALF_N], F32, name=f"late_slope{o}") for o in range(PASSES)]
         for o in range(PASSES):
             for c in range(2):
-                slope_into(early[c, o][:], c, o)
+                slope_into(early[c, o][:], scores(c, o, f"b{2 * c + o}"), c, o)
+        minus_a = sb.tile([P, 2, LANES, CHUNK], F32, name="minus_a", tag="diff11")
+        for c in range(2):
+            nc.scalar.activation(minus_a[:, c], scores(2 + c, 1, f"b{4 + c}")[:], ACT.Copy, scale=-1.0)
 
-        def weigh_chunk(c, tag):
-            g = sb.tile([P, PASSES * CHUNK * LANES], BF16, name=f"g{c}", tag=tag, align_bytes=64)
+        def weigh_chunk(c, g):
             for o in range(PASSES):
                 weigh(g[:, o * K_PASS : (o + 1) * K_PASS], early[c, o][:], o, c * CHUNK, (c + 1) * CHUNK)
             return g
 
-        g0 = weigh_chunk(0, "g0")
+        g0 = weigh_chunk(0, sb.tile([P, PASSES * CHUNK * LANES], BF16, name="g0", tag="y_sb10", align_bytes=64))
+        late0 = sb.tile([P, LANES, HALF_N], F32, name="late_slope0")
         for c in range(2):
-            slope_into(late[0][:, :, c * CHUNK : (c + 1) * CHUNK], 2 + c, 0)
-        q0 = quantize_g("first", g0, "y_sb01")
-        for c in range(2):
-            slope_into(late[1][:, :, c * CHUNK : (c + 1) * CHUNK], 2 + c, 1)
+            slope_into(late0[:, :, c * CHUNK : (c + 1) * CHUNK], scores(2 + c, 0, f"b{2 * c}"), 2 + c, 0)
+        q0 = quantize_g("first", g0, reuse.tile([P, PASSES * CHUNK], U32, name="first_codes", offset=AT_HELD, align_bytes=64))
+        sums = [turned_targets(2 + c, 1, f"b{6 + c}") for c in range(2)]
+        turned = [turned_slope(sums[c], minus_a[:, c], 2 + c) for c in range(2)]
         shared = (0, 1, 3)
-        row = {k: j for j, k in enumerate(shared)}
-        dx = sb.tile([P, len(shared), N], F32, name="dx", tag="diff31")
-        own_ps = ps.tile([P, HALF_N], F32, name="own_ps", tag="b1")
+        dx = sb.tile([P, len(shared) + 1, N], F32, name="dx", tag="slope_t2")
+        own_ps = ps.tile([P, HALF_N], F32, name="own_ps", tag="b3")
 
         def early_product(c, quantized, bank):
             acc = ps.tile([P, len(shared), CHUNK], F32, name="early_ps", tag=bank)
             for j, k in enumerate(shared):
                 project_chunk(acc[:, j, :], k, quantized)
             project_chunk(own_ps[:, c * CHUNK : (c + 1) * CHUNK], 2, quantized)
-            nc.scalar.activation(dx[:, :, c * CHUNK : (c + 1) * CHUNK], acc[:], ACT.Copy)
-            for k in range(2):
+            return acc
+
+        def early_scatter(c, acc):
+            nc.scalar.activation(dx[:, 0 : len(shared), c * CHUNK : (c + 1) * CHUNK], acc[:], ACT.Copy)
+            for k in range(2 - c):
                 scatter(False, dx[:, k, c * CHUNK : (c + 1) * CHUNK], k, c * CHUNK, (c + 1) * CHUNK)
 
-        early_product(0, q0, "b0")
-        g1 = weigh_chunk(1, "y_sb11")
-        early_product(1, quantize_g("second", g1, "second_codes"), "b2")
-
+        first_ps = early_product(0, q0, "b1")
+        late1 = [turn_back(turned[c], f"b{4 + c}") for c in range(2)]
+        early_scatter(0, first_ps)
+        g1 = weigh_chunk(1, reuse.tile([P, PASSES * CHUNK * LANES], BF16, name="g1", offset=AT_HELD + 1024, align_bytes=64))
         late_g = [sb.tile([P, HALF_N * LANES], BF16, name=f"late_g{o}", align_bytes=64) for o in range(PASSES)]
-        for o in range(PASSES):
-            weigh(late_g[o][:], late[o][:], o, HALF_N, N)
-        late_q = [quantize_g("late0", late_g[0], "late0_codes")]
+        weigh(late_g[0][:], late0[:], 0, HALF_N, N)
+        early_scatter(1, early_product(1, quantize_g("second", g1), "b0"))
+        for c in range(2):
+            weigh(late_g[1][:, c * K_PASS : (c + 1) * K_PASS], late1[c][:], 1, (2 + c) * CHUNK, (3 + c) * CHUNK)
+        late_q = [quantize_g("late0", late_g[0])]
         held_dx = sb.tile([P, HALF_N], F32, name="held_dx", tag="weight1")
         nc.vector.tensor_copy(held_dx[:], own_ps[:])
-        late_q.append(quantize_g("late1", late_g[1], "late1_codes"))
-        late_ps = {k: ps.tile([P, HALF_N], F32, name=f"late{k}_ps", tag=bank) for k, bank in ((2, "b3"), (0, "b4"), (3, "b5"), (1, "b6"))}
+        late_q.append(quantize_g("late1", late_g[1]))
+        late_tiles = ((3, 2), (0, 1))
+        late_ps = [ps.tile([P, 2, HALF_N], F32, name="late_ps", tag=bank) for bank in ("b2", "b6")]
         for o in range(PASSES):
-            for k in late_ps:
-                project(late_ps[k][:], k, o, late_q[o][0][:], late_q[o][1][:])
+            for acc, tiles in zip(late_ps, late_tiles):
+                for j, k in enumerate(tiles):
+                    project(acc[:, j, :], k, o, late_q[o][0][:], late_q[o][1][:], (o, j) == (0, 0), (o, j) == (1, 1))
 
         scatter(True, held_dx[:], 2, 0, HALF_N)
-        late_dx2 = sb.tile([P, HALF_N], F32, name="late_dx2")
-        nc.scalar.activation(late_dx2[:], late_ps[2][:], ACT.Copy)
-        for k in (0, 3, 1):
-            nc.scalar.activation(dx[:, row[k], HALF_N:N], late_ps[k][:], ACT.Copy)
-        scatter(True, late_dx2[:], 2, HALF_N, N)
+        nc.scalar.activation(dx[:, 2:4, HALF_N:N], late_ps[0][:], ACT.Copy)
+        nc.scalar.activation(dx[:, 0:2, HALF_N:N], late_ps[1][:], ACT.Copy)
+        scatter(True, dx[:, 3, HALF_N:N], 2, HALF_N, N)
         store(2)
-        for k in range(2):
-            scatter(False, dx[:, k, HALF_N:N], k, HALF_N, N)
+        for k, lo in ((0, HALF_N), (1, CHUNK)):
+            scatter(False, dx[:, k, lo:N], k, lo, N)
             store(k)
-        scatter(True, dx[:, row[3], :], 3, 0, N)
+        scatter(True, dx[:, 2, :], 3, 0, N)
         store(3)

@@ -55,14 +55,15 @@ def tile_attend_gml_lch_kernel(tc, xT, wd_words, wd_scales, wv_words, wv_scales,
         cw_sb = sb.tile([P, PASSES, 8], F32, name="cw_sb")
         nc.sync.dma_start(cw_sb[:, :, 0:LANES], cw.rearrange("(o p t) e -> p o (t e)", p=P, t=LANES))
         wd_sc_rows = wd_scales[0].bitcast(I32).rearrange("(q r) (o c) -> q o r c", r=SCALE_ROWS, o=PASSES)
-        for q in range(P // QUADRANT):
-            nc.sync.dma_start(wd_sc_raw[QUADRANT * q : QUADRANT * q + PASSES * SCALE_ROWS, :].bitcast(I32), wd_sc_rows[q])
 
         x_rows = xT.rearrange("(p t) n -> p t n", t=LANES)
         x_raw = {}
         for lo, hi in ((0, FIRST_PAIR_SPLIT), (FIRST_PAIR_SPLIT, T)):
             x_raw[lo] = sb.tile([P, 2, hi - lo], F32, name=f"x_raw{lo}")
             nc.sync.dma_start(x_raw[lo][:], x_rows[:, 0:2, lo:hi])
+            if lo == 0:
+                for q in range(P // QUADRANT):
+                    nc.sync.dma_start(wd_sc_raw[QUADRANT * q : QUADRANT * q + PASSES * SCALE_ROWS, :].bitcast(I32), wd_sc_rows[q])
         nc.sync.dma_start(offsets[:], offs)
         x_plane = {}
         for t in (2, 3):
@@ -281,47 +282,50 @@ def tile_attend_gml_lch_kernel(tc, xT, wd_words, wd_scales, wv_words, wv_scales,
         turned = [turned_slope(sums[c], minus_a[:, c], 2 + c) for c in range(2)]
         shared = (0, 1, 3)
         dx = sb.tile([P, len(shared) + 1, N], F32, name="dx", tag="slope_t2")
-        own_ps = ps.tile([P, HALF_N], F32, name="own_ps", tag="b3")
+        own_ps = ps.tile([P, 3 * CHUNK], F32, name="own_ps", tag="b3")
 
-        def early_product(c, quantized, bank):
-            acc = ps.tile([P, len(shared), CHUNK], F32, name="early_ps", tag=bank)
-            for j, k in enumerate(shared):
-                project_chunk(acc[:, j, :], k, quantized)
-            project_chunk(own_ps[:, c * CHUNK : (c + 1) * CHUNK], 2, quantized)
-            return acc
-
-        def early_scatter(c, acc):
-            nc.scalar.activation(dx[:, 0 : len(shared), c * CHUNK : (c + 1) * CHUNK], acc[:], ACT.Copy)
-            for k in range(2 - c):
-                scatter(False, dx[:, k, c * CHUNK : (c + 1) * CHUNK], k, c * CHUNK, (c + 1) * CHUNK)
-
-        first_ps = early_product(0, q0, "b1")
+        first_ps = ps.tile([P, 3, CHUNK], F32, name="first_ps", tag="b1")
+        for j, k in enumerate(shared):
+            project_chunk(first_ps[:, j, :], k, q0)
+        project_chunk(own_ps[:, 0:CHUNK], 2, q0)
         late1 = [turn_back(turned[c], f"b{4 + c}") for c in range(2)]
-        early_scatter(0, first_ps)
+        nc.scalar.activation(dx[:, 0:3, 0:CHUNK], first_ps[:], ACT.Copy)
+        for k in range(2):
+            scatter(False, dx[:, k, 0:CHUNK], k, 0, CHUNK)
         g1 = weigh_chunk(1, reuse.tile([P, PASSES * CHUNK * LANES], BF16, name="g1", offset=AT_HELD + 1024, align_bytes=64))
         late_g = [sb.tile([P, HALF_N * LANES], BF16, name=f"late_g{o}", align_bytes=64) for o in range(PASSES)]
         weigh(late_g[0][:], late0[:], 0, HALF_N, N)
-        early_scatter(1, early_product(1, quantize_g("second", g1), "b0"))
+        q1 = quantize_g("second", g1)
+        second_ps = ps.tile([P, 2, CHUNK], F32, name="second_ps", tag="b0")
+        for j, k in enumerate((0, 3)):
+            project_chunk(second_ps[:, j, :], k, q1)
+        for j, k in ((1, 2), (2, 1)):
+            project_chunk(own_ps[:, j * CHUNK : (j + 1) * CHUNK], k, q1)
+        nc.scalar.activation(dx[:, 0:3:2, CHUNK:HALF_N], second_ps[:], ACT.Copy)
+        scatter(False, dx[:, 0, CHUNK:HALF_N], 0, CHUNK, HALF_N)
         for c in range(2):
             weigh(late_g[1][:, c * K_PASS : (c + 1) * K_PASS], late1[c][:], 1, (2 + c) * CHUNK, (3 + c) * CHUNK)
         late_q = [quantize_g("late0", late_g[0])]
-        held_dx = sb.tile([P, HALF_N], F32, name="held_dx", tag="weight1")
+        held_dx = sb.tile([P, 3 * CHUNK], F32, name="held_dx", tag="weight1")
         nc.vector.tensor_copy(held_dx[:], own_ps[:])
         late_q.append(quantize_g("late1", late_g[1]))
-        late_tiles = ((3, 2), (0, 1))
-        late_ps = [ps.tile([P, 2, HALF_N], F32, name="late_ps", tag=bank) for bank in ("b2", "b6")]
+        late_tiles = ((0, 2), (1,), (3,))
+        late_ps = [ps.tile([P, len(tiles), HALF_N], F32, name="late_ps", tag=bank) for tiles, bank in zip(late_tiles, ("b2", "b6", "b7"))]
         for o in range(PASSES):
             for acc, tiles in zip(late_ps, late_tiles):
                 for j, k in enumerate(tiles):
-                    project(acc[:, j, :], k, o, late_q[o][0][:], late_q[o][1][:], (o, j) == (0, 0), (o, j) == (1, 1))
+                    project(acc[:, j, :], k, o, late_q[o][0][:], late_q[o][1][:], (o, j) == (0, 0), (o, j) == (1, len(tiles) - 1))
 
-        scatter(True, held_dx[:], 2, 0, HALF_N)
-        nc.scalar.activation(dx[:, 2:4, HALF_N:N], late_ps[0][:], ACT.Copy)
-        nc.scalar.activation(dx[:, 0:2, HALF_N:N], late_ps[1][:], ACT.Copy)
+        scatter(True, held_dx[:, 0:HALF_N], 2, 0, HALF_N)
+        scatter(True, held_dx[:, HALF_N : 3 * CHUNK], 1, CHUNK, HALF_N)
+        nc.vector.tensor_copy(dx[:, 2, HALF_N:N], late_ps[2][:, 0, :])
+        nc.scalar.activation(dx[:, 0:4:3, HALF_N:N], late_ps[0][:], ACT.Copy)
         scatter(True, dx[:, 3, HALF_N:N], 2, HALF_N, N)
         store(2)
-        for k, lo in ((0, HALF_N), (1, CHUNK)):
-            scatter(False, dx[:, k, lo:N], k, lo, N)
-            store(k)
+        scatter(False, dx[:, 0, HALF_N:N], 0, HALF_N, N)
+        store(0)
+        nc.scalar.activation(dx[:, 1, HALF_N:N], late_ps[1][:, 0, :], ACT.Copy)
+        scatter(False, dx[:, 1, HALF_N:N], 1, HALF_N, N)
+        store(1)
         scatter(True, dx[:, 2, :], 3, 0, N)
         store(3)

@@ -28,11 +28,12 @@ PAIR = 2
 HALF_N = N // 2
 CHUNK = 128
 
-FIRST_PAIR_SPLIT = 640
-VECTOR_PLANES = 6
+VECTOR_PLANES = 5
+
+VECTOR_ENTRIES = 320
 
 WINDOW_BYTES = 4 * T
-AT_LATE_X = WINDOW_BYTES - LANES * HALF_N
+AT_LATE_X = 0
 AT_HELD = 2 * WINDOW_BYTES
 AT_WD = 4 * WINDOW_BYTES
 
@@ -57,18 +58,15 @@ def tile_attend_gml_lch_kernel(tc, xT, wd_words, wd_scales, wv_words, wv_scales,
         wd_sc_rows = wd_scales[0].bitcast(I32).rearrange("(q r) (o c) -> q o r c", r=SCALE_ROWS, o=PASSES)
 
         x_rows = xT.rearrange("(p t) n -> p t n", t=LANES)
-        x_raw = {}
-        for lo, hi in ((0, FIRST_PAIR_SPLIT), (FIRST_PAIR_SPLIT, T)):
-            x_raw[lo] = sb.tile([P, 2, hi - lo], F32, name=f"x_raw{lo}")
-            nc.sync.dma_start(x_raw[lo][:], x_rows[:, 0:2, lo:hi])
-            if lo == 0:
-                for q in range(P // QUADRANT):
-                    nc.sync.dma_start(wd_sc_raw[QUADRANT * q : QUADRANT * q + PASSES * SCALE_ROWS, :].bitcast(I32), wd_sc_rows[q])
-        nc.sync.dma_start(offsets[:], offs)
         x_plane = {}
-        for t in (2, 3):
+        for t in range(LANES):
             x_plane[t] = sb.tile([P, T], F32, name=f"x_plane{t}")
             nc.sync.dma_start(x_plane[t][:], x_rows[:, t, :])
+            if t == 0:
+                nc.sync.dma_start(offsets[:], offs)
+            if t == 1:
+                for q in range(P // QUADRANT):
+                    nc.sync.dma_start(wd_sc_raw[QUADRANT * q : QUADRANT * q + PASSES * SCALE_ROWS, :].bitcast(I32), wd_sc_rows[q])
 
         wd_hbm = wd_words[0].rearrange("p v t -> p (v t)").bitcast(I32)
         wd_raw = [
@@ -121,50 +119,40 @@ def tile_attend_gml_lch_kernel(tc, xT, wd_words, wd_scales, wv_words, wv_scales,
                 else:
                     nc.scalar.activation(weight[o][:, t, :], rw_sb[:], ACT.Copy, scale=cw_copy[:, o, t : t + 1])
 
-        xg = [
-            sb.tile([P, HALF_N * LANES], BF16, name="xg_early", align_bytes=64),
-            reuse.tile([P, HALF_N * LANES], BF16, name="xg_late", offset=AT_LATE_X, align_bytes=64),
-        ]
-        pairs = sb.tile([P, 2 * T], BF16, name="pairs")
+        xg_first = sb.tile([P, CHUNK * LANES], BF16, name="xg_first", align_bytes=64)
+        xg_rest = reuse.tile([P, (N - CHUNK) * LANES], BF16, name="xg_rest", offset=AT_LATE_X, align_bytes=64)
 
         def entries(lo, hi):
             return offsets[:, lo // BAND : hi // BAND]
-
-        def gather_plane(t, lo, hi):
-            dst = xg[0][:].rearrange("p (i t) -> p i t", t=LANES)[:, lo:hi, t]
-            nc.vector.tensor_copy(dst, x_plane[t][:].indirect(entries(lo, hi)))
 
         x_codes, x_sc = {}, {}
 
         def quantize_x(lo, hi):
             if lo == 0:
                 codes = sb.tile([P, hi - lo], U32, name="x_codes0", align_bytes=64)
+                values = xg_first[:]
             else:
                 codes = reuse.tile([P, hi - lo], U32, name=f"x_codes{lo}", offset=AT_WD + 4 * lo, align_bytes=64)
+                values = xg_rest[:, LANES * (lo - CHUNK) : LANES * (hi - CHUNK)]
             scales = sb.tile([P, hi - lo], U8, name=f"x_sc{lo}", align_bytes=64)
-            h, first = divmod(lo, HALF_N)
-            nc.vector.quantize_mx(out=codes[:].bitcast(E4M3), scales=scales[:], in_=xg[h][:, LANES * first : LANES * (first + hi - lo)])
+            nc.vector.quantize_mx(out=codes[:].bitcast(E4M3), scales=scales[:], in_=values)
             for start in range(0, hi - lo, CHUNK):
                 x_codes[(lo + start) // CHUNK] = codes[:, start : start + CHUNK]
                 x_sc[(lo + start) // CHUNK] = scales[:, start : start + CHUNK]
 
-        pair_cols = pairs[:].rearrange("p (n e) -> p n e", e=2)
-        nc.scalar.activation(pair_cols[:, 0:FIRST_PAIR_SPLIT, :], x_raw[0][:].rearrange("p e n -> p n e"), ACT.Copy)
-        nc.vector.tensor_copy(pair_cols[:, FIRST_PAIR_SPLIT:T, :], x_raw[FIRST_PAIR_SPLIT][:].rearrange("p e n -> p n e"))
-        for h in range(2):
-            dst = xg[h][:].bitcast(U32).rearrange("p (i u) -> p i u", u=2)[:, :, 0]
-            nc.vector.tensor_copy(dst, pairs[:].bitcast(U32).indirect(entries(h * HALF_N, (h + 1) * HALF_N)))
-        gather_plane(2, 0, HALF_N)
-        for lo in (0, CHUNK):
-            gather_plane(3, lo, lo + CHUNK)
-        picked = sb.tile([P, 2, HALF_N], BF16, name="picked")
-        for t in (2, 3):
-            nc.scalar.activation(picked[:, t - 2, :], x_plane[t][:].indirect(entries(HALF_N, N)), ACT.Copy)
+        rest_lanes = xg_rest[:].rearrange("p (i t) -> p i t", t=LANES)
+        picked = sb.tile([P, LANES, N - VECTOR_ENTRIES], BF16, name="picked", tag="picked", align_bytes=64)
+        for t in range(LANES):
+            nc.vector.tensor_copy(xg_first[:].rearrange("p (i t) -> p i t", t=LANES)[:, :, t], x_plane[t][:].indirect(entries(0, CHUNK)))
+            nc.vector.tensor_copy(rest_lanes[:, 0 : VECTOR_ENTRIES - CHUNK, t], x_plane[t][:].indirect(entries(CHUNK, VECTOR_ENTRIES)))
+            nc.scalar.activation(picked[:, t, :], x_plane[t][:].indirect(entries(VECTOR_ENTRIES, N)), ACT.Copy)
         nc.scalar.activation(
-            xg[1][:].rearrange("p (i t) -> p i t", t=LANES)[:, :, 2:4], picked[:].rearrange("p e i -> p i e"), ACT.Copy
+            xg_rest[:, LANES * (VECTOR_ENTRIES - CHUNK) :].rearrange("p (b i t) -> p b t i", t=LANES, i=PAIR),
+            picked[:].rearrange("p t (b i) -> p b t i", i=PAIR),
+            ACT.Copy,
         )
 
-        wd_sb = [sb.tile([P, K_PASS], U32, name=f"wd_sb{o}", align_bytes=64) for o in range(PASSES)]
+        wd_sb = [sb.tile([P, K_PASS], U32, name=f"wd_sb{o}", tag=("wd_sb0", "picked")[o], align_bytes=64) for o in range(PASSES)]
         quantize_x(0, CHUNK)
         for t in (0, 2):
             nc.vector.tensor_copy(

from contextlib import ExitStack

import concourse.mybir as mybir
from concourse.masks import make_identity

N, T, D, V = 512, 1024, 512, 1024
FLOPS = 2 * 2 * N * D * V

F32 = mybir.dt.float32
BF16 = mybir.dt.bfloat16
I32 = mybir.dt.int32
U32 = mybir.dt.uint32
U16 = mybir.dt.uint16
U8 = mybir.dt.uint8
E4M3 = mybir.dt.float8_e4m3fn_x4
E5M2 = mybir.dt.float8_e5m2_x4
ACT = mybir.ActivationFunctionType
ALU = mybir.AluOpType

P = 128
LANES = 4
K_PASS = P * LANES
PASSES = V // K_PASS
QUADRANT = 32
SCALE_ROWS = 4
BAND = 16
PAIR = 2
HALF_N = N // 2
CHUNK = 128

VECTOR_PLANES = 5

VECTOR_ENTRIES = 320

WINDOW_BYTES = 4 * T
AT_LATE_X = 0
AT_HELD = 2 * WINDOW_BYTES
AT_WD = 4 * WINDOW_BYTES


def tile_attend_gml_lch_kernel(tc, xT, wd_words, wd_scales, wv_words, wv_scales, y, cw, rw, offs, out):
    nc = tc.nc
    with ExitStack() as ctx:
        sb = ctx.enter_context(tc.tile_pool(name="sb", bufs=1))
        reuse = ctx.enter_context(tc.tile_pool(name="reuse", bufs=1))
        ps = ctx.enter_context(tc.psum_pool(name="ps", bufs=1))

        offsets = sb.tile([P, N // BAND], U16, name="offsets")
        wd_sc_raw = sb.tile([P, K_PASS], U8, name="wd_sc_raw", align_bytes=64)
        wv_sc = sb.tile([P, PASSES, D], U8, name="wv_sc", align_bytes=64)
        nc.gpsimd.memset(wd_sc_raw[:].bitcast(I32), 0)
        nc.gpsimd.memset(wv_sc[:].rearrange("p o d -> p (o d)").bitcast(I32), 0)

        rw_sb = sb.tile([P, N], F32, name="rw_sb")
        nc.sync.dma_start(rw_sb[:], rw)
        cw_sb = sb.tile([P, PASSES, 8], F32, name="cw_sb")
        nc.sync.dma_start(cw_sb[:, :, 0:LANES], cw.rearrange("(o p t) e -> p o (t e)", p=P, t=LANES))
        wd_sc_rows = wd_scales[0].bitcast(I32).rearrange("(q r) (o c) -> q o r c", r=SCALE_ROWS, o=PASSES)

        x_rows = xT.rearrange("(p t) n -> p t n", t=LANES)
        x_plane = {}
        for t in range(LANES):
            x_plane[t] = sb.tile([P, T], F32, name=f"x_plane{t}")
            nc.sync.dma_start(x_plane[t][:], x_rows[:, t, :])
            if t == 0:
                nc.sync.dma_start(offsets[:], offs)
            if t == 1:
                for q in range(P // QUADRANT):
                    nc.sync.dma_start(wd_sc_raw[QUADRANT * q : QUADRANT * q + PASSES * SCALE_ROWS, :].bitcast(I32), wd_sc_rows[q])

        wd_hbm = wd_words[0].rearrange("p v t -> p (v t)").bitcast(I32)
        wd_raw = [
            reuse.tile([P, K_PASS], I32, name="wd_raw0", offset=AT_WD, align_bytes=64),
            sb.tile([P, K_PASS], I32, name="wd_raw1"),
        ]
        for o in range(PASSES):
            nc.sync.dma_start(wd_raw[o][:], wd_hbm[:, o * K_PASS : (o + 1) * K_PASS])
        y_rows = y.rearrange("(o p t) i -> o p t i", p=P, t=LANES)
        y_sb = {}

        def load_targets(h):
            for o in range(PASSES):
                if (o, h) == (0, 1):
                    y_sb[o, h] = reuse.tile([P, LANES, HALF_N], F32, name="y_sb01", offset=AT_HELD, align_bytes=64)
                else:
                    y_sb[o, h] = sb.tile([P, LANES, HALF_N], F32, name=f"y_sb{o}{h}", tag=f"y_sb{o}{h}", align_bytes=64)
                nc.sync.dma_start(y_sb[o, h][:], y_rows[o][:, :, h * HALF_N : (h + 1) * HALF_N])

        load_targets(0)
        load_targets(1)
        wv_sc_rows = wv_scales.rearrange("o (q r) d -> r q o d", r=SCALE_ROWS)
        for r in range(SCALE_ROWS):
            nc.gpsimd.dma_start(wv_sc[r:P:QUADRANT, :, :].bitcast(I32), wv_sc_rows[r].bitcast(I32))
        wv_sb = sb.tile([P, PASSES, D], I32, name="wv_sb", align_bytes=64)
        nc.sync.dma_start(wv_sb[:], wv_words.rearrange("o p d t -> p o (d t)").bitcast(I32))

        windows = []
        for k in range(2):
            windows.append(sb.tile([P, T], F32, name=f"window{k}"))
            nc.vector.memset(windows[k][:].bitcast(I32), 0)

        ident = sb.tile([P, P], F32, name="ident")
        make_identity(nc, ident[:])

        wd_sc = sb.tile([P, K_PASS], U8, name="wd_sc", align_bytes=64)
        nc.vector.tensor_copy(
            wd_sc[:].rearrange("p (t m) -> p t m", t=LANES),
            wd_sc_raw[:].rearrange("p (m t) -> p t m", t=LANES),
        )

        cw_copy = sb.tile([P, PASSES, LANES], F32, name="cw_copy")
        nc.scalar.activation(cw_copy[:], cw_sb[:, :, 0:LANES], ACT.Copy)
        weight = []
        for o in range(PASSES):
            weight.append(sb.tile([P, LANES, N], F32, name=f"weight{o}", tag=f"weight{o}"))
            for t in range(LANES):
                if o * LANES + t < VECTOR_PLANES:
                    nc.vector.tensor_scalar(weight[o][:, t, :], rw_sb[:], cw_sb[:, o, t : t + 1], None, ALU.mult)
                else:
                    nc.scalar.activation(weight[o][:, t, :], rw_sb[:], ACT.Copy, scale=cw_copy[:, o, t : t + 1])

        xg_first = sb.tile([P, CHUNK * LANES], BF16, name="xg_first", align_bytes=64)
        xg_rest = reuse.tile([P, (N - CHUNK) * LANES], BF16, name="xg_rest", offset=AT_LATE_X, align_bytes=64)

        def entries(lo, hi):
            return offsets[:, lo // BAND : hi // BAND]

        x_codes, x_sc = {}, {}

        def quantize_x(lo, hi):
            if lo == 0:
                codes = sb.tile([P, hi - lo], U32, name="x_codes0", align_bytes=64)
                values = xg_first[:]
            else:
                codes = reuse.tile([P, hi - lo], U32, name=f"x_codes{lo}", offset=AT_WD + 4 * lo, align_bytes=64)
                values = xg_rest[:, LANES * (lo - CHUNK) : LANES * (hi - CHUNK)]
            scales = sb.tile([P, hi - lo], U8, name=f"x_sc{lo}", align_bytes=64)
            nc.vector.quantize_mx(out=codes[:].bitcast(E4M3), scales=scales[:], in_=values)
            for start in range(0, hi - lo, CHUNK):
                x_codes[(lo + start) // CHUNK] = codes[:, start : start + CHUNK]
                x_sc[(lo + start) // CHUNK] = scales[:, start : start + CHUNK]

        rest_lanes = xg_rest[:].rearrange("p (i t) -> p i t", t=LANES)
        picked = sb.tile([P, LANES, N - VECTOR_ENTRIES], BF16, name="picked", tag="picked", align_bytes=64)
        for t in range(LANES):
            nc.vector.tensor_copy(xg_first[:].rearrange("p (i t) -> p i t", t=LANES)[:, :, t], x_plane[t][:].indirect(entries(0, CHUNK)))
            nc.vector.tensor_copy(rest_lanes[:, 0 : VECTOR_ENTRIES - CHUNK, t], x_plane[t][:].indirect(entries(CHUNK, VECTOR_ENTRIES)))
            nc.scalar.activation(picked[:, t, :], x_plane[t][:].indirect(entries(VECTOR_ENTRIES, N)), ACT.Copy)
        nc.scalar.activation(
            xg_rest[:, LANES * (VECTOR_ENTRIES - CHUNK) :].rearrange("p (b i t) -> p b t i", t=LANES, i=PAIR),
            picked[:].rearrange("p t (b i) -> p b t i", i=PAIR),
            ACT.Copy,
        )

        wd_sb = [sb.tile([P, K_PASS], U32, name=f"wd_sb{o}", tag=("wd_sb0", "picked")[o], align_bytes=64) for o in range(PASSES)]
        quantize_x(0, CHUNK)
        for t in (0, 2):
            nc.vector.tensor_copy(
                wd_sb[0][:].bitcast(I32).rearrange("p (t c i) -> p c t i", t=LANES, i=LANES)[:, :, t : t + 2, :],
                wd_raw[0][:].rearrange("p (c i t) -> p c t i", t=LANES, i=LANES)[:, :, t : t + 2, :],
            )
        nc.scalar.copy(
            wd_sb[1][:].rearrange("p (t m) -> p m t", t=LANES),
            wd_raw[1][:].bitcast(U32).rearrange("p (m t) -> p m t", t=LANES),
        )
        quantize_x(CHUNK, HALF_N)
        quantize_x(HALF_N, N)

        for e in range(2):
            windows.append(reuse.tile([P, T], F32, name=f"late_window{e}", offset=e * WINDOW_BYTES, align_bytes=64))
            nc.gpsimd.memset(windows[-1][:].bitcast(I32), 0)

        def scores(c, o, bank):
            a = ps.tile([P, LANES, CHUNK], F32, name="a", tag=bank)
            for t in range(LANES):
                nc.tensor.matmul_mx(
                    out=a[:, t, :], lhsT=wd_sb[o][:, t * P : (t + 1) * P].bitcast(E4M3),
                    lhsT_scale=wd_sc[SCALE_ROWS * o : P, t * P : (t + 1) * P],
                    rhs=x_codes[c].bitcast(E4M3), rhs_scale=x_sc[c], start=True, stop=True,
                )
            return a

        def targets(c, o):
            h, start = divmod(c * CHUNK, HALF_N)
            return y_sb[o, h][:, :, start : start + CHUNK]

        def slope_into(dst, a, c, o):
            diff = sb.tile([P, LANES, CHUNK], F32, name=f"diff{c}{o}", tag=f"diff{c}{o}")
            nc.vector.tensor_tensor(diff[:], a[:], targets(c, o), ALU.subtract)
            nc.scalar.activation(dst, diff[:], ACT.Tanh)

        def turned_targets(c, o, bank):
            y_minus_a = ps.tile([P, LANES, P], F32, name="y_minus_a", tag=bank)
            for t in range(LANES):
                nc.tensor.matmul(y_minus_a[:, t, :], targets(c, o)[:, t, :], ident[:], start=(t == 0), stop=False, is_transpose=True)
            return y_minus_a

        def turned_slope(y_minus_a, minus_a, c):
            for t in range(LANES):
                nc.tensor.matmul(y_minus_a[:, t, :], minus_a[:, t, :], ident[:], start=False, stop=(t == LANES - 1), is_transpose=True)
            slope_t = sb.tile([P, LANES, P], F32, name=f"slope_t{c}", tag=f"slope_t{c}")
            nc.scalar.activation(slope_t[:], y_minus_a[:], ACT.Tanh, scale=-1.0)
            return slope_t

        def turn_back(slope_t, bank):
            slope = ps.tile([P, LANES, CHUNK], F32, name="slope_ps", tag=bank)
            for t in range(LANES):
                nc.tensor.transpose(slope[:, t, :], slope_t[:, t, :], ident[:])
            return slope

        def weigh(dst, slope, o, lo, hi):
            nc.vector.tensor_tensor(
                dst.rearrange("p (b i t) -> p b t i", t=LANES, i=PAIR),
                slope.rearrange("p t (b i) -> p b t i", i=PAIR),
                weight[o][:, :, lo:hi].rearrange("p t (b i) -> p b t i", i=PAIR),
                ALU.mult,
            )

        def quantize_g(name, g, codes=None):
            width = g.shape[1] // LANES
            if codes is None:
                codes = sb.tile([P, width], U32, name=f"{name}_codes", align_bytes=64)
            scales = sb.tile([P, width], U8, name=f"{name}_sc", align_bytes=64)
            nc.vector.quantize_mx(out=codes[:].bitcast(E5M2), scales=scales[:], in_=g[:])
            return codes, scales

        def project(dst, k, o, codes, scales, start, stop):
            cols = slice(k * P, (k + 1) * P)
            nc.tensor.matmul_mx(
                out=dst, lhsT=wv_sb[:, o, cols].bitcast(E4M3), lhsT_scale=wv_sc[:, o, cols],
                rhs=codes.bitcast(E5M2), rhs_scale=scales, start=start, stop=stop,
            )

        def project_chunk(dst, k, quantized):
            codes, scales = quantized
            for o in range(PASSES):
                project(dst, k, o, codes[:, o * CHUNK : (o + 1) * CHUNK], scales[:, o * CHUNK : (o + 1) * CHUNK], o == 0, o == PASSES - 1)


        def scatter(on_vector, src, k, lo, hi):
            dst = windows[k][:].indirect(entries(lo, hi))
            if on_vector:
                nc.vector.tensor_copy(dst, src)
            else:
                nc.scalar.activation(dst, src, ACT.Copy)

        def store(k):
            queue = nc.sync if k >= 2 else nc.scalar
            queue.dma_start(out[k * P : (k + 1) * P, :], windows[k][:])

        early = {(c, o): sb.tile([P, LANES, CHUNK], F32, name=f"slope{c}{o}") for c in range(2) for o in range(PASSES)}
        for o in range(PASSES):
            for c in range(2):
                slope_into(early[c, o][:], scores(c, o, f"b{2 * c + o}"), c, o)
        minus_a = sb.tile([P, 2, LANES, CHUNK], F32, name="minus_a", tag="diff11")
        for c in range(2):
            nc.scalar.activation(minus_a[:, c], scores(2 + c, 1, f"b{4 + c}")[:], ACT.Copy, scale=-1.0)

        def weigh_chunk(c, g):
            for o in range(PASSES):
                weigh(g[:, o * K_PASS : (o + 1) * K_PASS], early[c, o][:], o, c * CHUNK, (c + 1) * CHUNK)
            return g

        g0 = weigh_chunk(0, sb.tile([P, PASSES * CHUNK * LANES], BF16, name="g0", tag="y_sb10", align_bytes=64))
        late0 = sb.tile([P, LANES, HALF_N], F32, name="late_slope0")
        for c in range(2):
            slope_into(late0[:, :, c * CHUNK : (c + 1) * CHUNK], scores(2 + c, 0, f"b{2 * c}"), 2 + c, 0)
        q0 = quantize_g("first", g0, reuse.tile([P, PASSES * CHUNK], U32, name="first_codes", offset=AT_HELD, align_bytes=64))
        sums = [turned_targets(2 + c, 1, f"b{6 + c}") for c in range(2)]
        turned = [turned_slope(sums[c], minus_a[:, c], 2 + c) for c in range(2)]
        shared = (0, 1, 3)
        dx = sb.tile([P, len(shared) + 1, N], F32, name="dx", tag="slope_t2")
        own_ps = ps.tile([P, 3 * CHUNK], F32, name="own_ps", tag="b3")

        first_ps = ps.tile([P, 3, CHUNK], F32, name="first_ps", tag="b1")
        for j, k in enumerate(shared):
            project_chunk(first_ps[:, j, :], k, q0)
        project_chunk(own_ps[:, 0:CHUNK], 2, q0)
        late1 = [turn_back(turned[c], f"b{4 + c}") for c in range(2)]
        nc.scalar.activation(dx[:, 0:3, 0:CHUNK], first_ps[:], ACT.Copy)
        for k in range(2):
            scatter(False, dx[:, k, 0:CHUNK], k, 0, CHUNK)
        g1 = weigh_chunk(1, reuse.tile([P, PASSES * CHUNK * LANES], BF16, name="g1", offset=AT_HELD + 1024, align_bytes=64))
        late_g = [sb.tile([P, HALF_N * LANES], BF16, name=f"late_g{o}", align_bytes=64) for o in range(PASSES)]
        weigh(late_g[0][:], late0[:], 0, HALF_N, N)
        q1 = quantize_g("second", g1)
        second_ps = ps.tile([P, 2, CHUNK], F32, name="second_ps", tag="b0")
        for j, k in enumerate((0, 3)):
            project_chunk(second_ps[:, j, :], k, q1)
        for j, k in ((1, 2), (2, 1)):
            project_chunk(own_ps[:, j * CHUNK : (j + 1) * CHUNK], k, q1)
        nc.scalar.activation(dx[:, 0:3:2, CHUNK:HALF_N], second_ps[:], ACT.Copy)
        scatter(False, dx[:, 0, CHUNK:HALF_N], 0, CHUNK, HALF_N)
        for c in range(2):
            weigh(late_g[1][:, c * K_PASS : (c + 1) * K_PASS], late1[c][:], 1, (2 + c) * CHUNK, (3 + c) * CHUNK)
        late_q = [quantize_g("late0", late_g[0])]
        held_dx = sb.tile([P, 3 * CHUNK], F32, name="held_dx", tag="weight1")
        nc.vector.tensor_copy(held_dx[:], own_ps[:])
        late_q.append(quantize_g("late1", late_g[1]))
        late_tiles = ((0, 2), (1,), (3,))
        late_ps = [ps.tile([P, len(tiles), HALF_N], F32, name="late_ps", tag=bank) for tiles, bank in zip(late_tiles, ("b2", "b6", "b7"))]
        for o in range(PASSES):
            for acc, tiles in zip(late_ps, late_tiles):
                for j, k in enumerate(tiles):
                    project(acc[:, j, :], k, o, late_q[o][0][:], late_q[o][1][:], (o, j) == (0, 0), (o, j) == (1, len(tiles) - 1))

        scatter(True, held_dx[:, 0:HALF_N], 2, 0, HALF_N)
        scatter(True, held_dx[:, HALF_N : 3 * CHUNK], 1, CHUNK, HALF_N)
        nc.vector.tensor_copy(dx[:, 2, HALF_N:N], late_ps[2][:, 0, :])
        nc.scalar.activation(dx[:, 0:4:3, HALF_N:N], late_ps[0][:], ACT.Copy)
        scatter(True, dx[:, 3, HALF_N:N], 2, HALF_N, N)
        store(2)
        scatter(False, dx[:, 0, HALF_N:N], 0, HALF_N, N)
        store(0)
        nc.scalar.activation(dx[:, 1, HALF_N:N], late_ps[1][:, 0, :], ACT.Copy)
        scatter(False, dx[:, 1, HALF_N:N], 1, HALF_N, N)
        store(1)
        scatter(True, dx[:, 2, :], 3, 0, N)
        store(3)
